import numpy as np, ml_dtypes
CORES = [5,29,101,125,133,157,229,253]
N = 8
import mx_ref
BF = ml_dtypes.bfloat16
def entries(a):
    return np.ascontiguousarray(a.T).reshape(-1)
def table(e):
    return np.ascontiguousarray(np.reshape(e, (-1, 16)).T).astype(np.int32)
def gcols(t, e):
    v = np.concatenate([t.reshape(8, 16, -1, 4), np.zeros((8, 16, 1, 4), BF)], axis=2)
    return np.ascontiguousarray(np.stack([v[g][:, e[g]] for g in range(8)])).reshape(128, -1)
def cols(t, e):
    v = np.concatenate([t.reshape(128, -1, 4), np.zeros((128, 1, 4), BF)], axis=1)
    return np.ascontiguousarray(v[:, e]).reshape(128, -1)
def tile(rs):
    return np.stack(rs, axis=2).reshape(128, -1).astype(BF)
def cut(t, i, w=512):
    return t[:, w * i:w * i + w]
def pick(q, e):
    c = np.concatenate([q[0].reshape(128, -1, 4), np.zeros((128, 1, 4), np.uint8)], axis=1); s = np.concatenate([q[1], np.ones((16, 1), np.uint8)], axis=1)
    return (np.ascontiguousarray(c[:, e].reshape(128, -1)), np.ascontiguousarray(s[:, e]))
def join(*qs):
    return (np.concatenate([q[0] for q in qs], axis=1), np.concatenate([q[1] for q in qs], axis=1))
def put(q, e, v):
    c, s = q[0].reshape(128, -1, 4).copy(), q[1].copy(); c[:, e] = v[0].reshape(128, -1, 4); s[:, e] = v[1]
    return (c.reshape(128, -1), s)
def pk(c, s):
    return (np.ascontiguousarray(c), mx_ref.live(s))
def emit(q):
    return q[0], q[1]
def packed(v, rng):
    q = [mx_ref.quantize(np.ascontiguousarray(v[r])) for r in range(N)]
    return np.stack([a for a, b in q]), np.stack([mx_ref.plane(b, rng) for a, b in q])
def values_of_codes():
    e, c = np.zeros((128, 128, 4), np.float32), np.zeros((128, 2, 4), np.uint8)
    e[np.arange(128), np.arange(128), 0] = 1
    c[:127, :, 0] = np.arange(256).reshape(2, 128).T[:127]
    return mx_ref.matmul(mx_ref.quantize(e.reshape(128, 512).astype(BF)), (c.reshape(128, 8), np.full((16, 2), 127, np.uint8))).T.reshape(-1).astype(np.float64)
CODE_VALUE, SCALE_VALUE = values_of_codes(), 2.0 ** (np.arange(256) - 127.0)
def decode(q):
    return (CODE_VALUE[q[0]].reshape(16, 8, -1, 4) * SCALE_VALUE[q[1]][:, None, :, None] + 0.0).reshape(128, -1).astype(np.float32)
def f(rng, *shape):
    return mx_ref.flush((rng.standard_normal(shape, dtype=np.float32) * np.exp2(rng.integers(-2, 3, shape[:-1] + (1,)))).astype(BF))
def wide(rng, *shape, cols=0):
    v = rng.standard_normal(shape, dtype=np.float32) * np.exp2(rng.integers(-12, 13, shape)).astype(np.float32)
    if cols: v *= np.repeat(np.exp2(rng.integers(-cols, cols + 1, shape[:-2] + (1, shape[-1] // 4))) * (rng.random(shape[:-2] + (1, shape[-1] // 4)) > 0.0625), 4, axis=-1).astype(np.float32)
    return mx_ref.flush(v.astype(BF))
C, M, F, R = 320, 96, 4, 3
def order(p):
    return np.argsort(-(p[::16] + np.float32(0.0)), axis=1, kind="stable")
def rewrite(t, e, h):
    a, b = t.reshape(8, 16, -1, 4).copy(), h.reshape(8, 16, -1, 4)
    for g in range(8):
        c, j = np.unique(e[g], return_index=True)
        a[g][:, c] = b[g][:, j]
    return a.reshape(128, -1)
def big(v):
    v = v.astype(np.float32)
    v[np.abs(v) < np.float32(2.0 ** -16)] = 0
    return v.astype(BF)
def offsets(a):
    return np.stack([table(np.concatenate([k, np.full(16 - F, -1)])) for k in a])
def numbers_of(rng):
    return {"x": big(f(rng, N, 128, 4 * C)), "m": big(f(rng, N, 128, 4 * M)), "kap": offsets(rng.integers(0, C, (N, F))), "u": np.array(f(rng, N, 128, 512)), "v": np.array(f(rng, N, 128, 512))}
def layers(rng):
    return big(f(rng, N, 128, 2048)).reshape(N, 8, 16, 4, 8, 16, 4)
def weights(rng, w):
    c, p = packed(np.ascontiguousarray(w).reshape(N, 128, 2048), rng)
    return {"wc": c, "ws": p}
def setup_inputs(rng):
    return {**numbers_of(rng), **weights(rng, layers(rng))}
def setup_inputs_ties(rng):
    d = numbers_of(rng)
    e = rng.permutation(N)
    x, m = d["x"].reshape(N, 8, 16, C, 4), d["m"].reshape(N, 8, 16, M, 4)
    for r in range(N):
        k = np.zeros(C, int) if r == e[0] else rng.permutation(C) % 3
        i = np.zeros(M, int) if r == e[0] else rng.permutation(M) % 3
        a = x[r][:, :8, :3].copy()
        a[:, :, 2] = 0
        x[r][:, :8] = a[:, :, k]
        m[r][:, :8] = a[:, :, i]
    x[e[1]] = 0
    u = d["u"].reshape(N, 8, 16, 128, 4)
    u[:, :, 8:, ::16] = 0
    u[:, :, 8:, 1] = 0
    w = layers(rng)
    w[:, :, 8:, :, :, :8] = 0
    kap = offsets(rng.integers(0, C, (N, 2))[:, rng.permutation(4) % 2])
    return {"x": x.reshape(N, 128, 4 * C), "m": m.reshape(N, 128, 4 * M), "kap": kap, "u": u.reshape(N, 128, 512), "v": d["v"], **weights(rng, w)}
def near_part(rng, s, b, size):
    p = np.zeros((16, s.size, 4))
    p[0, :, 0] = b
    g = ((s[:, None] >> np.arange(8)) & 1) * np.exp2(np.arange(8) - 23.0) * size
    p[8], p[9] = g[:, :4], g[:, 4:]
    p[10:] = rng.integers(4, 8, (6, s.size, 4)) * 2.0 ** -20 * size
    return p
def setup_inputs_near(rng):
    d = numbers_of(rng)
    kind = rng.permutation(8)
    c = np.where(kind < 6, kind % 2 * 2.0 - 1.0, 0.0)
    x, m = np.zeros((N, 8, 16, C, 4), np.float32), np.zeros((N, 8, 16, M, 4), np.float32)
    upper = np.arange(C) // (C // 2)
    for r in range(N):
        for g in range(8):
            i = (np.arange(C) + rng.integers(C)) % C
            b, a = np.full(C, c[g]), np.full(M, c[g])
            if kind[g] < 4: b[rng.integers(C)] *= 2.0 ** 30
            if kind[g] == 7:
                i = i % (C // 2) * 2 + upper
                b, a = (8 + upper) * 2.0 ** -33, (8 + rng.integers(0, 2, M)) * 2.0 ** -33
            size = 1.0 if kind[g] < 6 else 2.0 ** -4
            x[r, g] = near_part(rng, (i + 1) // 2, b, size)
            m[r, g] = near_part(rng, rng.integers(0, C // 2 + 1, M), a, size)
            if kind[g] == 7:
                x[r, g, 1, :, 0] = 17 * 2.0 ** -33 - b
                m[r, g, 1, :, 0] = 17 * 2.0 ** -33 - a
    u = d["u"].reshape(N, 128, 128, 4)
    k = np.where(rng.permutation(N) < N // 2, 2.0 ** -30, 1.0).astype(np.float32).astype(BF)
    u[:, :, ::16] = 0
    u[:, :, 1] = 0
    for h in range(0, 128, 16):
        u[:, h, h, 0] = k
        u[:, h + 8:h + 10, h] = k[:, None, None]
    h = 16 * int(np.argmax(kind))
    u[:, h, h, 0] = (k.astype(np.float32) * np.float32(1.125)).astype(BF)
    u[:, h + 1, h, 0] = k
    sort = rng.permutation(np.array([0, 5, 6, 7, 1, 2, 3, 4])[:N])
    one = np.argsort(kind)[sort]
    a = rng.integers(0, C, (N, F))
    for r in range(N):
        h = 16 * int(one[r])
        u[r, h:h + 16, 1] = u[r, h:h + 16, h]
        if sort[r] in (0, 5, 6, 7): a[r] = np.insert(rng.permutation(3), int(rng.integers(1, 4)), C - 1)
    w = layers(rng)
    w[:, :, :10] = 0
    w[:, :, :, :, :, :10] = 0
    w[:, :, :, :, np.flatnonzero(kind > 5)] = 0
    return {"x": x.reshape(N, 128, 4 * C).astype(BF), "m": m.reshape(N, 128, 4 * M).astype(BF), "kap": offsets(a), "u": u.reshape(N, 128, 512), "v": d["v"], **weights(rng, w)}
def setup_inputs_huge(rng):
    d = numbers_of(rng)
    o = rng.permutation(N)
    t = {}
    for key, n in (("x", C), ("m", M)):
        c = np.stack([rng.permutation(n) % 2 * 2.0 - 1.0 for r in range(N)])
        c[o < N // 2] = -1
        z = rng.random((N, 128, n, 4))
        z[:, ::8, :, 0] = 0
        t[key] = np.where(c[:, None, :, None] < 0, -2.0 ** 30 * (1 - 0.125 * z), 2.0 ** 28 * (0.8 - 0.2 * z)).astype(np.float32).reshape(N, 128, 4 * n).astype(BF)
    u = d["u"].reshape(N, 128, 128, 4)
    s = np.stack([np.append(rng.permutation(8) % 2 * 2.0 - 1.0, o[r] % 2 * 2.0 - 1.0) for r in range(N)])
    a = (2.0 ** 30 * (1 - 0.0625 * rng.integers(0, 2, (N, 128, 9, 4))) * s[:, None, :, None]).astype(np.float32).astype(BF)
    u[:, :, ::16] = a[:, :, :8]
    u[:, :, 1] = a[:, :, 8]
    w = np.zeros((N, 128, 4, 128, 4), np.float32)
    i = np.arange(128)
    for b in range(4): w[:, i, b, i, b] = 16
    return {"x": t["x"], "m": t["m"], "kap": d["kap"], "u": u.reshape(N, 128, 512), "v": d["v"], **weights(rng, w.astype(BF))}
def setup_inputs_wrap(rng):
    d = numbers_of(rng)
    x, m = d["x"].astype(np.float32).reshape(N, 8, 16, C, 4), d["m"].astype(np.float32).reshape(N, 8, 16, M, 4)
    u = d["u"].reshape(N, 128, 128, 4)
    x[:, :, :11] = 0
    m[:, :, :11] = 0
    u[:, :, ::16] = 0
    u[:, :, 1] = 0
    a = np.stack([rng.permutation(np.array([0, 1, C // 2, C - 1])) for r in range(N)])
    a[rng.integers(N)] = C - 1
    q = rng.integers(0, C + 1, (N, 8, M))
    o = rng.permutation(N)
    for r in range(N):
        g = rng.permutation(8)
        q[r, g[0]] = 0
        q[r, g[1]] = C
        q[r, g[2]] = rng.permutation(C)[:M]
        q[r, g[3]] = rng.integers(C - 2, C + 1, M)
        q[r, g[4]] = (rng.integers(C) - a[r][rng.integers(0, F, M)]) % C
        x[r, g[2], 0, :, 0] = rng.integers(1, 8, C)
        m[r, g[2], 0, :, 0] = rng.integers(1, 8, M)
        u[r, 16 * g[2], 1, 0] = -1 if o[r] < N // 2 else 1
    for h in range(0, 128, 16): u[:, h + 8:h + 11, h] = 1
    for t, key in ((x, 2 * (C - np.argsort(rng.random((N, 8, C)), axis=2))), (m, 2 * (C - q) + rng.integers(0, 2, q.shape))):
        z = ((key[:, :, :, None] >> np.arange(12)) & 1) * np.exp2(np.arange(12.0))
        for i in range(3): t[:, :, 8 + i] = z[:, :, :, 4 * i:4 * i + 4]
    w = layers(rng)
    w[:, :, :11] = 0
    w[:, :, :, :, :, :11] = 0
    return {"x": x.reshape(N, 128, 4 * C).astype(BF), "m": m.reshape(N, 128, 4 * M).astype(BF), "kap": offsets(a), "u": u.reshape(N, 128, 512), "v": d["v"], **weights(rng, w)}
def setup_inputs_spread(rng):
    d = setup_inputs(rng)
    d["x"] = big(wide(rng, N, 128, 4 * C, cols=6))
    d["m"] = big(wide(rng, N, 128, 4 * M, cols=6))
    return d
def check_inputs(d):
    b = []
    for k in ("x", "m", "u", "v"):
        a = np.abs(d[k].astype(np.float32))
        if not (np.isfinite(a).all() and ((a == 0) | (a >= 2.0 ** -30) & (a <= 2.0 ** 30)).all()): b.append("a value of " + k)
    none, least, most = [emit(mx_ref.quantize(np.full((128, 16), k, np.float32).astype(BF)))[1][0, 0] for k in (0.0, 2.0 ** -30, 2.0 ** 30)]
    for r in range(N):
        k = entries(d["kap"][r])
        if ((k[:F] < 0) | (k[:F] >= C)).any(): b.append("an offset of kap")
        if (k[F:] != -1).any(): b.append("kap: an entry that means nothing isn't -1")
        if ((d["wc"][r] == 0x7F) | (d["wc"][r] == 0xFF)).any(): b.append("wc: a code that is no number")
        s = mx_ref.live(d["ws"][r])
        if ((s != none) & ((s < least) | (s > most))).any(): b.append("ws: a scale out of range")
    return b
def reference(x, m, kap, u, v, wc, ws):
    qu = [mx_ref.quantize(u[r]) for r in range(N)]
    lay = [pk(wc[r], ws[r]) for r in range(N)]
    disc, msg = [x[r] for r in range(N)], [m[r] for r in range(N)]
    ok = np.zeros((N, R, M), np.float32)
    for t in range(R):
        won = []
        for r in range(N):
            p = mx_ref.matmul(qu[r], mx_ref.quantize(disc[r]))
            s = mx_ref.matmul(qu[r], mx_ref.quantize(msg[r]))
            n = np.sum(p[::16][:, :, None] > s[::16][:, None, :], axis=1)
            c = (n[:, None, :] + entries(kap[r])[:F][None, :, None]) % C
            e = np.take_along_axis(order(p), c.reshape(8, F * M), axis=1)
            z = ((gcols(disc[r], e).astype(np.float32) + np.tile(msg[r], (1, F)).astype(np.float32)) * np.float32(0.5)).astype(BF)
            best = np.argmax(mx_ref.matmul(qu[r], mx_ref.quantize(z))[1].reshape(F, M) + np.float32(0.0), axis=0)
            i = best * M + np.arange(M)
            h = cols(z, i)
            disc[r] = rewrite(disc[r], e[:, i], h)
            ok[r, t] = best
            won.append(mx_ref.quantize(h))
        came = decode(join(*won))
        for r in range(N):
            o = (r - 1) % N
            n = cut(came, o, 4 * M)
            msg[r] = tile([np.maximum(mx_ref.matmul(pick(lay[r], np.arange(128 * b, 128 * b + 128)), won[o]), np.float32(0.0)) * np.float32(0.03125) + n[:, b::4] for b in range(4)])
    y = np.zeros((N, 128, C + M), np.float32)
    oc, osc = np.zeros((N, 128, 4 * C + 4 * M), np.uint8), np.zeros((N, 16, C + M), np.uint8)
    for r in range(N):
        q = mx_ref.quantize(np.concatenate([disc[r], msg[r]], axis=1))
        y[r] = mx_ref.matmul(mx_ref.quantize(v[r]), q)
        oc[r], osc[r] = emit(q)
    return {"y": y, "ok": ok, "oc": oc, "osc": osc}

@@ -1,0 +1,554 @@
+import numpy as np
+from concourse.bass import DstId, RemoteDMATransfer
+from concourse.mybir import dt, AluOpType as Op, ActivationFunctionType as Act
+
+C, M, F, R = 320, 96, 4, 3
+BIG = 1.0e29
+BF, F16, F32, I32, U16, Q4, U8 = "bfloat16", "float16", "float32", "int32", "uint16", "float8_e4m3fn_x4", "uint8"
+
+TILES = [(0, 320, (0, 19, 18, 17)), (320, 256, (16, 15, 14, 13)), (576, 192, (12, 11, 10, 9)),
+         (768, 128, (5, 6, 7, 8)), (896, 64, (1, 2, 3, 4))]
+DVE_ROWS = [11, 12, 12]
+DVE_NROWS = [2, 2, 2]
+EB_DVE = 14
+Z_ACT = 2
+PIECES = [("c", 0, 48, 0), ("c", 48, 96, 2), ("s", 0, 96, 1)]
+CY, LAT, COMM, SLACK, BOOST, LOADU, LOADX = 0.83, 60.0, 6000.0, 70.0, 1500.0, 2800.0, 3700.0
+
+
+def sb(n, t):
+    return ("sbuf", [128, n], t)
+
+
+SCRATCH = {
+    "PA": ("psum", [128, 2048], F32), "PB": ("psum", [128, 2048], F32),
+    "X": sb(4 * (C + M), BF), "Xh": sb(4 * C, BF), "Y": sb(512, BF), "ub": sb(512, BF), "vb": sb(512, BF),
+    "uq": sb(128, Q4), "us": sb(128, U8), "ugq": sb(128, Q4), "ugs": sb(128, U8), "vq": sb(128, Q4), "vs": sb(128, U8),
+    "wq": sb(512, Q4), "wp": sb(512, U8), "aq": sb(448, Q4), "asc": sb(448, U8),
+    "E": sb(2048, BF), "eq": sb(512, Q4), "es": sb(512, U8), "CC": sb(1024, BF), "cq": sb(256, Q4), "cs": sb(256, U8),
+    "zq0": sb(128, Q4), "zs0": sb(128, U8), "BT": sb(4 * 960, BF), "bq": sb(1024, Q4), "bs": sb(1024, U8),
+    "Z": sb(4 * 416, BF), "zq": sb(416, Q4), "zs": sb(416, U8), "Bw": sb(512, BF), "bwq": sb(128, Q4), "bws": sb(128, U8),
+    "ones": sb(512, BF), "pc": sb(8, I32), "pf": sb(8, F32), "c16": sb(32, BF), "c4": sb(96, BF),
+    "M16": sb(C, BF), "K16": sb(C, BF), "r16": sb(C, BF), "r16m": sb(C, BF), "r192": sb(192, BF), "K4": sb(384, BF),
+    "r2": sb(768, BF), "ZI": sb(1536, BF), "ZJ": sb(1536, BF),
+    "IO": sb(C, BF), "Kc": sb(384, F32), "CK": sb(336, BF), "B4": sb(64, F32), "t16": sb(26, F32), "J": sb(32, F32),
+    "lui": sb(8, I32), "lu": sb(8, U16), "lwf": sb(8, F32), "lw": sb(2, U16), "lri": sb(8, F32), "lr": sb(6, U16),
+    "kp1": sb(16, I32), "kpb": sb(16, I32), "kpf": sb(4, F32), "z4": sb(4, F32),
+    "Pm": sb(C, F32), "Fv": sb(C, F32), "Sm": sb(M, F32), "Fs": sb(M, F32), "T0": sb(C, BF), "T1": sb(C, BF),
+    "SC": sb(13 * 208, BF), "DS": sb(C, BF), "RA": sb(20, F32), "base": sb(20, F32), "Fc": sb(C, F32),
+    "rkf": sb(20, F32), "rk": sb(20, U16), "O": sb(2 * C, BF), "NB": sb(6 * C, BF), "NS": sb(6 * C, BF), "nb": sb(6, F32),
+    "pos": sb(24, U16), "Fe": sb(384, F16), "eb": sb(384, BF), "zo": sb(96, U16),
+    "pm": sb(8, F32), "idf": sb(8, F32), "wi": sb(6, U16), "hf": sb(32, F32), "ho": sb(24, U16), "so": sb(24, U16), "H": sb(384, BF),
+    "ewb": sb(M, BF), "Fw": sb(M, F32), "e5": sb(32, F32), "tg": sb(64, F32), "EQ": sb(336, BF), "ES": sb(336, BF),
+    "RS": sb(384, F32), "KO": sb(R * M, F32), "yo": sb(C + M, F32),
+}
+for _r in range(R):
+    for _n, _w in (("slot", M), ("hop", M), ("land", 128)):
+        SCRATCH["%sc%d" % (_n, _r)] = sb(_w, Q4)
+        SCRATCH["%ss%d" % (_n, _r)] = sb(_w, U8)
+
+SEMAPHORES = (["qv", "qa", "qt", "qg", "sent"] + ["hop%d" % r for r in range(R)] + ["land%d" % r for r in range(R)]
+              + ["d%d" % k for k in range(40)])
+
+
+def helpers(topo, src, dst):
+    h = [c for c in topo.cores_of(src) if c != src and topo.may_write(c, dst)]
+    return sorted(h, key=lambda c: (topo.die(c) != topo.die(src), c))
+
+
+def some(engines, k, n):
+    w = len(engines) // n
+    return sum(1 << e for e in engines[k * w:(k + 1) * w])
+
+
+def piece(T, name, r, kind, a, b):
+    v = T["%s%s%d" % (name, kind, r)][:, a:b]
+    return v.bitcast(dt.uint8) if kind == "c" else v
+
+
+def first_hop(topo, src, dst):
+    h = helpers(topo, src, dst)
+    calls = {}
+    for kind, a, b, k in PIECES:
+        calls.setdefault((b - a) * (4 if kind == "c" else 1), []).append((kind, a, b, h[k % len(h)]))
+    return [[p + (some(topo.engines(src, p[3]), i, len(ps)),) for i, p in enumerate(ps)] for ps in calls.values()]
+
+
+def bits(m):
+    return bin(m).count("1")
+
+
+def helper_program(g, core, T, topo, src, dst):
+    mine = [p for call in first_hop(topo, src, dst) for p in call if p[3] == core]
+    if not mine:
+        return
+    rid, pid = topo.addr(dst, core)
+    mask = topo.mask(core, dst)
+    n = 0
+    for r in range(R):
+        g.wait_ge(T.sem["hop%d" % r], sum(bits(p[4]) for p in mine))
+        for kind, a, b, _, _ in mine:
+            g.remote_dma(piece(T, "land", r, kind, a, b), piece(T, "hop", r, kind, a, b), T.sem["land%d" % r], T.sem.sent, pid, rid, mask)
+            n += bits(mask)
+    g.wait_ge(T.sem.sent, n)
+
+
+def rank_program(g, core, T, topo):
+    cores = list(T.cores)
+    rank = T.rank_of(core)
+    if rank is None:
+        for i, c in enumerate(cores):
+            if core in topo.cores_of(c):
+                helper_program(g, core, T, topo, c, cores[(i + 1) % len(cores)])
+        return
+    nxt, prv = cores[(rank + 1) % len(cores)], cores[(rank - 1) % len(cores)]
+    calls = first_hop(topo, core, nxt)
+    landing = sum(bits(topo.mask(p[3], core)) for call in first_hop(topo, prv, core) for p in call)
+
+    ops = []
+    lastw = {n: np.full(s[1][1], -1) for n, s in SCRATCH.items()}
+    lastr = {n: [set() for _ in range(s[1][1])] for n, s in SCRATCH.items()}
+
+    def V(name, a=0, b=None, s=1, p=None):
+        if b is None:
+            b = SCRATCH[name][1][1]
+        rows = slice(None) if p is None else slice(p[0], p[1])
+        return {"ap": T[name][rows, a:b:s] if s > 1 else T[name][rows, a:b], "at": [(name, range(a, b, s))], "n": len(range(a, b, s)),
+                "two": SCRATCH[name][2] in (BF, F16, U16), "ps": SCRATCH[name][0] == "psum", "ind": False}
+
+    def bank(k, a=0, b=512):
+        return V("PA" if k < 4 else "PB", 512 * (k % 4) + a, 512 * (k % 4) + b)
+
+    def ind(win, off, word=None):
+        w = win["ap"].bitcast(word) if word else win["ap"]
+        return {"ap": w.indirect(off["ap"]), "at": win["at"] + off["at"], "n": 16 * off["n"], "two": False, "ps": False, "ind": True, "win": win, "off": off}
+
+    def add(q, fn, outs, ins, cost, lat=None, after=(), ext=None, soft=None, kind="c"):
+        me, deps, order = len(ops), set(after), set()
+        reads, writes = [], []
+        for v in ins:
+            if isinstance(v, dict):
+                reads += v["at"]
+        for v in outs:
+            writes += v["win"]["at"] if v["ind"] else v["at"]
+            reads += v["off"]["at"] if v["ind"] else []
+        psum = lambda n: SCRATCH[n][0] == "psum"
+        whole = lambda n, cols: sorted(set(c // 512 * 512 for c in cols)) if psum(n) else cols
+        for n, cols in reads:
+            for c in whole(n, cols):
+                deps.add(int(lastw[n][c]))
+                if psum(n):
+                    deps.update(o for o in lastr[n][c] if ops[o]["q"] != q)
+        for n, cols in writes:
+            for c in whole(n, cols):
+                (order if psum(n) else deps).add(int(lastw[n][c]))
+                deps.update(lastr[n][c])
+        for n, cols in reads:
+            for c in whole(n, cols):
+                lastr[n][c].add(me)
+        for n, cols in writes:
+            for c in whole(n, cols):
+                lastw[n][c] = me
+                lastr[n][c] = set()
+        deps -= {-1, me}
+        order.discard(-1)
+        ops.append({"q": q, "fn": fn, "deps": deps, "order": order - deps, "cost": cost, "lat": LAT if lat is None else lat, "ext": ext, "soft": soft, "kind": kind, "boost": 0.0})
+        return me
+
+    def ap(v):
+        return v["ap"] if isinstance(v, dict) else v
+
+    def plain(n, f=1.0):
+        return max(64.0, n * f) * CY
+
+    def vcost(out, a, f):
+        if out["ind"]:
+            return 50 + out["n"] * 3.8 * CY
+        if a["ind"]:
+            return 50 + out["n"] * 1.56 * CY
+        return plain(out["n"], f)
+
+    def fast(*vs):
+        return 0.5 if all(v["two"] for v in vs) else 1.0
+
+    def ts(out, in0, s1, op0, s2=None, op1=None):
+        if op1 is None:
+            fn = lambda: g.vector.tensor_scalar(out["ap"], in0["ap"], ap(s1), None, op0)
+        else:
+            fn = lambda: g.vector.tensor_scalar(out["ap"], in0["ap"], ap(s1), ap(s2), op0, op1)
+        return add("v", fn, [out], [in0, s1, s2], vcost(out, in0, fast(out, in0)))
+
+    def tt(out, a, b, op):
+        return add("v", lambda: g.vector.tensor_tensor(out["ap"], a["ap"], b["ap"], op), [out], [a, b], vcost(out, a, 1.0 if a["ps"] or b["ps"] else 2.0))
+
+    def cp(out, a):
+        return add("v", lambda: g.vector.tensor_copy(out["ap"], a["ap"]), [out], [a], vcost(out, a, fast(out, a)))
+
+    def scan(out, d0, d1, init, op0, op1):
+        return add("v", lambda: g.vector.tensor_tensor_scan(out["ap"], d0["ap"], d1["ap"], init, op0, op1), [out], [d0, d1], plain(out["n"], fast(out, d0, d1)))
+
+    def fill(out, c):
+        return add("v", lambda: g.vector.memset(out["ap"], c), [out], [], plain(out["n"], fast(out)))
+
+    def quant(q, s, a, src):
+        n = src["n"] // 4
+        oq, osc = V(q, a, a + n), V(s, a, a + n)
+        return add("v", lambda: g.vector.quantize_mx(oq["ap"], osc["ap"], src["ap"]), [oq, osc], [src], 12 + 0.22 * src["n"])
+
+    def act(out, a, func, bias=None, scale=None, acc=None):
+        kw = {}
+        if bias is not None:
+            kw["bias"] = ap(bias)
+        if scale is not None:
+            kw["scale"] = scale
+        if acc is not None:
+            kw["accum_out"] = acc["ap"]
+        cost = 65 + out["n"] * 1.56 * CY if a["ind"] else plain(out["n"]) + (20 if acc else 0)
+        return add("a", lambda: g.scalar.activation(out["ap"], a["ap"], func, **kw), [out] + ([acc] if acc else []), [a, bias], cost)
+
+    def mm(k, lq, ls, la, rq, rs, ra, n, start=True, stop=True, ext=None, soft=None):
+        o, l, l2, m1, m2 = bank(k, 0, n), V(lq, la, la + 128), V(ls, la, la + 128), V(rq, ra, ra + n), V(rs, ra, ra + n)
+        return add("t", lambda: g.tensor.matmul_mx(o["ap"], l["ap"], l2["ap"], m1["ap"], m2["ap"], start, stop), [o], [l, l2, m1, m2], (n + 16) * 0.6, ext=ext, soft=soft)
+
+    def iota(out, pattern, base=0, cm=0):
+        if SCRATCH[out["at"][0][0]][2] == I32:
+            fn = lambda: g.iota(out["ap"], pattern, base, cm)
+        else:
+            fn = lambda: g.iota(out["ap"], pattern, base, cm, allow_small_or_imprecise_dtypes=True)
+        return add("g", fn, [out], [], 130 + 2 * CY * out["n"])
+
+    def dma(q, out, in_, after=(), lat=2000.0, slow=False):
+        eng = {"s": g.sync, "a": g.scalar, "g": g}[q]
+        if slow:
+            fn = lambda: eng.dma_start(ap(out), ap(in_), allow_slow_non_contiguous=True)
+        else:
+            fn = lambda: eng.dma_start(ap(out), ap(in_))
+        return add(q, fn, [out] if isinstance(out, dict) else [], [in_], 60.0, lat=lat, after=after, kind="d")
+
+    def cast(v, t):
+        w = dict(v)
+        w["ap"] = v["ap"].bitcast(t)
+        return w
+
+    def pick(oq, os_, q, s, n, off):
+        cp(cast(V(oq, 0, 16 * off["n"]), dt.uint32), ind(V(q, 0, n), off, dt.uint32))
+        act(V(os_, 0, 16 * off["n"]), ind(V(s, 0, n), off), Act.Copy)
+
+    def spread(name, w, n, a=0):
+        while w < n:
+            k = min(w, n - w)
+            act(V(name, a + w, a + w + k), V(name, a, a + k), Act.Copy)
+            w += k
+
+    def keeper(name, n, c, tmp, col, w):
+        out = V(name, 0, n)
+        ts(out, c, col, Op.is_lt, -4096.0, Op.mult)
+        ts(tmp, c, col, Op.is_equal, 1024.0, Op.mult)
+        tt(out, out, tmp, Op.add)
+        ts(V(name, w - 1, n, w), V(name, w - 1, n, w), -2048.0, Op.add)
+
+    def zero(v):
+        act(v, V("ones", 0, v["n"]), Act.Copy, scale=0.0)
+
+    dma("a", V("ub"), T.u[:], lat=LOADU)
+    lx = dma("s", V("X", 0, 4 * C), T.x[:], lat=LOADX)
+    dma("a", V("Y", 0, 4 * M), T.m[:], lat=LOADU)
+    dma("s", cast(V("wq"), dt.uint8), T.wc[:], after=[lx])
+    dma("s", V("wp"), T.ws[:], after=[lx])
+    dma("s", V("vb"), T.v[:], after=[lx])
+    dma("g", V("kp1", p=(0, 1)), T.kap[:], slow=True)
+
+    fill(V("ones"), 1.0)
+    iota(V("pc", 0, 2), [[1, 2]], 0, 1)
+    ts(V("pc", 2, 4), V("pc", 0, 2), 3, Op.bitwise_and)
+    ts(V("pc", 4, 5), V("pc", 0, 1), 15, Op.bitwise_and)
+    ts(V("pc", 5, 6), V("pc", 0, 1), 4, Op.arith_shift_right)
+    ts(V("pc", 6, 7), V("pc", 0, 1), 2, Op.arith_shift_right, 3, Op.bitwise_and)
+    cp(V("pf", 0, 5), V("pc", 2, 7))
+    bcol, b1col, icol, gcol, i4col = (V("pf", k, k + 1) for k in range(5))
+    ts(V("pf", 5, 6), bcol, 4.0 * (160 + 1024), Op.add)
+    iota(V("lui"), [[16, 8]])
+    cp(V("lu"), V("lui"))
+    c16 = V("c16", 0, 16)
+    iota(c16, [[1, 16]])
+    ts(V("M16", 0, 16), c16, icol, Op.not_equal, BIG, Op.mult)
+    ts(V("r16", 0, 16), c16, 0.0, Op.is_equal, 2 * BIG, Op.mult)
+    act(V("r16m", 0, 16), c16, Act.Sign)
+    keeper("K16", 16, c16, V("c16", 16, 32), icol, 16)
+    for name in ("M16", "r16", "r16m", "K16"):
+        spread(name, 16, C)
+    iota(V("t16", 0, 20), [[16, 20]], 1024)
+    iota(V("t16", 20, 26), [[16, 6]])
+    act(V("J", 0, 26), V("t16", 0, 26), Act.Identity, bias=icol)
+    iota(V("CC", 0, 512), [[1, 8], [0, 64]])
+    ts(V("CC", 0, 512), V("CC", 0, 512), gcol, Op.is_equal)
+    quant("cq", "cs", 0, V("CC", 0, 512))
+    iota(V("IO"), [[1, C]], -160)
+    add("g", lambda: g.partition_broadcast(T.kpb[:], T.kp1[0:1, :], 128), [V("kpb")], [V("kp1")], 200.0)
+    cp(V("kpf"), V("kpb", 0, 4))
+    iota(V("c4", 0, 48), [[0, 12], [1, 4]])
+    keeper("K4", 48, V("c4", 0, 48), V("c4", 48, 96), i4col, 4)
+    spread("K4", 48, 384)
+    iota(V("CC", 512, 576), [[1, 16], [0, 4]])
+    ts(V("CC", 512, 576), V("CC", 512, 576), icol, Op.is_equal, float(M), Op.mult)
+    spread("CC", 64, 512, 512)
+    quant("cq", "cs", 128, V("CC", 512, 1024))
+    iota(V("lwf", 0, 2), [[4, 2]])
+    fill(V("lwf", 4, 5), 1.5)
+    fill(V("lwf", 5, 6), 1.0)
+    ts(V("lwf", 2, 4), V("lwf", 0, 2), i4col, Op.add, gcol, Op.is_equal)
+    ts(V("lw"), V("lwf", 2, 4), b1col, Op.mult)
+    iota(V("pm", 0, 1), [[0, 1]], 1)
+    act(V("pm", 0, 1), V("pm", 0, 1), Act.Copy, scale=BIG)
+    ts(V("lri", 0, 2), V("lwf", 0, 2), i4col, Op.add, 5.0, Op.min)
+    cp(V("lr", 0, 2), V("lri", 0, 2))
+    ts(V("lr", 2, 4), V("lri", 0, 2), 16.0, Op.mult, 15.0, Op.add)
+    act(V("lri", 2, 4), V("lri", 0, 2), Act.Square, bias=V("lwf", 4, 5))
+    ts(V("lr", 4, 6), V("lri", 2, 4), 8.0, Op.mult, -4.0, Op.add)
+    iota(V("B4", 0, 32), [[0, 8], [1, 4]], 4 * 1536)
+    act(V("B4", 0, 32), V("B4", 0, 32), Act.Copy, scale=0.25)
+    iota(V("B4", 32, 56), [[64, 6], [1, 4]], 4 * 672)
+    act(V("B4", 32, 56), V("B4", 32, 56), Act.Identity, scale=0.25, bias=icol)
+    iota(V("r2", 0, 48), [[0, 24], [1, 2]])
+    spread("r2", 48, 768)
+    iota(V("idf"), [[0, 8]])
+    iota(V("z4"), [[0, 4]])
+    iota(V("Kc"), [[1, 4], [0, M]])
+    tri = [8 * t * (t + 1) for t in range(7)]
+    for t in range(6):
+        iota(V("CK", tri[t], tri[t + 1]), [[1, 16 * t + 16]], 1 - 16 * t)
+    ts(V("CK"), V("CK"), icol, Op.is_equal, 4096.0, Op.mult)
+    act(V("CK"), V("CK"), Act.Identity, bias=V("lwf", 5, 6))
+    for t in range(6):
+        iota(V("CK", tri[t + 1] - 1, tri[t + 1]), [[0, 1]])
+    act(V("r192"), V("ones", 0, 192), Act.Copy)
+    iota(V("r192", 128, 129), [[0, 1]])
+    for b in range(4):
+        o = V("E", 512 * b, 512 * b + 512)
+        add("g", lambda o=o, b=b: g.affine_select(o["ap"], T.ones[:], [[8, 128], [1, 4]], Op.is_equal, 0.0, -b, -8), [o], [V("ones")], 170 + 2 * CY * 512)
+    quant("eq", "es", 0, V("E", 0, 1024))
+    quant("eq", "es", 256, V("E", 1024, 2048))
+    zero(V("Bw"))
+    quant("zq0", "zs0", 0, V("Bw"))
+    dma("s", cast(V("bq", 960, 1024), dt.uint8), cast(V("zq0", 0, 64), dt.uint8))
+    dma("s", V("bs", 960, 1024), V("zs0", 0, 64))
+    for r in range(R):
+        dma("s", cast(V("landc%d" % r, M, 128), dt.uint8), cast(V("zq0", 0, 32), dt.uint8))
+        dma("s", V("lands%d" % r, M, 128), V("zs0", 0, 32))
+    for a, n, _ in TILES:
+        fill(V("BT", 4 * (a + n - 48), 4 * (a + n)), 0.0)
+    fill(V("Y", 4 * M, 512), 0.0)
+    zero(V("Z", 4 * F * M, 4 * 416))
+    quant("uq", "us", 0, V("ub"))
+    pick("ugq", "ugs", "uq", "us", 128, V("lu"))
+    quant("vq", "vs", 0, V("vb"))
+
+    slot = {t: (a, b) for a, n, rows in TILES for b, t in enumerate(rows)}
+
+    def rowview(t, n):
+        a, b = slot[t]
+        return V("BT", 4 * a + b, 4 * (a + n), 4)
+
+    flip = [0]
+
+    def signs(n, col):
+        flip[0] ^= 1
+        o = V("T%d" % flip[0], 0, n)
+        act(o, bank(5, 0, n), Act.Sign, bias=col, scale=-1.0)
+        return o
+
+    outs = []
+    for r in range(R):
+        quant("aq", "asc", 0, V("X", 0, 4 * C))
+        mm(4, "ugq", "ugs", 0, "aq", "asc", 0, C)
+        mm(5, "ugq", "ugs", 0, "aq", "asc", 0, C)
+        for h in range(4):
+            act(V("Xh", C * h, C * h + C), V("X", C * h, C * h + C), Act.Copy, scale=0.5)
+        for a, b in ((160, C), (0, 160)):
+            tt(V("Pm", a, b), bank(4, a, b), V("M16", a, b), Op.add)
+            scan(V("Fv", a, b), V("r16", a, b), V("Pm", a, b), 0.0, Op.add, Op.min)
+        tt(rowview(0, C), V("Fv"), bank(4, 0, C), Op.is_ge)
+        scan(V("DS"), V("r16m"), rowview(0, C), 0.0, Op.mult, Op.add)
+        tt(V("base"), V("J", 0, 20), V("DS", 15, C, 16), Op.subtract)
+        nv = DVE_ROWS[r]
+        for t in range(19, nv, -1):
+            s = signs(16 * t, V("Fv", 16 * t + 15, 16 * t + 16))
+            act(rowview(t, 16 * t), s, Act.Relu, acc=V("RA", t, t + 1))
+        for t in range(nv, 0, -1):
+            ts(rowview(t, 16 * t), bank(4, 0, 16 * t), V("Fv", 16 * t + 15, 16 * t + 16), Op.is_lt)
+            if t > 8:
+                scan(V("SC", 208 * t - 16 * t, 208 * t), V("ones", 0, 16 * t), rowview(t, 16 * t), 0.0, Op.mult, Op.add)
+        for b in range(4):
+            scan(V("SC", 208 * b, 208 * b + 192), V("r192"), V("BT", 4 * 768 + b, 4 * 960, 4), 0.0, Op.mult, Op.add)
+        tt(V("base", 1, 5), V("base", 1, 5), V("SC", 191, 832, 208), Op.subtract)
+        tt(V("base", 5, 9), V("base", 5, 9), V("SC", 127, 832, 208), Op.subtract)
+        if nv > 8:
+            tt(V("base", 9, nv + 1), V("base", 9, nv + 1), V("SC", 208 * 9 - 1, 208 * nv, 208), Op.subtract)
+        tt(V("base", nv + 1, 20), V("base", nv + 1, 20), V("RA", nv + 1, 20), Op.subtract)
+        quant("bq", "bs", 0, V("BT", 0, 4 * 320))
+        mm(7, "cq", "cs", 0, "bq", "bs", 0, 320, True, False)
+        quant("bq", "bs", 768, V("BT", 4 * 768, 4 * 960))
+        mm(7, "cq", "cs", 0, "bq", "bs", 768, 128, False, False)
+        mm(7, "cq", "cs", 0, "bq", "bs", 896, 128, False, False)
+        late = ((320, 256), (576, 192)) if nv < 12 else ((576, 192), (320, 256))
+        for a, n in late:
+            quant("bq", "bs", a, V("BT", 4 * a, 4 * (a + n)))
+            mm(7, "cq", "cs", 0, "bq", "bs", a, n, False, (a, n) == late[1])
+        scan(V("Fc"), bank(7, 0, C), V("K16"), -4096.0, Op.max, Op.add)
+        tt(V("rkf"), V("Fc", 15, C, 16), V("base"), Op.add)
+        cp(V("rk"), V("rkf"))
+        cp(ind(V("O", 0, C), V("rk")), V("IO"))
+        cp(V("O", C, 2 * C), V("O", 0, C))
+
+        quant("aq", "asc", C, V("Y"))
+        for a in range(0, 768 * Z_ACT, 768):
+            act(V("ZI", a + 1, a + 768, 2), V("Y", 0, 4 * M), Act.Copy, scale=0.5)
+        mm(6, "ugq", "ugs", 0, "aq", "asc", C, 128)
+        tt(V("Sm"), bank(6, 0, M), V("M16", 0, M), Op.add)
+        ops[scan(V("Fs"), V("r16", 0, M), V("Sm"), 0.0, Op.add, Op.min)]["boost"] = BOOST if r else 0.0
+        nn = DVE_NROWS[r]
+        for t in range(6):
+            col, row = V("Fs", 16 * t + 15, 16 * t + 16), V("NB", C * t, C * t + C)
+            if t < nn:
+                ts(row, bank(4, 0, C), col, Op.is_gt)
+                scan(V("NS", C * t, C * t + C), V("ones", 0, C), row, -160.0, Op.mult, Op.add)
+            else:
+                act(row, signs(C, col), Act.Relu, scale=-1.0, acc=V("nb", t, t + 1))
+        ts(V("nb", 0, nn), V("NS", C - 1, C * nn, C), 160.0, Op.add)
+        for k in range(F):
+            ts(V("pos", 6 * k, 6 * k + 6), V("nb"), V("kpf", k, k + 1), Op.add)
+
+        cp(V("eb", 0, 16 * EB_DVE), ind(V("O"), V("pos", 0, EB_DVE)))
+        act(V("eb", 16 * EB_DVE, 384), ind(V("O"), V("pos", EB_DVE, 24)), Act.Copy)
+        scan(V("Fe"), V("eb"), V("K4"), -4096.0, Op.max, Op.add)
+        ts(V("zo"), V("Fe", 3, 384, 4), 4.0, Op.mult, V("pf", 5, 6), Op.add)
+        for k in range(F - Z_ACT):
+            tt(V("Z", 384 * k, 384 * k + 384), ind(V("Xh"), V("zo", 24 * k, 24 * k + 24)), V("ZI", 1, 768, 2), Op.add)
+        for k in range(F - Z_ACT, F):
+            a = 768 * (k - F + Z_ACT)
+            act(V("ZI", a, a + 768, 2), ind(V("Xh"), V("zo", 24 * k, 24 * k + 24)), Act.Copy)
+            scan(V("ZJ", a, a + 768), V("r2"), V("ZI", a, a + 768), 0.0, Op.mult, Op.add)
+            act(V("Z", 384 * k, 384 * k + 384), V("ZJ", a + 1, a + 768, 2), Act.Copy)
+        quant("zq", "zs", 0, V("Z", 0, 4 * 288))
+        quant("zq", "zs", 288, V("Z", 4 * 288, 4 * 416))
+        for k in range(F):
+            mm(k, "zq", "zs", M * k, "uq", "us", 0, 128)
+
+        scan(V("pm", 1, 5), V("z4"), V("PA", 1, 2048, 512), -BIG, Op.add, Op.max)
+        ts(V("Bw", 0, 32), ind(V("pm", 0, 4), V("lw")), V("pm", 4, 5), Op.is_lt)
+        quant("bwq", "bws", 0, V("Bw"))
+        mm(6, "cq", "cs", 128, "bwq", "bws", 0, 128)
+        tt(V("idf", 0, 6), bank(6, 0, 6), V("J", 20, 26), Op.add)
+        cp(V("wi"), V("idf", 0, 6))
+        pick("slotc%d" % r, "slots%d" % r, "zq", "zs", F * M, V("wi"))
+        sends = []
+        for call in calls:
+            def send(call=call, r=r):
+                tr = []
+                for kind, a, b, h, mask in call:
+                    rid, pid = topo.addr(h, core)
+                    if len(call) == 1:
+                        return g.remote_dma(piece(T, "hop", r, kind, a, b), piece(T, "slot", r, kind, a, b), T.sem["hop%d" % r], T.sem.sent, pid, rid, mask)
+                    tr.append(RemoteDMATransfer(dst_ids=[DstId(rid=rid, pnc=pid)], dma_engine_mask=mask, remote_sem=T.sem["hop%d" % r],
+                                                src=piece(T, "slot", r, kind, a, b), dst=piece(T, "hop", r, kind, a, b)))
+                return g.remote_dma_fused(tr, local_sem=T.sem.sent)
+            sends.append(add("g", send, [], [V("slot%s%d" % (p[0], r), p[1], p[2]) for p in call], 500.0, kind="r"))
+        if len(sends) > 1:
+            ops[sends[1]]["order"].add(sends[0])
+        act(V("KO", M * r, M * r + M), ind(V("Kc"), V("wi")), Act.Copy)
+
+        act(V("ewb"), ind(V("eb"), V("wi")), Act.Copy)
+        scan(V("Fw"), V("ewb"), V("K16", 0, M), -4096.0, Op.max, Op.add)
+        tt(V("hf"), ind(V("idf"), V("lr", 0, 2)), V("B4", 0, 32), Op.add)
+        ts(V("ho"), V("hf", 0, 24), 4.0, Op.mult, -4.0 * 1536, Op.add)
+        act(V("H"), ind(V("Z", 0, 4 * F * M), V("ho")), Act.Copy)
+        for t in range(6):
+            ts(V("EQ", tri[t], tri[t + 1]), V("ewb", 0, 16 * t + 16), -1024.0, Op.add, V("Fw", 16 * t + 15, 16 * t + 16), Op.is_equal)
+        tt(V("e5"), ind(V("Fw"), V("lr", 2, 4)), V("B4", 0, 32), Op.add)
+        scan(V("ES"), V("EQ"), V("CK"), 0.0, Op.add, Op.mult)
+        tt(V("tg", 0, 32), ind(V("ES"), V("lr", 4, 6)), V("e5"), Op.max)
+        tt(V("tg", 32, 56), V("tg", 0, 24), V("B4", 32, 56), Op.min)
+        ts(V("so"), V("tg", 32, 56), 4.0, Op.mult, -4.0 * 352, Op.add)
+        cp(ind(V("X"), V("so")), V("H"))
+
+        lc, ls = "landc%d" % r, "lands%d" % r
+        ext = ("land%d" % r, landing)
+        wb, db = ((0, 2, 6, 2), (1, 3, 0, 1)) if r < R - 1 else ((0, 1, 2, 3), (4, 5, 6, 0))
+        for b in range(4):
+            mm(wb[b], "wq", "wp", 128 * b, lc, ls, 0, 128, ext=ext, soft=sends)
+            act(V("RS", M * b, M * b + M), bank(wb[b], 0, M), Act.Relu, scale=0.03125)
+            mm(db[b], "eq", "es", 128 * b, lc, ls, 0, 128, ext=ext, soft=sends)
+            tt(V("Y", b, 4 * M, 4), V("RS", M * b, M * b + M), bank(db[b], 0, M), Op.add)
+
+    outs.append(dma("s", T.ok[:], V("KO", p=(0, 1))))
+    for a, n, w, src, k in ((0, C, C, V("X", 0, 4 * C), 7), (C, M, 128, V("Y"), 1)):
+        quant("aq", "asc", a, src)
+        mm(k, "vq", "vs", 0, "aq", "asc", a, w)
+        if a:
+            cp(V("yo", a, a + n), bank(k, 0, n))
+        else:
+            act(V("yo", a, a + n), bank(k, 0, n), Act.Copy)
+        outs.append(dma("a", T.oc[:, 4 * a:4 * (a + n)], cast(V("aq", a, a + n), dt.uint8)))
+        for j in range(4):
+            outs.append(dma("sa"[j % 2], T.osc[4 * j:4 * j + 4, a:a + n], V("asc", a, a + n, p=(32 * j, 32 * j + 4))))
+        outs.append(dma("s", T.y[:, a:a + n], V("yo", a, a + n)))
+
+    n = len(ops)
+    kids = [[] for _ in range(n)]
+    for i, o in enumerate(ops):
+        o["pre"] = [(d, ops[d]["lat"]) for d in o["deps"]] + [(d, 0.0) for d in o["order"]] + [(d, COMM) for d in (o["soft"] or [])]
+        for d, l in o["pre"]:
+            kids[d].append((i, l))
+    tail = [0.0] * n
+    for i in range(n - 1, -1, -1):
+        tail[i] = ops[i]["cost"] + ops[i]["boost"] + max([l + tail[k] for k, l in kids[i]] + [ops[i]["lat"]])
+    left = [len(o["pre"]) for o in ops]
+    ready = [0.0] * n
+    free = {q: 0.0 for q in "vatgs"}
+    pool = [i for i in range(n) if left[i] == 0]
+    plan = []
+    while pool:
+        at = lambda i: max(ready[i], free[ops[i]["q"]])
+        j0 = min(pool, key=at)
+        q, first = ops[j0]["q"], at(j0)
+        i = max((j for j in pool if ops[j]["q"] == q and at(j) <= first + SLACK), key=lambda j: tail[j])
+        pool.remove(i)
+        free[q] = at(i) + ops[i]["cost"]
+        plan.append(i)
+        for k, l in kids[i]:
+            ready[k] = max(ready[k], free[q] + l)
+            left[k] -= 1
+            if left[k] == 0:
+                pool.append(k)
+
+    queue = {"v": g.vector, "a": g.scalar, "t": g.tensor, "g": g, "s": g.sync}
+    needed = set(d for o in ops for d in o["deps"])
+    count, seen, mark, nd = {q: 0 for q in queue}, {q: {} for q in queue}, {}, 0
+
+    def wait(q, sem, val):
+        if seen[q].get(sem, 0) < val:
+            queue[q].wait_ge(T.sem[sem], val)
+            seen[q][sem] = val
+
+    for i in plan:
+        o = ops[i]
+        want = {}
+        for d in o["deps"]:
+            s, v = mark[d]
+            want[s] = max(want.get(s, 0), v)
+        for s, v in want.items():
+            wait(o["q"], s, v)
+        if o["ext"]:
+            wait(o["q"], *o["ext"])
+        ins = o["fn"]()
+        if o["kind"] == "d":
+            mark[i] = ("d%d" % nd, 16)
+            ins.then_inc(T.sem["d%d" % nd], 16)
+            nd += 1
+        elif o["kind"] == "c" and i in needed:
+            count[o["q"]] += 1
+            mark[i] = ("q" + o["q"], count[o["q"]])
+            ins.then_inc(T.sem["q" + o["q"]], 1)
+    for i in outs:
+        wait(ops[i]["q"], *mark[i])
+    g.wait_ge(T.sem.sent, R * sum(bits(p[4]) for call in calls for p in call))

@@ -8,12 +8,12 @@ BF, F16, F32, I32, U16, Q4, U8 = "bfloat16", "float16", "float32", "int32", "uin
 
 TILES = [(0, 320, (0, 19, 18, 17)), (320, 256, (16, 15, 14, 13)), (576, 192, (12, 11, 10, 9)),
          (768, 128, (5, 6, 7, 8)), (896, 64, (1, 2, 3, 4))]
-DVE_ROWS = [11, 12, 12]
+DVE_ROWS = [12, 12, 12]
 DVE_NROWS = [2, 2, 2]
 EB_DVE = 14
 Z_ACT = 2
 PIECES = [("c", 0, 48, 0), ("c", 48, 96, 2), ("s", 0, 96, 1)]
-CY, LAT, COMM, SLACK, BOOST, LOADU, LOADX = 0.83, 60.0, 6000.0, 70.0, 1500.0, 2800.0, 3700.0
+CY, LAT, ADD, COMM, SLACK, BOOST, LOADU, LOADX = 0.83, 180.0, 30.0, 7000.0, 90.0, 1500.0, 2800.0, 3700.0
 
 
 def sb(n, t):
@@ -30,13 +30,13 @@ SCRATCH = {
     "Z": sb(4 * 416, BF), "zq": sb(416, Q4), "zs": sb(416, U8), "Bw": sb(512, BF), "bwq": sb(128, Q4), "bws": sb(128, U8),
     "ones": sb(512, BF), "pc": sb(8, I32), "pf": sb(8, F32), "c16": sb(32, BF), "c4": sb(96, BF),
     "M16": sb(C, BF), "K16": sb(C, BF), "r16": sb(C, BF), "r16m": sb(C, BF), "r192": sb(192, BF), "K4": sb(384, BF),
-    "r2": sb(768, BF), "ZI": sb(1536, BF), "ZJ": sb(1536, BF),
+    "KB": sb(C, F32), "r2": sb(768, BF), "ZI": sb(1536, BF), "ZJ": sb(1536, BF),
     "IO": sb(C, BF), "Kc": sb(384, F32), "CK": sb(336, BF), "B4": sb(64, F32), "t16": sb(26, F32), "J": sb(32, F32),
     "lui": sb(8, I32), "lu": sb(8, U16), "lwf": sb(8, F32), "lw": sb(2, U16), "lri": sb(8, F32), "lr": sb(6, U16),
     "kp1": sb(16, I32), "kpb": sb(16, I32), "kpf": sb(4, F32), "z4": sb(4, F32),
     "Pm": sb(C, F32), "Fv": sb(C, F32), "Sm": sb(M, F32), "Fs": sb(M, F32), "T0": sb(C, BF), "T1": sb(C, BF),
-    "SC": sb(13 * 208, BF), "DS": sb(C, BF), "RA": sb(20, F32), "base": sb(20, F32), "Fc": sb(C, F32),
-    "rkf": sb(20, F32), "rk": sb(20, U16), "O": sb(2 * C, BF), "NB": sb(6 * C, BF), "NS": sb(6 * C, BF), "nb": sb(6, F32),
+    "SC": sb(13 * 208, BF), "DS": sb(C, BF), "RA": sb(20, F32), "Fc": sb(C, F32),
+    "rk": sb(20, U16), "O": sb(2 * C, BF), "NB": sb(6 * C, BF), "NS": sb(6 * C, BF), "nb": sb(6, F32),
     "pos": sb(24, U16), "Fe": sb(384, F16), "eb": sb(384, BF), "zo": sb(96, U16),
     "pm": sb(8, F32), "idf": sb(8, F32), "wi": sb(6, U16), "hf": sb(32, F32), "ho": sb(24, U16), "so": sb(24, U16), "H": sb(384, BF),
     "ewb": sb(M, BF), "Fw": sb(M, F32), "e5": sb(32, F32), "tg": sb(64, F32), "EQ": sb(336, BF), "ES": sb(336, BF),
@@ -152,7 +152,8 @@ def rank_program(g, core, T, topo):
                 lastr[n][c] = set()
         deps -= {-1, me}
         order.discard(-1)
-        ops.append({"q": q, "fn": fn, "deps": deps, "order": order - deps, "cost": cost, "lat": LAT if lat is None else lat, "ext": ext, "soft": soft, "kind": kind, "boost": 0.0})
+        ops.append({"q": q, "fn": fn, "deps": deps, "order": order - deps, "cost": cost, "pc": cost + (ADD if kind == "c" and q in "va" else 0.0),
+                    "lat": LAT if lat is None else lat, "ext": ext, "soft": soft, "kind": kind, "boost": 0.0})
         return me
 
     def ap(v):
@@ -277,9 +278,11 @@ def rank_program(g, core, T, topo):
     keeper("K16", 16, c16, V("c16", 16, 32), icol, 16)
     for name in ("M16", "r16", "r16m", "K16"):
         spread(name, 16, C)
-    iota(V("t16", 0, 20), [[16, 20]], 1024)
+    iota(V("t16", 0, 20), [[16, 20]])
     iota(V("t16", 20, 26), [[16, 6]])
     act(V("J", 0, 26), V("t16", 0, 26), Act.Identity, bias=icol)
+    act(V("KB"), V("K16"), Act.Copy)
+    act(V("J", 0, 20), V("J", 0, 20), Act.Identity, bias=V("KB", 15, 16))
     iota(V("CC", 0, 512), [[1, 8], [0, 64]])
     ts(V("CC", 0, 512), V("CC", 0, 512), gcol, Op.is_equal)
     quant("cq", "cs", 0, V("CC", 0, 512))
@@ -349,6 +352,9 @@ def rank_program(g, core, T, topo):
         a, b = slot[t]
         return V("BT", 4 * a + b, 4 * (a + n), 4)
 
+    def base(a, b):
+        return V("KB", 16 * a + 15, 16 * b, 16)
+
     flip = [0]
 
     def signs(n, col):
@@ -369,7 +375,7 @@ def rank_program(g, core, T, topo):
             scan(V("Fv", a, b), V("r16", a, b), V("Pm", a, b), 0.0, Op.add, Op.min)
         tt(rowview(0, C), V("Fv"), bank(4, 0, C), Op.is_ge)
         scan(V("DS"), V("r16m"), rowview(0, C), 0.0, Op.mult, Op.add)
-        tt(V("base"), V("J", 0, 20), V("DS", 15, C, 16), Op.subtract)
+        tt(base(0, 20), V("J", 0, 20), V("DS", 15, C, 16), Op.subtract)
         nv = DVE_ROWS[r]
         for t in range(19, nv, -1):
             s = signs(16 * t, V("Fv", 16 * t + 15, 16 * t + 16))
@@ -380,11 +386,11 @@ def rank_program(g, core, T, topo):
                 scan(V("SC", 208 * t - 16 * t, 208 * t), V("ones", 0, 16 * t), rowview(t, 16 * t), 0.0, Op.mult, Op.add)
         for b in range(4):
             scan(V("SC", 208 * b, 208 * b + 192), V("r192"), V("BT", 4 * 768 + b, 4 * 960, 4), 0.0, Op.mult, Op.add)
-        tt(V("base", 1, 5), V("base", 1, 5), V("SC", 191, 832, 208), Op.subtract)
-        tt(V("base", 5, 9), V("base", 5, 9), V("SC", 127, 832, 208), Op.subtract)
+        tt(base(1, 5), base(1, 5), V("SC", 191, 832, 208), Op.subtract)
+        tt(base(5, 9), base(5, 9), V("SC", 127, 832, 208), Op.subtract)
         if nv > 8:
-            tt(V("base", 9, nv + 1), V("base", 9, nv + 1), V("SC", 208 * 9 - 1, 208 * nv, 208), Op.subtract)
-        tt(V("base", nv + 1, 20), V("base", nv + 1, 20), V("RA", nv + 1, 20), Op.subtract)
+            tt(base(9, nv + 1), base(9, nv + 1), V("SC", 208 * 9 - 1, 208 * nv, 208), Op.subtract)
+        tt(base(nv + 1, 20), base(nv + 1, 20), V("RA", nv + 1, 20), Op.subtract)
         quant("bq", "bs", 0, V("BT", 0, 4 * 320))
         mm(7, "cq", "cs", 0, "bq", "bs", 0, 320, True, False)
         quant("bq", "bs", 768, V("BT", 4 * 768, 4 * 960))
@@ -394,9 +400,8 @@ def rank_program(g, core, T, topo):
         for a, n in late:
             quant("bq", "bs", a, V("BT", 4 * a, 4 * (a + n)))
             mm(7, "cq", "cs", 0, "bq", "bs", a, n, False, (a, n) == late[1])
-        scan(V("Fc"), bank(7, 0, C), V("K16"), -4096.0, Op.max, Op.add)
-        tt(V("rkf"), V("Fc", 15, C, 16), V("base"), Op.add)
-        cp(V("rk"), V("rkf"))
+        scan(V("Fc"), bank(7, 0, C), V("KB"), -4096.0, Op.max, Op.add)
+        ts(V("rk"), V("Fc", 15, C, 16), 1024.0, Op.add)
         cp(ind(V("O", 0, C), V("rk")), V("IO"))
         cp(V("O", C, 2 * C), V("O", 0, C))
 
@@ -501,7 +506,7 @@ def rank_program(g, core, T, topo):
             kids[d].append((i, l))
     tail = [0.0] * n
     for i in range(n - 1, -1, -1):
-        tail[i] = ops[i]["cost"] + ops[i]["boost"] + max([l + tail[k] for k, l in kids[i]] + [ops[i]["lat"]])
+        tail[i] = ops[i]["pc"] + ops[i]["boost"] + max([l + tail[k] for k, l in kids[i]] + [ops[i]["lat"]])
     left = [len(o["pre"]) for o in ops]
     ready = [0.0] * n
     free = {q: 0.0 for q in "vatgs"}
@@ -513,7 +518,7 @@ def rank_program(g, core, T, topo):
         q, first = ops[j0]["q"], at(j0)
         i = max((j for j in pool if ops[j]["q"] == q and at(j) <= first + SLACK), key=lambda j: tail[j])
         pool.remove(i)
-        free[q] = at(i) + ops[i]["cost"]
+        free[q] = at(i) + ops[i]["pc"]
         plan.append(i)
         for k, l in kids[i]:
             ready[k] = max(ready[k], free[q] + l)
@@ -523,23 +528,23 @@ def rank_program(g, core, T, topo):
 
     queue = {"v": g.vector, "a": g.scalar, "t": g.tensor, "g": g, "s": g.sync}
     needed = set(d for o in ops for d in o["deps"])
-    count, seen, mark, nd = {q: 0 for q in queue}, {q: {} for q in queue}, {}, 0
+    count, seen, mark, knew, nd = {q: 0 for q in queue}, {q: {} for q in queue}, {}, {}, 0
 
     def wait(q, sem, val):
         if seen[q].get(sem, 0) < val:
             queue[q].wait_ge(T.sem[sem], val)
             seen[q][sem] = val
 
+    place = {i: k for k, i in enumerate(plan)}
     for i in plan:
         o = ops[i]
-        want = {}
-        for d in o["deps"]:
-            s, v = mark[d]
-            want[s] = max(want.get(s, 0), v)
-        for s, v in want.items():
-            wait(o["q"], s, v)
+        for d in sorted(o["deps"], key=lambda d: -place[d]):
+            wait(o["q"], *mark[d])
+            for s, v in knew[d].items():
+                seen[o["q"]][s] = max(seen[o["q"]].get(s, 0), v)
         if o["ext"]:
             wait(o["q"], *o["ext"])
+        knew[i] = dict(seen[o["q"]])
         ins = o["fn"]()
         if o["kind"] == "d":
             mark[i] = ("d%d" % nd, 16)
@@ -551,4 +556,7 @@ def rank_program(g, core, T, topo):
             ins.then_inc(T.sem["q" + o["q"]], 1)
     for i in outs:
         wait(ops[i]["q"], *mark[i])
+    for q in "vatg":
+        if max(seen[k].get("q" + q, 0) for k in queue) < count[q]:
+            wait("g", "q" + q, count[q])
     g.wait_ge(T.sem.sent, R * sum(bits(p[4]) for call in calls for p in call))

@@ -3,17 +3,19 @@ from concourse.bass import DstId, RemoteDMATransfer
 from concourse.mybir import dt, AluOpType as Op, ActivationFunctionType as Act
 
 C, M, F, R = 320, 96, 4, 3
-BIG = 1.0e29
+BIG = 2.0 ** 93
 BF, F16, F32, I32, U16, Q4, U8 = "bfloat16", "float16", "float32", "int32", "uint16", "float8_e4m3fn_x4", "uint8"
 
-TILES = [(0, 320, (0, 19, 18, 17)), (320, 256, (16, 15, 14, 13)), (576, 192, (12, 11, 10, 9)),
+TILES = [(0, 320, (0, 17, 18, 19)), (320, 256, (13, 14, 15, 16)), (576, 192, (9, 10, 11, 12)),
          (768, 128, (5, 6, 7, 8)), (896, 64, (1, 2, 3, 4))]
-DVE_ROWS = [12, 12, 12]
-DVE_NROWS = [2, 2, 2]
-EB_DVE = 14
-Z_ACT = 2
+DVE_ROWS = 12
+SCW = 385
+LAYER = [0, 3, 2]
+JOIN = [(1, 0), (14, 13, 11, 10), (14, 12, 8, 7)]
+EB_DVE = 10
+Z_ACT = [(224, 320), (320, 384)]
+Z_DVE = [(96, 224), (0,), (1,), (0, 96), (128, 416, [2, 3]), (0, 128, [0, 1])]
 PIECES = [("c", 0, 48, 0), ("c", 48, 96, 2), ("s", 0, 96, 1)]
-CY, LAT, ADD, COMM, SLACK, BOOST, LOADU, LOADX = 0.83, 180.0, 30.0, 7000.0, 90.0, 1500.0, 2800.0, 3700.0
 
 
 def sb(n, t):
@@ -25,21 +27,21 @@ SCRATCH = {
     "X": sb(4 * (C + M), BF), "Xh": sb(4 * C, BF), "Y": sb(512, BF), "ub": sb(512, BF), "vb": sb(512, BF),
     "uq": sb(128, Q4), "us": sb(128, U8), "ugq": sb(128, Q4), "ugs": sb(128, U8), "vq": sb(128, Q4), "vs": sb(128, U8),
     "wq": sb(512, Q4), "wp": sb(512, U8), "aq": sb(448, Q4), "asc": sb(448, U8),
-    "E": sb(2048, BF), "eq": sb(512, Q4), "es": sb(512, U8), "CC": sb(1024, BF), "cq": sb(256, Q4), "cs": sb(256, U8),
-    "zq0": sb(128, Q4), "zs0": sb(128, U8), "BT": sb(4 * 960, BF), "bq": sb(1024, Q4), "bs": sb(1024, U8),
+    "I": sb(128, BF), "E": sb(2048, BF), "eq": sb(512, Q4), "es": sb(512, U8), "CC": sb(1024, BF), "cq": sb(256, Q4), "cs": sb(256, U8),
+    "BT": sb(4 * 960, BF), "bq": sb(1024, Q4), "bs": sb(1024, U8),
     "Z": sb(4 * 416, BF), "zq": sb(416, Q4), "zs": sb(416, U8), "Bw": sb(512, BF), "bwq": sb(128, Q4), "bws": sb(128, U8),
-    "ones": sb(512, BF), "pc": sb(8, I32), "pf": sb(8, F32), "c16": sb(32, BF), "c4": sb(96, BF),
-    "M16": sb(C, BF), "K16": sb(C, BF), "r16": sb(C, BF), "r16m": sb(C, BF), "r192": sb(192, BF), "K4": sb(384, BF),
-    "KB": sb(C, F32), "r2": sb(768, BF), "ZI": sb(1536, BF), "ZJ": sb(1536, BF),
-    "IO": sb(C, BF), "Kc": sb(384, F32), "CK": sb(336, BF), "B4": sb(64, F32), "t16": sb(26, F32), "J": sb(32, F32),
+    "ones": sb(512, BF), "pc": sb(24, I32), "pf": sb(16, F32), "c16": sb(C + 16, BF), "c4": sb(96, BF),
+    "M16": sb(C, BF), "K16": sb(M, BF), "r16": sb(C, BF), "rB": sb(384, BF), "K4": sb(384, BF),
+    "KB": sb(512, F32), "r2": sb(768, BF), "ZI": sb(1536, BF), "ZJ": sb(1536, BF),
+    "IO": sb(C, BF), "Kc": sb(384, F32), "CK": sb(360, BF), "B4": sb(64, F32), "B6": sb(24, F32), "t16": sb(26, F32), "J": sb(32, F32),
     "lui": sb(8, I32), "lu": sb(8, U16), "lwf": sb(8, F32), "lw": sb(2, U16), "lri": sb(8, F32), "lr": sb(6, U16),
-    "kp1": sb(16, I32), "kpb": sb(16, I32), "kpf": sb(4, F32), "z4": sb(4, F32),
-    "Pm": sb(C, F32), "Fv": sb(C, F32), "Sm": sb(M, F32), "Fs": sb(M, F32), "T0": sb(C, BF), "T1": sb(C, BF),
-    "SC": sb(13 * 208, BF), "DS": sb(C, BF), "RA": sb(20, F32), "Fc": sb(C, F32),
-    "rk": sb(20, U16), "O": sb(2 * C, BF), "NB": sb(6 * C, BF), "NS": sb(6 * C, BF), "nb": sb(6, F32),
+    "kp1": sb(16, I32), "kpb": sb(16, I32), "kpf": sb(4, F32), "z4": sb(4, F32), "ls": sb(2, U16),
+    "Pm": sb(C, F32), "Fv": sb(C, F32), "Sm": sb(M, F32), "Fs": sb(M, F32), "T0": sb(C, BF), "T1": sb(C, BF), "T2": sb(C, BF),
+    "SC": sb(4 * SCW, BF), "DS": sb(2 * C, F16), "RA": sb(20, F32), "Fc": sb(C, F32),
+    "rk": sb(20, U16), "O": sb(2 * C, BF), "NB": sb(6 * C, BF), "NS": sb(C, BF), "nb": sb(6, F32),
     "pos": sb(24, U16), "Fe": sb(384, F16), "eb": sb(384, BF), "zo": sb(96, U16),
     "pm": sb(8, F32), "idf": sb(8, F32), "wi": sb(6, U16), "hf": sb(32, F32), "ho": sb(24, U16), "so": sb(24, U16), "H": sb(384, BF),
-    "ewb": sb(M, BF), "Fw": sb(M, F32), "e5": sb(32, F32), "tg": sb(64, F32), "EQ": sb(336, BF), "ES": sb(336, BF),
+    "ewb": sb(M, BF), "Fw": sb(M, F32), "e5": sb(32, F32), "tg": sb(32, F32), "EQ": sb(360, BF), "ES": sb(360, BF),
     "RS": sb(384, F32), "KO": sb(R * M, F32), "yo": sb(C + M, F32),
 }
 for _r in range(R):
@@ -48,7 +50,7 @@ for _r in range(R):
         SCRATCH["%ss%d" % (_n, _r)] = sb(_w, U8)
 
 SEMAPHORES = (["qv", "qa", "qt", "qg", "sent"] + ["hop%d" % r for r in range(R)] + ["land%d" % r for r in range(R)]
-              + ["d%d" % k for k in range(40)])
+              + ["d%d" % k for k in range(48)])
 
 
 def helpers(topo, src, dst):
@@ -113,18 +115,17 @@ def rank_program(g, core, T, topo):
         if b is None:
             b = SCRATCH[name][1][1]
         rows = slice(None) if p is None else slice(p[0], p[1])
-        return {"ap": T[name][rows, a:b:s] if s > 1 else T[name][rows, a:b], "at": [(name, range(a, b, s))], "n": len(range(a, b, s)),
-                "two": SCRATCH[name][2] in (BF, F16, U16), "ps": SCRATCH[name][0] == "psum", "ind": False}
+        return {"ap": T[name][rows, a:b:s] if s > 1 else T[name][rows, a:b], "at": [(name, range(a, b, s))], "n": len(range(a, b, s)), "ind": False}
 
     def bank(k, a=0, b=512):
         return V("PA" if k < 4 else "PB", 512 * (k % 4) + a, 512 * (k % 4) + b)
 
     def ind(win, off, word=None):
         w = win["ap"].bitcast(word) if word else win["ap"]
-        return {"ap": w.indirect(off["ap"]), "at": win["at"] + off["at"], "n": 16 * off["n"], "two": False, "ps": False, "ind": True, "win": win, "off": off}
+        return {"ap": w.indirect(off["ap"]), "at": win["at"] + off["at"], "n": 16 * off["n"], "ind": True, "win": win, "off": off}
 
-    def add(q, fn, outs, ins, cost, lat=None, after=(), ext=None, soft=None, kind="c"):
-        me, deps, order = len(ops), set(after), set()
+    def add(q, fn, outs, ins, after=(), ext=None, kind="c"):
+        me, deps = len(ops), set(after)
         reads, writes = [], []
         for v in ins:
             if isinstance(v, dict):
@@ -141,7 +142,8 @@ def rank_program(g, core, T, topo):
                     deps.update(o for o in lastr[n][c] if ops[o]["q"] != q)
         for n, cols in writes:
             for c in whole(n, cols):
-                (order if psum(n) else deps).add(int(lastw[n][c]))
+                if not psum(n):
+                    deps.add(int(lastw[n][c]))
                 deps.update(lastr[n][c])
         for n, cols in reads:
             for c in whole(n, cols):
@@ -151,50 +153,35 @@ def rank_program(g, core, T, topo):
                 lastw[n][c] = me
                 lastr[n][c] = set()
         deps -= {-1, me}
-        order.discard(-1)
-        ops.append({"q": q, "fn": fn, "deps": deps, "order": order - deps, "cost": cost, "pc": cost + (ADD if kind == "c" and q in "va" else 0.0),
-                    "lat": LAT if lat is None else lat, "ext": ext, "soft": soft, "kind": kind, "boost": 0.0})
+        ops.append({"q": q, "fn": fn, "deps": deps, "ext": ext, "kind": kind})
         return me
 
     def ap(v):
         return v["ap"] if isinstance(v, dict) else v
-
-    def plain(n, f=1.0):
-        return max(64.0, n * f) * CY
-
-    def vcost(out, a, f):
-        if out["ind"]:
-            return 50 + out["n"] * 3.8 * CY
-        if a["ind"]:
-            return 50 + out["n"] * 1.56 * CY
-        return plain(out["n"], f)
-
-    def fast(*vs):
-        return 0.5 if all(v["two"] for v in vs) else 1.0
 
     def ts(out, in0, s1, op0, s2=None, op1=None):
         if op1 is None:
             fn = lambda: g.vector.tensor_scalar(out["ap"], in0["ap"], ap(s1), None, op0)
         else:
             fn = lambda: g.vector.tensor_scalar(out["ap"], in0["ap"], ap(s1), ap(s2), op0, op1)
-        return add("v", fn, [out], [in0, s1, s2], vcost(out, in0, fast(out, in0)))
+        add("v", fn, [out], [in0, s1, s2])
 
     def tt(out, a, b, op):
-        return add("v", lambda: g.vector.tensor_tensor(out["ap"], a["ap"], b["ap"], op), [out], [a, b], vcost(out, a, 1.0 if a["ps"] or b["ps"] else 2.0))
+        add("v", lambda: g.vector.tensor_tensor(out["ap"], a["ap"], b["ap"], op), [out], [a, b])
 
     def cp(out, a):
-        return add("v", lambda: g.vector.tensor_copy(out["ap"], a["ap"]), [out], [a], vcost(out, a, fast(out, a)))
+        add("v", lambda: g.vector.tensor_copy(out["ap"], a["ap"]), [out], [a])
 
     def scan(out, d0, d1, init, op0, op1):
-        return add("v", lambda: g.vector.tensor_tensor_scan(out["ap"], d0["ap"], d1["ap"], init, op0, op1), [out], [d0, d1], plain(out["n"], fast(out, d0, d1)))
+        add("v", lambda: g.vector.tensor_tensor_scan(out["ap"], d0["ap"], d1["ap"], init, op0, op1), [out], [d0, d1])
 
     def fill(out, c):
-        return add("v", lambda: g.vector.memset(out["ap"], c), [out], [], plain(out["n"], fast(out)))
+        add("v", lambda: g.vector.memset(out["ap"], c), [out], [])
 
     def quant(q, s, a, src):
         n = src["n"] // 4
         oq, osc = V(q, a, a + n), V(s, a, a + n)
-        return add("v", lambda: g.vector.quantize_mx(oq["ap"], osc["ap"], src["ap"]), [oq, osc], [src], 12 + 0.22 * src["n"])
+        add("v", lambda: g.vector.quantize_mx(oq["ap"], osc["ap"], src["ap"]), [oq, osc], [src])
 
     def act(out, a, func, bias=None, scale=None, acc=None):
         kw = {}
@@ -204,147 +191,217 @@ def rank_program(g, core, T, topo):
             kw["scale"] = scale
         if acc is not None:
             kw["accum_out"] = acc["ap"]
-        cost = 65 + out["n"] * 1.56 * CY if a["ind"] else plain(out["n"]) + (20 if acc else 0)
-        return add("a", lambda: g.scalar.activation(out["ap"], a["ap"], func, **kw), [out] + ([acc] if acc else []), [a, bias], cost)
+        add("a", lambda: g.scalar.activation(out["ap"], a["ap"], func, **kw), [out] + ([acc] if acc else []), [a, bias])
 
-    def mm(k, lq, ls, la, rq, rs, ra, n, start=True, stop=True, ext=None, soft=None):
+    def mm(k, lq, ls, la, rq, rs, ra, n, start=True, stop=True, ext=None):
         o, l, l2, m1, m2 = bank(k, 0, n), V(lq, la, la + 128), V(ls, la, la + 128), V(rq, ra, ra + n), V(rs, ra, ra + n)
-        return add("t", lambda: g.tensor.matmul_mx(o["ap"], l["ap"], l2["ap"], m1["ap"], m2["ap"], start, stop), [o], [l, l2, m1, m2], (n + 16) * 0.6, ext=ext, soft=soft)
+        add("t", lambda: g.tensor.matmul_mx(o["ap"], l["ap"], l2["ap"], m1["ap"], m2["ap"], start, stop), [o], [l, l2, m1, m2], ext=ext)
 
     def iota(out, pattern, base=0, cm=0):
         if SCRATCH[out["at"][0][0]][2] == I32:
             fn = lambda: g.iota(out["ap"], pattern, base, cm)
         else:
             fn = lambda: g.iota(out["ap"], pattern, base, cm, allow_small_or_imprecise_dtypes=True)
-        return add("g", fn, [out], [], 130 + 2 * CY * out["n"])
+        add("g", fn, [out], [])
 
-    def dma(q, out, in_, after=(), lat=2000.0, slow=False):
+    def dma(q, out, in_, after=(), slow=False):
         eng = {"s": g.sync, "a": g.scalar, "g": g}[q]
         if slow:
             fn = lambda: eng.dma_start(ap(out), ap(in_), allow_slow_non_contiguous=True)
         else:
             fn = lambda: eng.dma_start(ap(out), ap(in_))
-        return add(q, fn, [out] if isinstance(out, dict) else [], [in_], 60.0, lat=lat, after=after, kind="d")
+        return add(q, fn, [out] if isinstance(out, dict) else [], [in_], after=after, kind="d")
 
     def cast(v, t):
         w = dict(v)
         w["ap"] = v["ap"].bitcast(t)
         return w
 
-    def pick(oq, os_, q, s, n, off):
+    def acopy(out, a):
+        act(out, a, Act.Copy)
+
+    def gcopy(out, a):
+        add("g", lambda: g.affine_select(out["ap"], a["ap"], [[0, out["n"]]], Op.is_equal, 0.0, 0, 0), [out], [a])
+
+    def pick_codes(oq, q, n, off):
         cp(cast(V(oq, 0, 16 * off["n"]), dt.uint32), ind(V(q, 0, n), off, dt.uint32))
-        act(V(os_, 0, 16 * off["n"]), ind(V(s, 0, n), off), Act.Copy)
+
+    def pick_scales(os_, s, n, off):
+        acopy(V(os_, 0, 16 * off["n"]), ind(V(s, 0, n), off))
 
     def spread(name, w, n, a=0):
         while w < n:
             k = min(w, n - w)
-            act(V(name, a + w, a + w + k), V(name, a, a + k), Act.Copy)
+            gcopy(V(name, a + w, a + w + k), V(name, a, a + k))
             w += k
 
-    def keeper(name, n, c, tmp, col, w):
+    def keeper(name, n, c, tmp, col, w, unit):
         out = V(name, 0, n)
-        ts(out, c, col, Op.is_lt, -4096.0, Op.mult)
-        ts(tmp, c, col, Op.is_equal, 1024.0, Op.mult)
-        tt(out, out, tmp, Op.add)
-        ts(V(name, w - 1, n, w), V(name, w - 1, n, w), -2048.0, Op.add)
 
-    def zero(v):
-        act(v, V("ones", 0, v["n"]), Act.Copy, scale=0.0)
+        def first():
+            ts(out, c, col, Op.is_lt, -4.0 * unit, Op.mult)
+            ts(tmp, c, col, Op.is_equal, unit, Op.mult)
+        return first, lambda: tt(out, out, tmp, Op.add), lambda: ts(V(name, w - 1, n, w), V(name, w - 1, n, w), -2.0 * unit, Op.add)
 
-    dma("a", V("ub"), T.u[:], lat=LOADU)
-    lx = dma("s", V("X", 0, 4 * C), T.x[:], lat=LOADX)
-    dma("a", V("Y", 0, 4 * M), T.m[:], lat=LOADU)
-    dma("s", cast(V("wq"), dt.uint8), T.wc[:], after=[lx])
-    dma("s", V("wp"), T.ws[:], after=[lx])
-    dma("s", V("vb"), T.v[:], after=[lx])
-    dma("g", V("kp1", p=(0, 1)), T.kap[:], slow=True)
+    def pad(k):
+        a, n, _ = TILES[k]
+        fill(V("BT", 4 * (a + n - 48), 4 * (a + n)), 0.0)
 
-    fill(V("ones"), 1.0)
-    iota(V("pc", 0, 2), [[1, 2]], 0, 1)
-    ts(V("pc", 2, 4), V("pc", 0, 2), 3, Op.bitwise_and)
-    ts(V("pc", 4, 5), V("pc", 0, 1), 15, Op.bitwise_and)
-    ts(V("pc", 5, 6), V("pc", 0, 1), 4, Op.arith_shift_right)
-    ts(V("pc", 6, 7), V("pc", 0, 1), 2, Op.arith_shift_right, 3, Op.bitwise_and)
-    cp(V("pf", 0, 5), V("pc", 2, 7))
-    bcol, b1col, icol, gcol, i4col = (V("pf", k, k + 1) for k in range(5))
-    ts(V("pf", 5, 6), bcol, 4.0 * (160 + 1024), Op.add)
+    dma("s", V("ub"), T.u[:])
+    lx = dma("s", V("X", 0, 4 * C), T.x[:])
+    dma("s", V("Y", 0, 4 * M), T.m[:])
+
+    bcol, b1col, _, bmcol, i4col, qcol, icol, gcol, zcol, mcol, s0, s1, ecol, socol, lcol = (V("pf", k, k + 1) for k in range(15))
+    tri = [8 * t * t + 12 * t for t in range(7)]
+    iota(V("pc", 0, 16), [[1, 16]], 0, 1)
+    iota(V("c16", 0, C), [[0, 20], [1, 16]])
     iota(V("lui"), [[16, 8]])
-    cp(V("lu"), V("lui"))
-    c16 = V("c16", 0, 16)
-    iota(c16, [[1, 16]])
-    ts(V("M16", 0, 16), c16, icol, Op.not_equal, BIG, Op.mult)
-    ts(V("r16", 0, 16), c16, 0.0, Op.is_equal, 2 * BIG, Op.mult)
-    act(V("r16m", 0, 16), c16, Act.Sign)
-    keeper("K16", 16, c16, V("c16", 16, 32), icol, 16)
-    for name in ("M16", "r16", "r16m", "K16"):
-        spread(name, 16, C)
     iota(V("t16", 0, 20), [[16, 20]])
     iota(V("t16", 20, 26), [[16, 6]])
-    act(V("J", 0, 26), V("t16", 0, 26), Act.Identity, bias=icol)
-    act(V("KB"), V("K16"), Act.Copy)
-    act(V("J", 0, 20), V("J", 0, 20), Act.Identity, bias=V("KB", 15, 16))
-    iota(V("CC", 0, 512), [[1, 8], [0, 64]])
-    ts(V("CC", 0, 512), V("CC", 0, 512), gcol, Op.is_equal)
-    quant("cq", "cs", 0, V("CC", 0, 512))
-    iota(V("IO"), [[1, C]], -160)
-    add("g", lambda: g.partition_broadcast(T.kpb[:], T.kp1[0:1, :], 128), [V("kpb")], [V("kp1")], 200.0)
-    cp(V("kpf"), V("kpb", 0, 4))
     iota(V("c4", 0, 48), [[0, 12], [1, 4]])
-    keeper("K4", 48, V("c4", 0, 48), V("c4", 48, 96), i4col, 4)
-    spread("K4", 48, 384)
     iota(V("CC", 512, 576), [[1, 16], [0, 4]])
-    ts(V("CC", 512, 576), V("CC", 512, 576), icol, Op.is_equal, float(M), Op.mult)
-    spread("CC", 64, 512, 512)
-    quant("cq", "cs", 128, V("CC", 512, 1024))
+    dma("g", V("kp1", p=(0, 1)), T.kap[:], slow=True)
+    iota(V("IO"), [[1, C]], -160)
+    iota(V("CC", 0, 512), [[1, 8], [0, 64]])
     iota(V("lwf", 0, 2), [[4, 2]])
-    fill(V("lwf", 4, 5), 1.5)
-    fill(V("lwf", 5, 6), 1.0)
-    ts(V("lwf", 2, 4), V("lwf", 0, 2), i4col, Op.add, gcol, Op.is_equal)
-    ts(V("lw"), V("lwf", 2, 4), b1col, Op.mult)
-    iota(V("pm", 0, 1), [[0, 1]], 1)
-    act(V("pm", 0, 1), V("pm", 0, 1), Act.Copy, scale=BIG)
-    ts(V("lri", 0, 2), V("lwf", 0, 2), i4col, Op.add, 5.0, Op.min)
-    cp(V("lr", 0, 2), V("lri", 0, 2))
-    ts(V("lr", 2, 4), V("lri", 0, 2), 16.0, Op.mult, 15.0, Op.add)
-    act(V("lri", 2, 4), V("lri", 0, 2), Act.Square, bias=V("lwf", 4, 5))
-    ts(V("lr", 4, 6), V("lri", 2, 4), 8.0, Op.mult, -4.0, Op.add)
-    iota(V("B4", 0, 32), [[0, 8], [1, 4]], 4 * 1536)
-    act(V("B4", 0, 32), V("B4", 0, 32), Act.Copy, scale=0.25)
-    iota(V("B4", 32, 56), [[64, 6], [1, 4]], 4 * 672)
-    act(V("B4", 32, 56), V("B4", 32, 56), Act.Identity, scale=0.25, bias=icol)
-    iota(V("r2", 0, 48), [[0, 24], [1, 2]])
-    spread("r2", 48, 768)
-    iota(V("idf"), [[0, 8]])
-    iota(V("z4"), [[0, 4]])
-    iota(V("Kc"), [[1, 4], [0, M]])
-    tri = [8 * t * (t + 1) for t in range(7)]
-    for t in range(6):
-        iota(V("CK", tri[t], tri[t + 1]), [[1, 16 * t + 16]], 1 - 16 * t)
-    ts(V("CK"), V("CK"), icol, Op.is_equal, 4096.0, Op.mult)
-    act(V("CK"), V("CK"), Act.Identity, bias=V("lwf", 5, 6))
-    for t in range(6):
-        iota(V("CK", tri[t + 1] - 1, tri[t + 1]), [[0, 1]])
-    act(V("r192"), V("ones", 0, 192), Act.Copy)
-    iota(V("r192", 128, 129), [[0, 1]])
-    for b in range(4):
-        o = V("E", 512 * b, 512 * b + 512)
-        add("g", lambda o=o, b=b: g.affine_select(o["ap"], T.ones[:], [[8, 128], [1, 4]], Op.is_equal, 0.0, -b, -8), [o], [V("ones")], 170 + 2 * CY * 512)
-    quant("eq", "es", 0, V("E", 0, 1024))
-    quant("eq", "es", 256, V("E", 1024, 2048))
-    zero(V("Bw"))
-    quant("zq0", "zs0", 0, V("Bw"))
-    dma("s", cast(V("bq", 960, 1024), dt.uint8), cast(V("zq0", 0, 64), dt.uint8))
-    dma("s", V("bs", 960, 1024), V("zs0", 0, 64))
-    for r in range(R):
-        dma("s", cast(V("landc%d" % r, M, 128), dt.uint8), cast(V("zq0", 0, 32), dt.uint8))
-        dma("s", V("lands%d" % r, M, 128), V("zs0", 0, 32))
-    for a, n, _ in TILES:
-        fill(V("BT", 4 * (a + n - 48), 4 * (a + n)), 0.0)
+    iota(V("SC", 0, 4 * SCW, SCW), [[0, 4]])
+
+    fill(V("ones"), 1.0)
+    ts(V("pc", 16, 20), V("pc", 0, 4), 3, Op.bitwise_and)
+    ts(V("pc", 20, 22), V("pc", 0, 16, 15), 2, Op.arith_shift_right, 3, Op.bitwise_and)
+    ts(V("pc", 22, 23), V("pc", 0, 1), 15, Op.bitwise_and)
+    ts(V("pc", 23, 24), V("pc", 0, 1), 4, Op.arith_shift_right)
+    pad(0)
+    cp(V("pf", 0, 8), V("pc", 16, 24))
+    pad(1)
+    act(V("Bw"), V("ones"), Act.Copy, scale=0.0)
+    act(mcol, icol, Act.Copy, scale=-BIG)
+    act(V("r16"), V("c16", 0, C), Act.Relu, scale=-BIG, bias=BIG)
+    act(V("M16"), V("c16", 0, C), Act.Abs, scale=BIG, bias=mcol)
+    k16 = keeper("KB", 16, V("c16", 0, 16), V("c16", C, C + 16), icol, 16, 512.0)
+    k4 = keeper("K4", 48, V("c4", 0, 48), V("c4", 48, 96), i4col, 4, 1.0)
+    k16[0]()
+    cp(V("lu"), V("lui"))
+    k16[1]()
     fill(V("Y", 4 * M, 512), 0.0)
-    zero(V("Z", 4 * F * M, 4 * 416))
+    k16[2]()
+    quant("bq", "bs", 896, V("Bw"))
     quant("uq", "us", 0, V("ub"))
-    pick("ugq", "ugs", "uq", "us", 128, V("lu"))
-    quant("vq", "vs", 0, V("vb"))
+    k4[0]()
+    pick_codes("ugq", "uq", 128, V("lu"))
+    k4[1]()
+    pad(2)
+    k4[2]()
+    ts(V("DS", C, 2 * C), V("c16", 0, C), 0.0, Op.is_gt, -2048.0, Op.mult)
+    dma("s", V("rB"), V("ones", 0, 384), after=[lx])
+    dma("s", cast(V("wq"), dt.uint8), T.wc[:])
+    dma("s", V("wp"), T.ws[:])
+    dma("s", V("vb"), T.v[:])
+    dma("s", V("Z", 4 * F * M, 4 * 416), V("Bw", 0, 128))
+    for a in range(0, 2048, 512):
+        dma("s", V("E", a, a + 512), V("Bw"))
+    for r in range(R):
+        dma("s", cast(V("landc%d" % r, M, 128), dt.uint8), cast(V("bq", 960, 992), dt.uint8))
+        dma("s", V("lands%d" % r, M, 128), V("bs", 960, 992))
+    acopy(V("KB", 16, 32), V("KB", 0, 16))
+    act(s0, qcol, Act.Square, bias=0.5)
+    acopy(V("KB", 32, 64), V("KB", 0, 32))
+    act(s1, s0, Act.Identity, scale=-32.0, bias=392.0)
+    acopy(V("KB", 64, 128), V("KB", 0, 64))
+    pick_scales("ugs", "us", 128, V("lu"))
+    acopy(V("KB", 128, 256), V("KB", 0, 128))
+    act(V("J", 0, 26), V("t16", 0, 26), Act.Identity, bias=icol)
+    acopy(V("KB", 256, C), V("KB", 0, 64))
+    act(V("K16"), V("KB", 0, M), Act.Copy, scale=1 / 512)
+
+    def after_x():
+        pad(3)
+        pad(4)
+        ts(V("CC", 512, 576), V("CC", 512, 576), icol, Op.is_equal, float(M), Op.mult)
+        spread("K4", 48, 384)
+        for a, n, rows in TILES[2:]:
+            iota(V("rB", a - 576, a - 575), [[0, 1]])
+        iota(V("r2"), [[0, 384], [1, 2]])
+        add("g", lambda: g.partition_broadcast(T.kpb[:], T.kp1[0:1, :], 128), [V("kpb")], [V("kp1")])
+        for t in range(6):
+            iota(V("CK", tri[t], tri[t + 1]), [[1, 16 * t + 20]], 1 - 16 * t)
+        iota(V("pm", 0, 1), [[0, 1]], 1)
+        iota(V("B4", 0, 32), [[0, 8], [1, 4]], 4 * 1024)
+        spread("CC", 64, 512, 512)
+
+    def after_halves():
+        act(V("IO"), V("IO"), Act.Copy, scale=1 / 512)
+
+    def after_mask():
+        ts(V("DS", C, 2 * C, 16), V("J", 0, 20), V("KB", 15, 16), Op.add)
+        fill(V("ls", 1, 2), 3 * SCW)
+
+    def after_own():
+        ts(V("CC", 0, 512), V("CC", 0, 512), gcol, Op.is_equal)
+
+    def after_message():
+        quant("cq", "cs", 0, V("CC", 0, 512))
+
+    def before_diagonal():
+        ts(V("ls", 0, 1), bmcol, float(SCW), Op.mult, s1, Op.add)
+
+    def after_counts():
+        iota(V("B4", 32, 64), [[0, 8], [1, 4]], 4 * 304)
+        iota(V("B6"), [[0, 24]], 1)
+        iota(V("z4"), [[0, 4]])
+        iota(V("B6", 0, 24, 4), [[64, 6]], -4096 - 192)
+        iota(V("idf"), [[0, 8]])
+        add("g", lambda: g.affine_select(T.I[:], T.ones[:, 0:128], [[1, 128]], Op.is_equal, 0.0, 0, -1), [V("I")], [V("ones", 0, 128)])
+
+    def before_base():
+        ts(V("lwf", 2, 4), V("lwf", 0, 2), i4col, Op.add, gcol, Op.is_equal)
+
+    def before_places():
+        cp(V("kpf"), V("kpb", 0, 4))
+
+    def before_ranks():
+        ts(V("lri", 0, 2), V("lwf", 0, 2), i4col, Op.add, 5.0, Op.min)
+
+    def before_order():
+        ts(V("lw"), V("lwf", 2, 4), b1col, Op.mult)
+
+    def after_order():
+        cp(V("lr", 0, 2), V("lri", 0, 2))
+        act(zcol, bcol, Act.Identity, bias=4.0 * (160 + 512))
+        act(V("pm", 0, 1), V("pm", 0, 1), Act.Copy, scale=BIG)
+        act(V("lri", 2, 4), V("lri", 0, 2), Act.Square, bias=1.75)
+        act(lcol, bcol, Act.Identity, bias=-8.5)
+        act(ecol, icol, Act.Copy, scale=-1 / 512)
+        act(V("B4", 0, 32), V("B4", 0, 32), Act.Copy, scale=0.25)
+        act(socol, icol, Act.Identity, scale=4.0, bias=4.0 * 368)
+
+    def after_lookup():
+        ts(V("CK"), V("CK"), icol, Op.is_equal)
+
+    def after_discs():
+        ts(V("lr", 2, 4), V("lri", 0, 2), 16.0, Op.mult, 15.0, Op.add)
+
+    def after_offsets():
+        ts(V("lr", 4, 6), V("lri", 2, 4), 8.0, Op.mult, lcol, Op.add)
+
+    def after_readings():
+        quant("cq", "cs", 128, V("CC", 512, 1024))
+        act(V("B4", 32, 64), V("B4", 32, 64), Act.Identity, scale=1 / 2048, bias=ecol)
+        iota(V("Kc"), [[1, 4], [0, M]])
+        for t in range(6):
+            act(V("CK", tri[t + 1] - 4, tri[t + 1]), V("B6", 4 * t, 4 * t + 4), Act.Copy, scale=1 / 2048)
+            iota(V("EQ", tri[t + 1] - 4, tri[t + 1]), [[0, 4]], -4)
+        for b in range(4):
+            acopy(V("E", 512 * b + b, 512 * b + 512, 4), V("I"))
+
+    def after_bits():
+        quant("eq", "es", 0, V("E", 0, 1024))
+
+    def after_twins():
+        quant("eq", "es", 256, V("E", 1024, 1536))
+
+    def after_spare():
+        quant("eq", "es", 384, V("E", 1536, 2048))
 
     slot = {t: (a, b) for a, n, rows in TILES for b, t in enumerate(rows)}
 
@@ -352,101 +409,173 @@ def rank_program(g, core, T, topo):
         a, b = slot[t]
         return V("BT", 4 * a + b, 4 * (a + n), 4)
 
-    def base(a, b):
-        return V("KB", 16 * a + 15, 16 * b, 16)
+    def message(r):
+        lc, ls, ext = "landc%d" % r, "lands%d" % r, ("land%d" % r, landing)
+        wb, db = (0, 1, 2, 3), (6, 7, 0, 1) if r < R - 1 else (6, 7, 4, 5)
 
-    flip = [0]
+        def layer():
+            for b in range(4):
+                mm(wb[b], "wq", "wp", 128 * b, lc, ls, 0, 128, ext=ext)
+                act(V("RS", M * b, M * b + M), bank(wb[b], 0, M), Act.Relu, scale=0.03125)
+                for k in [b] if r == R - 1 else range(4) if b == 3 else []:
+                    mm(db[k], "eq", "es", 128 * k, lc, ls, 0, 128, ext=ext)
 
-    def signs(n, col):
-        flip[0] ^= 1
-        o = V("T%d" % flip[0], 0, n)
-        act(o, bank(5, 0, n), Act.Sign, bias=col, scale=-1.0)
-        return o
+        def join():
+            for b in range(4):
+                tt(V("Y", b, 4 * M, 4), V("RS", M * b, M * b + M), bank(db[b], 0, M), Op.add)
+        return layer, join
+
+    def vrow(t):
+        ts(rowview(t, 16 * t), bank(4, 0, 16 * t), V("Fv", 16 * t + 15, 16 * t + 16), Op.is_lt)
+
+    waiting = []
+
+    def counted(n, col, out, acc, scale):
+        signs = V("T%d" % (len(waiting) % 3), 0, n)
+        act(signs, bank(5, 0, n), Act.Sign, bias=col, scale=-1.0)
+        finish()
+        waiting.append(lambda: act(out, signs, Act.Relu, scale=scale, acc=acc))
+
+    def finish():
+        if waiting and waiting[-1]:
+            waiting[-1]()
+            waiting[-1] = None
+
+    def nrows(rows):
+        for t in rows:
+            counted(C, V("Fs", 16 * t + 15, 16 * t + 16), V("NB", C * t, C * t + C), V("nb", t, t + 1), -1.0)
+
+    def across(a, b, last=False):
+        quant("bq", "bs", a, V("BT", 4 * a, 4 * b))
+        for a1, n, _ in TILES:
+            if a <= a1 < b:
+                mm(7, "cq", "cs", 0, "bq", "bs", a1, max(n, 128), a1 == 0, last and a1 + n == b)
+
+    def scores():
+        quant("aq", "asc", C, V("Y"))
+        mm(6, "ugq", "ugs", 0, "aq", "asc", C, 128)
+
+    def zspan(a, b, k=0):
+        return 768 * k + 8 * (a % M), 768 * k + 8 * (a % M + b - a)
 
     outs = []
     for r in range(R):
-        quant("aq", "asc", 0, V("X", 0, 4 * C))
+        layer, join = message(r - 1) if r else (lambda: None, None)
+        once = (lambda f: None) if r else (lambda f: f())
+        quant("aq", "asc", 160, V("X", 640, 4 * C))
+        mm(7, "ugq", "ugs", 0, "aq", "asc", 160, 160)
+        quant("aq", "asc", 0, V("X", 0, 640))
         mm(4, "ugq", "ugs", 0, "aq", "asc", 0, C)
         mm(5, "ugq", "ugs", 0, "aq", "asc", 0, C)
+        once(scores)
+        once(after_x)
+        if r == 1:
+            quant("vq", "vs", 0, V("vb"))
         for h in range(4):
             act(V("Xh", C * h, C * h + C), V("X", C * h, C * h + C), Act.Copy, scale=0.5)
-        for a, b in ((160, C), (0, 160)):
-            tt(V("Pm", a, b), bank(4, a, b), V("M16", a, b), Op.add)
-            scan(V("Fv", a, b), V("r16", a, b), V("Pm", a, b), 0.0, Op.add, Op.min)
-        tt(rowview(0, C), V("Fv"), bank(4, 0, C), Op.is_ge)
-        scan(V("DS"), V("r16m"), rowview(0, C), 0.0, Op.mult, Op.add)
-        tt(base(0, 20), V("J", 0, 20), V("DS", 15, C, 16), Op.subtract)
-        nv = DVE_ROWS[r]
-        for t in range(19, nv, -1):
-            s = signs(16 * t, V("Fv", 16 * t + 15, 16 * t + 16))
-            act(rowview(t, 16 * t), s, Act.Relu, acc=V("RA", t, t + 1))
-        for t in range(nv, 0, -1):
-            ts(rowview(t, 16 * t), bank(4, 0, 16 * t), V("Fv", 16 * t + 15, 16 * t + 16), Op.is_lt)
-            if t > 8:
-                scan(V("SC", 208 * t - 16 * t, 208 * t), V("ones", 0, 16 * t), rowview(t, 16 * t), 0.0, Op.mult, Op.add)
-        for b in range(4):
-            scan(V("SC", 208 * b, 208 * b + 192), V("r192"), V("BT", 4 * 768 + b, 4 * 960, 4), 0.0, Op.mult, Op.add)
-        tt(base(1, 5), base(1, 5), V("SC", 191, 832, 208), Op.subtract)
-        tt(base(5, 9), base(5, 9), V("SC", 127, 832, 208), Op.subtract)
-        if nv > 8:
-            tt(base(9, nv + 1), base(9, nv + 1), V("SC", 208 * 9 - 1, 208 * nv, 208), Op.subtract)
-        tt(base(nv + 1, 20), base(nv + 1, 20), V("RA", nv + 1, 20), Op.subtract)
-        quant("bq", "bs", 0, V("BT", 0, 4 * 320))
-        mm(7, "cq", "cs", 0, "bq", "bs", 0, 320, True, False)
-        quant("bq", "bs", 768, V("BT", 4 * 768, 4 * 960))
-        mm(7, "cq", "cs", 0, "bq", "bs", 768, 128, False, False)
-        mm(7, "cq", "cs", 0, "bq", "bs", 896, 128, False, False)
-        late = ((320, 256), (576, 192)) if nv < 12 else ((576, 192), (320, 256))
-        for a, n in late:
-            quant("bq", "bs", a, V("BT", 4 * a, 4 * (a + n)))
-            mm(7, "cq", "cs", 0, "bq", "bs", a, n, False, (a, n) == late[1])
-        scan(V("Fc"), bank(7, 0, C), V("KB"), -4096.0, Op.max, Op.add)
-        ts(V("rk"), V("Fc", 15, C, 16), 1024.0, Op.add)
-        cp(ind(V("O", 0, C), V("rk")), V("IO"))
-        cp(V("O", C, 2 * C), V("O", 0, C))
+        once(after_halves)
+        tt(V("Pm", 160, C), bank(7, 0, 160), V("M16", 160, C), Op.add)
+        once(after_mask)
+        scan(V("Fv", 160, C), V("r16", 160, C), V("Pm", 160, C), 0.0, Op.add, Op.min)
+        tt(V("Pm", 0, 160), bank(4, 0, 160), V("M16", 0, 160), Op.add)
+        vrow(12)
+        scan(V("Fv", 0, 160), V("r16", 0, 160), V("Pm", 0, 160), 0.0, Op.add, Op.min)
+        for k, t in enumerate(range(19, DVE_ROWS, -1)):
+            if k == LAYER[r]:
+                layer()
+            counted(16 * t, V("Fv", 16 * t + 15, 16 * t + 16), rowview(t, 16 * t), V("RA", t, t + 1), 1.0)
 
-        quant("aq", "asc", C, V("Y"))
-        for a in range(0, 768 * Z_ACT, 768):
-            act(V("ZI", a + 1, a + 768, 2), V("Y", 0, 4 * M), Act.Copy, scale=0.5)
-        mm(6, "ugq", "ugs", 0, "aq", "asc", C, 128)
-        tt(V("Sm"), bank(6, 0, M), V("M16", 0, M), Op.add)
-        ops[scan(V("Fs"), V("r16", 0, M), V("Sm"), 0.0, Op.add, Op.min)]["boost"] = BOOST if r else 0.0
-        nn = DVE_NROWS[r]
-        for t in range(6):
-            col, row = V("Fs", 16 * t + 15, 16 * t + 16), V("NB", C * t, C * t + C)
-            if t < nn:
-                ts(row, bank(4, 0, C), col, Op.is_gt)
-                scan(V("NS", C * t, C * t + C), V("ones", 0, C), row, -160.0, Op.mult, Op.add)
-            else:
-                act(row, signs(C, col), Act.Relu, scale=-1.0, acc=V("nb", t, t + 1))
-        ts(V("nb", 0, nn), V("NS", C - 1, C * nn, C), 160.0, Op.add)
+        def diagonal():
+            tt(rowview(0, C), V("Fv"), bank(4, 0, C), Op.is_ge)
+
+        def diagonal_sums():
+            once(before_diagonal)
+            scan(V("DS", 0, C), V("DS", C, 2 * C), rowview(0, C), -2048.0, Op.max, Op.subtract)
+
+        def masked():
+            tt(V("Sm"), bank(6, 0, M), V("M16", 0, M), Op.add)
+            once(after_own)
+
+        def least():
+            scan(V("Fs"), V("r16", 0, M), V("Sm"), 0.0, Op.add, Op.min)
+            once(after_message)
+
+        steps = [lambda t=t: vrow(t) for t in (11, 10)] + [diagonal] + [lambda t=t: vrow(t) for t in range(9, 0, -1)]
+        steps += [diagonal_sums, lambda: across(0, 320), lambda: across(576, 960)]
+        for k, f in zip(JOIN[r], (least, masked, scores, join)):
+            steps.insert(k, f)
+        for f in steps:
+            f()
+        nrows([5])
+        for b in range(4):
+            scan(V("SC", SCW * b + 1, SCW * b + SCW), V("rB"), V("BT", 4 * 576 + b, 4 * 960, 4), 0.0, Op.mult, Op.subtract)
+        across(320, 576, True)
+        ends = V("DS", 16 * DVE_ROWS + 31, C, 16)
+        tt(ends, ends, V("RA", DVE_ROWS + 1, 20), Op.subtract)
+        nrows([4, 3, 2, 1])
+        finish()
+        act(V("ZI", 1, 768, 2), V("Y", 0, 4 * M), Act.Copy, scale=0.5)
+        gcopy(V("ZI", 769, 1536, 2), V("ZI", 1, 768, 2))
+        once(after_counts)
+        once(before_base)
+        ts(V("NB", 0, 160), bank(4, 0, 160), V("Fs", 15, 16), Op.is_gt)
+        tt(V("KB", 15, 512, 16), ind(V("SC"), V("ls")), V("DS", 15, 512, 16), Op.add)
+        once(before_places)
+        ts(V("NB", 160, C), bank(4, 160, C), V("Fs", 15, 16), Op.is_gt)
+        scan(V("Fc"), bank(7, 0, C), V("KB", 0, C), -4096.0, Op.max, Op.add)
+        once(before_ranks)
+        scan(V("NS"), V("ones", 0, C), V("NB", 0, C), -160.0, Op.mult, Op.add)
+        ts(V("rk"), V("Fc", 15, C, 16), 512.0, Op.add)
+        once(before_order)
+        ts(V("nb", 0, 1), V("NS", C - 1, C), 160.0, Op.add)
+        cp(ind(V("O", 0, C), V("rk")), V("IO"))
+        once(after_order)
         for k in range(F):
+            if k == 1:
+                cp(V("O", C, 2 * C), V("O", 0, C))
             ts(V("pos", 6 * k, 6 * k + 6), V("nb"), V("kpf", k, k + 1), Op.add)
 
-        cp(V("eb", 0, 16 * EB_DVE), ind(V("O"), V("pos", 0, EB_DVE)))
-        act(V("eb", 16 * EB_DVE, 384), ind(V("O"), V("pos", EB_DVE, 24)), Act.Copy)
+        acopy(V("eb", 0, 384 - 16 * EB_DVE), ind(V("O"), V("pos", 0, 24 - EB_DVE)))
+        cp(V("eb", 384 - 16 * EB_DVE, 384), ind(V("O"), V("pos", 24 - EB_DVE, 24)))
+        once(after_lookup)
         scan(V("Fe"), V("eb"), V("K4"), -4096.0, Op.max, Op.add)
-        ts(V("zo"), V("Fe", 3, 384, 4), 4.0, Op.mult, V("pf", 5, 6), Op.add)
-        for k in range(F - Z_ACT):
-            tt(V("Z", 384 * k, 384 * k + 384), ind(V("Xh"), V("zo", 24 * k, 24 * k + 24)), V("ZI", 1, 768, 2), Op.add)
-        for k in range(F - Z_ACT, F):
-            a = 768 * (k - F + Z_ACT)
-            act(V("ZI", a, a + 768, 2), ind(V("Xh"), V("zo", 24 * k, 24 * k + 24)), Act.Copy)
-            scan(V("ZJ", a, a + 768), V("r2"), V("ZI", a, a + 768), 0.0, Op.mult, Op.add)
-            act(V("Z", 384 * k, 384 * k + 384), V("ZJ", a + 1, a + 768, 2), Act.Copy)
-        quant("zq", "zs", 0, V("Z", 0, 4 * 288))
-        quant("zq", "zs", 288, V("Z", 4 * 288, 4 * 416))
-        for k in range(F):
-            mm(k, "zq", "zs", M * k, "uq", "us", 0, 128)
+        once(after_discs)
+        ts(V("zo"), V("Fe", 3, 384, 4), 2048.0, Op.mult, zcol, Op.add)
+        once(after_offsets)
+        for k, (a, b) in enumerate(Z_ACT):
+            i0, i1 = zspan(a, b, k)
+            acopy(V("ZI", i0, i1, 2), ind(V("Xh"), V("zo", a // 4, b // 4)))
+        for step in Z_DVE:
+            if len(step) == 1:
+                a, b = Z_ACT[step[0]]
+                i0, i1 = zspan(a, b, step[0])
+                scan(V("ZJ", i0, i1), V("r2", 0, i1 - i0), V("ZI", i0, i1), 0.0, Op.mult, Op.add)
+                acopy(V("Z", 4 * a, 4 * b), V("ZJ", i0 + 1, i1, 2))
+            elif len(step) == 2:
+                a, b = step
+                i0, i1 = zspan(a, b)
+                tt(V("Z", 4 * a, 4 * b), ind(V("Xh"), V("zo", a // 4, b // 4)), V("ZI", i0 + 1, i1, 2), Op.add)
+            else:
+                a, b, readings = step
+                quant("zq", "zs", a, V("Z", 4 * a, 4 * b))
+                for k in readings:
+                    mm(k, "zq", "zs", M * k, "uq", "us", 0, 128)
+        once(after_readings)
 
         scan(V("pm", 1, 5), V("z4"), V("PA", 1, 2048, 512), -BIG, Op.add, Op.max)
         ts(V("Bw", 0, 32), ind(V("pm", 0, 4), V("lw")), V("pm", 4, 5), Op.is_lt)
         quant("bwq", "bws", 0, V("Bw"))
         mm(6, "cq", "cs", 128, "bwq", "bws", 0, 128)
+        once(after_bits)
         tt(V("idf", 0, 6), bank(6, 0, 6), V("J", 20, 26), Op.add)
         cp(V("wi"), V("idf", 0, 6))
-        pick("slotc%d" % r, "slots%d" % r, "zq", "zs", F * M, V("wi"))
-        sends = []
+        tt(V("hf"), ind(V("idf"), V("lr", 0, 2)), V("B4", 0, 32), Op.add)
+        if r < R - 1:
+            acopy(V("ewb"), ind(V("eb"), V("wi")))
+        pick_codes("slotc%d" % r, "zq", F * M, V("wi"))
+        pick_scales("slots%d" % r, "zs", F * M, V("wi"))
+        if r == R - 1:
+            acopy(V("ewb"), ind(V("eb"), V("wi")))
         for call in calls:
             def send(call=call, r=r):
                 tr = []
@@ -457,74 +586,43 @@ def rank_program(g, core, T, topo):
                     tr.append(RemoteDMATransfer(dst_ids=[DstId(rid=rid, pnc=pid)], dma_engine_mask=mask, remote_sem=T.sem["hop%d" % r],
                                                 src=piece(T, "slot", r, kind, a, b), dst=piece(T, "hop", r, kind, a, b)))
                 return g.remote_dma_fused(tr, local_sem=T.sem.sent)
-            sends.append(add("g", send, [], [V("slot%s%d" % (p[0], r), p[1], p[2]) for p in call], 500.0, kind="r"))
-        if len(sends) > 1:
-            ops[sends[1]]["order"].add(sends[0])
-        act(V("KO", M * r, M * r + M), ind(V("Kc"), V("wi")), Act.Copy)
+            add("g", send, [], [V("slot%s%d" % (p[0], r), p[1], p[2]) for p in call], kind="r")
 
-        act(V("ewb"), ind(V("eb"), V("wi")), Act.Copy)
-        scan(V("Fw"), V("ewb"), V("K16", 0, M), -4096.0, Op.max, Op.add)
-        tt(V("hf"), ind(V("idf"), V("lr", 0, 2)), V("B4", 0, 32), Op.add)
-        ts(V("ho"), V("hf", 0, 24), 4.0, Op.mult, -4.0 * 1536, Op.add)
-        act(V("H"), ind(V("Z", 0, 4 * F * M), V("ho")), Act.Copy)
+        ts(V("ho"), V("hf", 0, 24), 4.0, Op.mult, -4.0 * 1024, Op.add)
+        acopy(V("H"), ind(V("Z", 0, 4 * F * M), V("ho")))
+        acopy(V("KO", M * r, M * r + M), ind(V("Kc"), V("wi")))
+        scan(V("Fw"), V("ewb"), V("K16"), -4096.0, Op.max, Op.add)
         for t in range(6):
-            ts(V("EQ", tri[t], tri[t + 1]), V("ewb", 0, 16 * t + 16), -1024.0, Op.add, V("Fw", 16 * t + 15, 16 * t + 16), Op.is_equal)
-        tt(V("e5"), ind(V("Fw"), V("lr", 2, 4)), V("B4", 0, 32), Op.add)
-        scan(V("ES"), V("EQ"), V("CK"), 0.0, Op.add, Op.mult)
-        tt(V("tg", 0, 32), ind(V("ES"), V("lr", 4, 6)), V("e5"), Op.max)
-        tt(V("tg", 32, 56), V("tg", 0, 24), V("B4", 32, 56), Op.min)
-        ts(V("so"), V("tg", 32, 56), 4.0, Op.mult, -4.0 * 352, Op.add)
+            ts(V("EQ", tri[t], tri[t + 1] - 4), V("ewb", 0, 16 * t + 16), -1.0, Op.add, V("Fw", 16 * t + 15, 16 * t + 16), Op.is_equal)
+        tt(V("e5"), ind(V("Fw"), V("lr", 2, 4)), V("B4", 32, 64), Op.add)
+        scan(V("ES"), V("EQ"), V("CK"), 0.0, Op.max, Op.add)
+        once(after_twins)
+        tt(V("tg"), ind(V("ES"), V("lr", 4, 6)), V("e5"), Op.max)
+        once(after_spare)
+        ts(V("so"), V("tg", 0, 24), 2048.0, Op.mult, socol, Op.add)
         cp(ind(V("X"), V("so")), V("H"))
 
-        lc, ls = "landc%d" % r, "lands%d" % r
-        ext = ("land%d" % r, landing)
-        wb, db = ((0, 2, 6, 2), (1, 3, 0, 1)) if r < R - 1 else ((0, 1, 2, 3), (4, 5, 6, 0))
-        for b in range(4):
-            mm(wb[b], "wq", "wp", 128 * b, lc, ls, 0, 128, ext=ext, soft=sends)
-            act(V("RS", M * b, M * b + M), bank(wb[b], 0, M), Act.Relu, scale=0.03125)
-            mm(db[b], "eq", "es", 128 * b, lc, ls, 0, 128, ext=ext, soft=sends)
-            tt(V("Y", b, 4 * M, 4), V("RS", M * b, M * b + M), bank(db[b], 0, M), Op.add)
+    def store(a, n, q):
+        outs.append(dma(q, T.oc[:, 4 * a:4 * (a + n)], cast(V("aq", a, a + n), dt.uint8)))
+        for j in range(4):
+            outs.append(dma(q, T.osc[4 * j:4 * j + 4, a:a + n], V("asc", a, a + n, p=(32 * j, 32 * j + 4))))
 
     outs.append(dma("s", T.ok[:], V("KO", p=(0, 1))))
-    for a, n, w, src, k in ((0, C, C, V("X", 0, 4 * C), 7), (C, M, 128, V("Y"), 1)):
-        quant("aq", "asc", a, src)
-        mm(k, "vq", "vs", 0, "aq", "asc", a, w)
-        if a:
-            cp(V("yo", a, a + n), bank(k, 0, n))
-        else:
-            act(V("yo", a, a + n), bank(k, 0, n), Act.Copy)
-        outs.append(dma("a", T.oc[:, 4 * a:4 * (a + n)], cast(V("aq", a, a + n), dt.uint8)))
-        for j in range(4):
-            outs.append(dma("sa"[j % 2], T.osc[4 * j:4 * j + 4, a:a + n], V("asc", a, a + n, p=(32 * j, 32 * j + 4))))
-        outs.append(dma("s", T.y[:, a:a + n], V("yo", a, a + n)))
-
-    n = len(ops)
-    kids = [[] for _ in range(n)]
-    for i, o in enumerate(ops):
-        o["pre"] = [(d, ops[d]["lat"]) for d in o["deps"]] + [(d, 0.0) for d in o["order"]] + [(d, COMM) for d in (o["soft"] or [])]
-        for d, l in o["pre"]:
-            kids[d].append((i, l))
-    tail = [0.0] * n
-    for i in range(n - 1, -1, -1):
-        tail[i] = ops[i]["pc"] + ops[i]["boost"] + max([l + tail[k] for k, l in kids[i]] + [ops[i]["lat"]])
-    left = [len(o["pre"]) for o in ops]
-    ready = [0.0] * n
-    free = {q: 0.0 for q in "vatgs"}
-    pool = [i for i in range(n) if left[i] == 0]
-    plan = []
-    while pool:
-        at = lambda i: max(ready[i], free[ops[i]["q"]])
-        j0 = min(pool, key=at)
-        q, first = ops[j0]["q"], at(j0)
-        i = max((j for j in pool if ops[j]["q"] == q and at(j) <= first + SLACK), key=lambda j: tail[j])
-        pool.remove(i)
-        free[q] = at(i) + ops[i]["pc"]
-        plan.append(i)
-        for k, l in kids[i]:
-            ready[k] = max(ready[k], free[q] + l)
-            left[k] -= 1
-            if left[k] == 0:
-                pool.append(k)
+    layer, join = message(R - 1)
+    for k in range(2):
+        quant("aq", "asc", 160 * k, V("X", 640 * k, 640 * k + 640))
+        mm(4 + k, "vq", "vs", 0, "aq", "asc", 160 * k, 160)
+    store(0, C, "s")
+    for k, (copy, q) in enumerate(((acopy, "a"), (cp, "s"))):
+        copy(V("yo", 160 * k, 160 * k + 160), bank(4 + k, 0, 160))
+        outs.append(dma(q, T.y[:, 160 * k:160 * k + 160], V("yo", 160 * k, 160 * k + 160)))
+    layer()
+    join()
+    quant("aq", "asc", C, V("Y"))
+    mm(2, "vq", "vs", 0, "aq", "asc", C, 128)
+    store(C, M, "a")
+    cp(V("yo", C, C + M), bank(2, 0, M))
+    outs.append(dma("s", T.y[:, C:C + M], V("yo", C, C + M)))
 
     queue = {"v": g.vector, "a": g.scalar, "t": g.tensor, "g": g, "s": g.sync}
     needed = set(d for o in ops for d in o["deps"])
@@ -535,10 +633,8 @@ def rank_program(g, core, T, topo):
             queue[q].wait_ge(T.sem[sem], val)
             seen[q][sem] = val
 
-    place = {i: k for k, i in enumerate(plan)}
-    for i in plan:
-        o = ops[i]
-        for d in sorted(o["deps"], key=lambda d: -place[d]):
+    for i, o in enumerate(ops):
+        for d in sorted(o["deps"], reverse=True):
             wait(o["q"], *mark[d])
             for s, v in knew[d].items():
                 seen[o["q"]][s] = max(seen[o["q"]].get(s, 0), v)

@@ -10,11 +10,13 @@ TILES = [(0, 320, (0, 17, 18, 19)), (320, 256, (13, 14, 15, 16)), (576, 192, (9,
          (768, 128, (5, 6, 7, 8)), (896, 64, (1, 2, 3, 4))]
 DVE_ROWS = 12
 SCW = 385
-LAYER = [0, 3, 2]
-JOIN = [(1, 0), (14, 13, 11, 10), (14, 12, 8, 7)]
-EB_DVE = 10
-Z_ACT = [(224, 320), (320, 384)]
-Z_DVE = [(96, 224), (0,), (1,), (0, 96), (128, 416, [2, 3]), (0, 128, [0, 1])]
+LAYER = [0, 4, 2]
+ORDER = [[11, 10, "masked", "diagonal", "least", 9, 8, 7, 6, 5, 4, 3, 2, 1, "its sums", "narrow", "wide", 0, -1, -2, -3],
+         [11, 10, "diagonal", 9, 8, 7, 6, 5, 4, 3, 2, 1, "its sums", "narrow", "join", 0, "scores", "wide", -1, "masked", -2, "least", -3],
+         [11, 10, "diagonal", 9, 8, 7, 6, 5, 4, "join", 3, 2, 1, "scores", "its sums", "narrow", "masked", 0, "least", "wide", -1, -2, -3]]
+SHARE = [192, 192, 160]
+Z_ACT = [(224, 304), (304, 368)]
+Z_DVE = [(96, 224), (0,), (368, 384), (1,), (0, 96), (128, 416, [2, 3]), (0, 128, [0, 1])]
 PIECES = [("c", 0, 48, 0), ("c", 48, 96, 2), ("s", 0, 96, 1)]
 
 
@@ -24,24 +26,25 @@ def sb(n, t):
 
 SCRATCH = {
     "PA": ("psum", [128, 2048], F32), "PB": ("psum", [128, 2048], F32),
-    "X": sb(4 * (C + M), BF), "Xh": sb(4 * C, BF), "Y": sb(512, BF), "ub": sb(512, BF), "vb": sb(512, BF),
+    "X": sb(4 * (C + M), BF), "Xh": sb(4 * C, BF), "Y": sb(512, BF), "Yh": sb(512, BF), "ub": sb(512, BF), "vb": sb(512, BF),
     "uq": sb(128, Q4), "us": sb(128, U8), "ugq": sb(128, Q4), "ugs": sb(128, U8), "vq": sb(128, Q4), "vs": sb(128, U8),
     "wq": sb(512, Q4), "wp": sb(512, U8), "aq": sb(448, Q4), "asc": sb(448, U8),
     "I": sb(128, BF), "E": sb(2048, BF), "eq": sb(512, Q4), "es": sb(512, U8), "CC": sb(1024, BF), "cq": sb(256, Q4), "cs": sb(256, U8),
     "BT": sb(4 * 960, BF), "bq": sb(1024, Q4), "bs": sb(1024, U8),
     "Z": sb(4 * 416, BF), "zq": sb(416, Q4), "zs": sb(416, U8), "Bw": sb(512, BF), "bwq": sb(128, Q4), "bws": sb(128, U8),
-    "ones": sb(512, BF), "pc": sb(24, I32), "pf": sb(16, F32), "c16": sb(C + 16, BF), "c4": sb(96, BF),
-    "M16": sb(C, BF), "K16": sb(M, BF), "r16": sb(C, BF), "rB": sb(384, BF), "K4": sb(384, BF),
+    "ones": sb(512, BF), "pc": sb(24, I32), "pf": sb(20, F32), "c16": sb(C + 16, BF), "c4": sb(96, BF),
+    "M16": sb(C, BF), "K16": sb(384, BF), "r16": sb(C, BF), "rB": sb(384, BF), "K4": sb(384, BF),
     "KB": sb(512, F32), "r2": sb(768, BF), "ZI": sb(1536, BF), "ZJ": sb(1536, BF),
     "IO": sb(C, BF), "Kc": sb(384, F32), "CK": sb(360, BF), "B4": sb(64, F32), "B6": sb(24, F32), "t16": sb(26, F32), "J": sb(32, F32),
-    "lui": sb(8, I32), "lu": sb(8, U16), "lwf": sb(8, F32), "lw": sb(2, U16), "lri": sb(8, F32), "lr": sb(6, U16),
+    "lui": sb(8, I32), "lu": sb(8, U16), "lwf": sb(8, F32), "lw": sb(6, U16), "ld": sb(2, U16), "lri": sb(8, F32), "lr": sb(8, U16),
+    "E16": sb(384, F16), "DE": sb(24, F32), "DT": sb(32, F32), "E0": sb(24, F32), "PW": sb(24, F32), "T2": sb(6, F32),
     "kp1": sb(16, I32), "kpb": sb(16, I32), "kpf": sb(4, F32), "z4": sb(4, F32), "ls": sb(2, U16),
-    "Pm": sb(C, F32), "Fv": sb(C, F32), "Sm": sb(M, F32), "Fs": sb(M, F32), "T0": sb(C, BF), "T1": sb(C, BF), "T2": sb(C, BF),
+    "Pm": sb(C, F32), "Fv": sb(C, F32), "Sm": sb(M, F32), "Fs": sb(M, F32), "T": sb(12 * C, BF),
     "SC": sb(4 * SCW, BF), "DS": sb(2 * C, F16), "RA": sb(20, F32), "Fc": sb(C, F32),
-    "rk": sb(20, U16), "O": sb(2 * C, BF), "NB": sb(6 * C, BF), "NS": sb(C, BF), "nb": sb(6, F32),
+    "rk": sb(20, U16), "O": sb(2 * C, BF), "NB": sb(6 * C, BF), "NS": sb(2 * C, BF), "nb": sb(8, F32),
     "pos": sb(24, U16), "Fe": sb(384, F16), "eb": sb(384, BF), "zo": sb(96, U16),
     "pm": sb(8, F32), "idf": sb(8, F32), "wi": sb(6, U16), "hf": sb(32, F32), "ho": sb(24, U16), "so": sb(24, U16), "H": sb(384, BF),
-    "ewb": sb(M, BF), "Fw": sb(M, F32), "e5": sb(32, F32), "tg": sb(32, F32), "EQ": sb(360, BF), "ES": sb(360, BF),
+    "ewb": sb(M, BF), "Fw": sb(24, F32), "e5": sb(32, F32), "tg": sb(32, F32), "EQ": sb(360, BF), "ES": sb(360, BF),
     "RS": sb(384, F32), "KO": sb(R * M, F32), "yo": sb(C + M, F32),
 }
 for _r in range(R):
@@ -117,8 +120,8 @@ def rank_program(g, core, T, topo):
         rows = slice(None) if p is None else slice(p[0], p[1])
         return {"ap": T[name][rows, a:b:s] if s > 1 else T[name][rows, a:b], "at": [(name, range(a, b, s))], "n": len(range(a, b, s)), "ind": False}
 
-    def bank(k, a=0, b=512):
-        return V("PA" if k < 4 else "PB", 512 * (k % 4) + a, 512 * (k % 4) + b)
+    def bank(k, a=0, b=512, s=1):
+        return V("PA" if k < 4 else "PB", 512 * (k % 4) + a, 512 * (k % 4) + b, s)
 
     def ind(win, off, word=None):
         w = win["ap"].bitcast(word) if word else win["ap"]
@@ -251,7 +254,7 @@ def rank_program(g, core, T, topo):
     lx = dma("s", V("X", 0, 4 * C), T.x[:])
     dma("s", V("Y", 0, 4 * M), T.m[:])
 
-    bcol, b1col, _, bmcol, i4col, qcol, icol, gcol, zcol, mcol, s0, s1, ecol, socol, lcol = (V("pf", k, k + 1) for k in range(15))
+    bcol, b1col, _, bmcol, i4col, qcol, icol, gcol, zcol, mcol, s0, s1, ecol, socol, lcol, b6col, w0, w1, wcol, l2col = (V("pf", k, k + 1) for k in range(20))
     tri = [8 * t * t + 12 * t for t in range(7)]
     iota(V("pc", 0, 16), [[1, 16]], 0, 1)
     iota(V("c16", 0, C), [[0, 20], [1, 16]])
@@ -264,6 +267,7 @@ def rank_program(g, core, T, topo):
     iota(V("IO"), [[1, C]], -160)
     iota(V("CC", 0, 512), [[1, 8], [0, 64]])
     iota(V("lwf", 0, 2), [[4, 2]])
+    iota(V("lwf", 2, 8), [[1, 6]])
     iota(V("SC", 0, 4 * SCW, SCW), [[0, 4]])
 
     fill(V("ones"), 1.0)
@@ -274,6 +278,8 @@ def rank_program(g, core, T, topo):
     pad(0)
     cp(V("pf", 0, 8), V("pc", 16, 24))
     pad(1)
+    pad(2)
+    fill(V("Y", 4 * M, 512), 0.0)
     act(V("Bw"), V("ones"), Act.Copy, scale=0.0)
     act(mcol, icol, Act.Copy, scale=-BIG)
     act(V("r16"), V("c16", 0, C), Act.Relu, scale=-BIG, bias=BIG)
@@ -281,18 +287,17 @@ def rank_program(g, core, T, topo):
     k16 = keeper("KB", 16, V("c16", 0, 16), V("c16", C, C + 16), icol, 16, 512.0)
     k4 = keeper("K4", 48, V("c4", 0, 48), V("c4", 48, 96), i4col, 4, 1.0)
     k16[0]()
-    cp(V("lu"), V("lui"))
+    ts(V("DS", C, 2 * C), V("c16", 0, C), 0.0, Op.is_gt, -2048.0, Op.mult)
     k16[1]()
-    fill(V("Y", 4 * M, 512), 0.0)
+    cp(V("lu"), V("lui"))
+    pad(3)
     k16[2]()
     quant("bq", "bs", 896, V("Bw"))
     quant("uq", "us", 0, V("ub"))
     k4[0]()
     pick_codes("ugq", "uq", 128, V("lu"))
     k4[1]()
-    pad(2)
-    k4[2]()
-    ts(V("DS", C, 2 * C), V("c16", 0, C), 0.0, Op.is_gt, -2048.0, Op.mult)
+    pad(4)
     dma("s", V("rB"), V("ones", 0, 384), after=[lx])
     dma("s", cast(V("wq"), dt.uint8), T.wc[:])
     dma("s", V("wp"), T.ws[:])
@@ -304,6 +309,8 @@ def rank_program(g, core, T, topo):
         dma("s", cast(V("landc%d" % r, M, 128), dt.uint8), cast(V("bq", 960, 992), dt.uint8))
         dma("s", V("lands%d" % r, M, 128), V("bs", 960, 992))
     acopy(V("KB", 16, 32), V("KB", 0, 16))
+    act(zcol, bcol, Act.Identity, bias=4.0 * (160 + 512))
+    act(b6col, bcol, Act.Copy, scale=6.0)
     act(s0, qcol, Act.Square, bias=0.5)
     acopy(V("KB", 32, 64), V("KB", 0, 32))
     act(s1, s0, Act.Identity, scale=-32.0, bias=392.0)
@@ -312,29 +319,23 @@ def rank_program(g, core, T, topo):
     acopy(V("KB", 128, 256), V("KB", 0, 128))
     act(V("J", 0, 26), V("t16", 0, 26), Act.Identity, bias=icol)
     acopy(V("KB", 256, C), V("KB", 0, 64))
-    act(V("K16"), V("KB", 0, M), Act.Copy, scale=1 / 512)
+    act(V("K16", C, 384), V("KB", 0, 64), Act.Copy, scale=1 / 512)
+    act(V("K16", 0, C), V("KB", 0, C), Act.Copy, scale=1 / 512)
 
     def after_x():
-        pad(3)
-        pad(4)
         ts(V("CC", 512, 576), V("CC", 512, 576), icol, Op.is_equal, float(M), Op.mult)
+        k4[2]()
+        ts(V("DS", C, 2 * C, 16), V("J", 0, 20), V("KB", 15, 16), Op.add)
+        fill(V("ls", 1, 2), 3 * SCW)
+        ts(V("CC", 515, 576, 4), V("CC", 515, 576, 4), 1.0, Op.min)
         spread("K4", 48, 384)
         for a, n, rows in TILES[2:]:
             iota(V("rB", a - 576, a - 575), [[0, 1]])
         iota(V("r2"), [[0, 384], [1, 2]])
         add("g", lambda: g.partition_broadcast(T.kpb[:], T.kp1[0:1, :], 128), [V("kpb")], [V("kp1")])
-        for t in range(6):
-            iota(V("CK", tri[t], tri[t + 1]), [[1, 16 * t + 20]], 1 - 16 * t)
         iota(V("pm", 0, 1), [[0, 1]], 1)
         iota(V("B4", 0, 32), [[0, 8], [1, 4]], 4 * 1024)
         spread("CC", 64, 512, 512)
-
-    def after_halves():
-        act(V("IO"), V("IO"), Act.Copy, scale=1 / 512)
-
-    def after_mask():
-        ts(V("DS", C, 2 * C, 16), V("J", 0, 20), V("KB", 15, 16), Op.add)
-        fill(V("ls", 1, 2), 3 * SCW)
 
     def after_own():
         ts(V("CC", 0, 512), V("CC", 0, 512), gcol, Op.is_equal)
@@ -346,62 +347,66 @@ def rank_program(g, core, T, topo):
         ts(V("ls", 0, 1), bmcol, float(SCW), Op.mult, s1, Op.add)
 
     def after_counts():
-        iota(V("B4", 32, 64), [[0, 8], [1, 4]], 4 * 304)
-        iota(V("B6"), [[0, 24]], 1)
+        iota(V("T2"), [[2, 6]])
+        iota(V("DE", 0, 6), [[0, 6]])
+        iota(V("E0"), [[0, 24]], -4096)
+        for t in range(6):
+            iota(V("CK", tri[t], tri[t + 1]), [[1, 16 * t + 20]], 1 - 16 * t)
         iota(V("z4"), [[0, 4]])
+        add("g", lambda: g.affine_select(T.I[:], T.ones[:, 0:128], [[1, 128]], Op.is_equal, 0.0, 0, -1), [V("I")], [V("ones", 0, 128)])
+        iota(V("B6"), [[0, 24]], 1)
+        iota(V("B4", 32, 64), [[-4096, 8], [1, 4]], 4 * 304)
         iota(V("B6", 0, 24, 4), [[64, 6]], -4096 - 192)
         iota(V("idf"), [[0, 8]])
-        add("g", lambda: g.affine_select(T.I[:], T.ones[:, 0:128], [[1, 128]], Op.is_equal, 0.0, 0, -1), [V("I")], [V("ones", 0, 128)])
 
     def before_base():
-        ts(V("lwf", 2, 4), V("lwf", 0, 2), i4col, Op.add, gcol, Op.is_equal)
+        ts(w0, i4col, 0.0, Op.is_equal, b1col, Op.mult)
+        ts(w1, bcol, 3.0, Op.is_equal, i4col, Op.mult)
 
     def before_places():
         cp(V("kpf"), V("kpb", 0, 4))
+        ts(wcol, w0, w1, Op.add)
 
     def before_ranks():
         ts(V("lri", 0, 2), V("lwf", 0, 2), i4col, Op.add, 5.0, Op.min)
 
     def before_order():
-        ts(V("lw"), V("lwf", 2, 4), b1col, Op.mult)
+        ts(V("lw"), V("lwf", 2, 8), gcol, Op.is_equal, wcol, Op.mult)
+        ts(V("ld"), V("lri", 0, 2), b6col, Op.add)
 
     def after_order():
         cp(V("lr", 0, 2), V("lri", 0, 2))
-        act(zcol, bcol, Act.Identity, bias=4.0 * (160 + 512))
-        act(V("pm", 0, 1), V("pm", 0, 1), Act.Copy, scale=BIG)
-        act(V("lri", 2, 4), V("lri", 0, 2), Act.Square, bias=1.75)
-        act(lcol, bcol, Act.Identity, bias=-8.5)
-        act(ecol, icol, Act.Copy, scale=-1 / 512)
-        act(V("B4", 0, 32), V("B4", 0, 32), Act.Copy, scale=0.25)
-        act(socol, icol, Act.Identity, scale=4.0, bias=4.0 * 368)
-
-    def after_lookup():
-        ts(V("CK"), V("CK"), icol, Op.is_equal)
 
     def after_discs():
-        ts(V("lr", 2, 4), V("lri", 0, 2), 16.0, Op.mult, 15.0, Op.add)
-
-    def after_offsets():
-        ts(V("lr", 4, 6), V("lri", 2, 4), 8.0, Op.mult, lcol, Op.add)
+        ts(V("lr", 2, 4), V("lri", 0, 2), 4.0, Op.mult, 3.0, Op.add)
 
     def after_readings():
         quant("cq", "cs", 128, V("CC", 512, 1024))
+        ts(V("CK"), V("CK"), icol, Op.is_equal)
+        act(V("pm", 0, 1), V("pm", 0, 1), Act.Copy, scale=BIG)
+        act(V("lri", 2, 4), V("lri", 0, 2), Act.Square, bias=1.75)
+        act(lcol, bcol, Act.Identity, bias=-8.5)
+        act(l2col, bcol, Act.Identity, bias=-8.5 - tri[4])
+        for b in range(4):
+            acopy(V("E", 512 * b + b, 512 * b + 512, 4), V("I"))
+        act(ecol, icol, Act.Copy, scale=-1 / 512)
+        act(V("B4", 0, 32), V("B4", 0, 32), Act.Copy, scale=0.25)
+        act(socol, icol, Act.Identity, scale=4.0, bias=4.0 * 368)
         act(V("B4", 32, 64), V("B4", 32, 64), Act.Identity, scale=1 / 2048, bias=ecol)
         iota(V("Kc"), [[1, 4], [0, M]])
         for t in range(6):
             act(V("CK", tri[t + 1] - 4, tri[t + 1]), V("B6", 4 * t, 4 * t + 4), Act.Copy, scale=1 / 2048)
             iota(V("EQ", tri[t + 1] - 4, tri[t + 1]), [[0, 4]], -4)
-        for b in range(4):
-            acopy(V("E", 512 * b + b, 512 * b + 512, 4), V("I"))
 
     def after_bits():
         quant("eq", "es", 0, V("E", 0, 1024))
+        ts(V("lr", 4, 5), V("lri", 2, 3), 8.0, Op.mult, lcol, Op.add)
 
-    def after_twins():
+    def after_list():
+        ts(V("lr", 6, 7), V("lri", 3, 4), 8.0, Op.mult, l2col, Op.add)
+
+    def after_rewriting():
         quant("eq", "es", 256, V("E", 1024, 1536))
-
-    def after_spare():
-        quant("eq", "es", 384, V("E", 1536, 2048))
 
     slot = {t: (a, b) for a, n, rows in TILES for b, t in enumerate(rows)}
 
@@ -417,22 +422,25 @@ def rank_program(g, core, T, topo):
             for b in range(4):
                 mm(wb[b], "wq", "wp", 128 * b, lc, ls, 0, 128, ext=ext)
                 act(V("RS", M * b, M * b + M), bank(wb[b], 0, M), Act.Relu, scale=0.03125)
-                for k in [b] if r == R - 1 else range(4) if b == 3 else []:
-                    mm(db[k], "eq", "es", 128 * k, lc, ls, 0, 128, ext=ext)
+            for b in range(4):
+                mm(db[b], "eq", "es", 128 * b, lc, ls, 0, 128, ext=ext)
 
         def join():
             for b in range(4):
                 tt(V("Y", b, 4 * M, 4), V("RS", M * b, M * b + M), bank(db[b], 0, M), Op.add)
         return layer, join
 
+    def half(h):
+        act(V("Xh", C * h, C * h + C), V("X", C * h, C * h + C), Act.Copy, scale=0.5)
+
     def vrow(t):
         ts(rowview(t, 16 * t), bank(4, 0, 16 * t), V("Fv", 16 * t + 15, 16 * t + 16), Op.is_lt)
 
     waiting = []
 
-    def counted(n, col, out, acc, scale):
-        signs = V("T%d" % (len(waiting) % 3), 0, n)
-        act(signs, bank(5, 0, n), Act.Sign, bias=col, scale=-1.0)
+    def counted(n, col, out, acc, scale, a=0):
+        signs = V("T", C * (len(waiting) % 12), C * (len(waiting) % 12) + n)
+        act(signs, bank(5, a, a + n), Act.Sign, bias=col, scale=-1.0)
         finish()
         waiting.append(lambda: act(out, signs, Act.Relu, scale=scale, acc=acc))
 
@@ -441,19 +449,32 @@ def rank_program(g, core, T, topo):
             waiting[-1]()
             waiting[-1] = None
 
-    def nrows(rows):
-        for t in rows:
-            counted(C, V("Fs", 16 * t + 15, 16 * t + 16), V("NB", C * t, C * t + C), V("nb", t, t + 1), -1.0)
-
-    def across(a, b, last=False):
-        quant("bq", "bs", a, V("BT", 4 * a, 4 * b))
-        for a1, n, _ in TILES:
-            if a <= a1 < b:
-                mm(7, "cq", "cs", 0, "bq", "bs", a1, max(n, 128), a1 == 0, last and a1 + n == b)
-
     def scores():
         quant("aq", "asc", C, V("Y"))
         mm(6, "ugq", "ugs", 0, "aq", "asc", C, 128)
+
+    def diagonal():
+        tt(rowview(0, C), V("Fv"), bank(4, 0, C), Op.is_ge)
+
+    def narrow():
+        quant("bq", "bs", 576, V("BT", 4 * 576, 4 * 960))
+
+    def wide():
+        quant("bq", "bs", 0, V("BT", 0, 4 * C))
+        for a, n, _ in TILES[:1] + TILES[2:]:
+            mm(7, "cq", "cs", 0, "bq", "bs", a, max(n, 128), a == 0, False)
+
+    def sums(b):
+        scan(V("SC", SCW * b + 1, SCW * b + SCW), V("rB"), V("BT", 4 * 576 + b, 4 * 960, 4), 0.0, Op.mult, Op.subtract)
+
+    def look(a, b):
+        ts(V("eb", 16 * a, 16 * b), ind(V("O"), V("pos", a, b)), 1 / 512, Op.mult)
+
+    def discs(a, b):
+        scan(V("Fe", 16 * a, 16 * b), V("eb", 16 * a, 16 * b), V("K4", 0, 16 * (b - a)), -4096.0, Op.max, Op.add)
+
+    def offsets(a, b):
+        ts(V("zo", 4 * a, 4 * b), V("Fe", 16 * a + 3, 16 * b, 4), 2048.0, Op.mult, zcol, Op.add)
 
     def zspan(a, b, k=0):
         return 768 * k + 8 * (a % M), 768 * k + 8 * (a % M + b - a)
@@ -462,31 +483,30 @@ def rank_program(g, core, T, topo):
     for r in range(R):
         layer, join = message(r - 1) if r else (lambda: None, None)
         once = (lambda f: None) if r else (lambda f: f())
+        later = (lambda f: f()) if r else (lambda f: None)
         quant("aq", "asc", 160, V("X", 640, 4 * C))
         mm(7, "ugq", "ugs", 0, "aq", "asc", 160, 160)
         quant("aq", "asc", 0, V("X", 0, 640))
-        mm(4, "ugq", "ugs", 0, "aq", "asc", 0, C)
+        mm(3, "ugq", "ugs", 0, "aq", "asc", 0, 160)
         mm(5, "ugq", "ugs", 0, "aq", "asc", 0, C)
-        once(scores)
+        mm(4, "ugq", "ugs", 0, "aq", "asc", 0, C)
         once(after_x)
         if r == 1:
+            quant("eq", "es", 384, V("E", 1536, 2048))
+        if r == 2:
             quant("vq", "vs", 0, V("vb"))
-        for h in range(4):
-            act(V("Xh", C * h, C * h + C), V("X", C * h, C * h + C), Act.Copy, scale=0.5)
-        once(after_halves)
+        for h in range(4 if r else 2):
+            half(h)
         tt(V("Pm", 160, C), bank(7, 0, 160), V("M16", 160, C), Op.add)
-        once(after_mask)
-        scan(V("Fv", 160, C), V("r16", 160, C), V("Pm", 160, C), 0.0, Op.add, Op.min)
-        tt(V("Pm", 0, 160), bank(4, 0, 160), V("M16", 0, 160), Op.add)
+        tt(V("Pm", 0, 160), bank(3, 0, 160), V("M16", 0, 160), Op.add)
+        scan(V("Fv", 192, C), V("r16", 192, C), V("Pm", 192, C), 0.0, Op.add, Op.min)
+        scan(V("Fv", 0, 192), V("r16", 0, 192), V("Pm", 0, 192), 0.0, Op.add, Op.min)
+        once(scores)
         vrow(12)
-        scan(V("Fv", 0, 160), V("r16", 0, 160), V("Pm", 0, 160), 0.0, Op.add, Op.min)
         for k, t in enumerate(range(19, DVE_ROWS, -1)):
             if k == LAYER[r]:
                 layer()
             counted(16 * t, V("Fv", 16 * t + 15, 16 * t + 16), rowview(t, 16 * t), V("RA", t, t + 1), 1.0)
-
-        def diagonal():
-            tt(rowview(0, C), V("Fv"), bank(4, 0, C), Op.is_ge)
 
         def diagonal_sums():
             once(before_diagonal)
@@ -500,82 +520,102 @@ def rank_program(g, core, T, topo):
             scan(V("Fs"), V("r16", 0, M), V("Sm"), 0.0, Op.add, Op.min)
             once(after_message)
 
-        steps = [lambda t=t: vrow(t) for t in (11, 10)] + [diagonal] + [lambda t=t: vrow(t) for t in range(9, 0, -1)]
-        steps += [diagonal_sums, lambda: across(0, 320), lambda: across(576, 960)]
-        for k, f in zip(JOIN[r], (least, masked, scores, join)):
-            steps.insert(k, f)
-        for f in steps:
-            f()
-        nrows([5])
-        for b in range(4):
-            scan(V("SC", SCW * b + 1, SCW * b + SCW), V("rB"), V("BT", 4 * 576 + b, 4 * 960, 4), 0.0, Op.mult, Op.subtract)
-        across(320, 576, True)
+        steps = {"diagonal": diagonal, "its sums": diagonal_sums, "narrow": narrow, "wide": wide,
+                 "join": join, "scores": scores, "masked": masked, "least": least}
+        for step in ORDER[r]:
+            if step in steps:
+                steps[step]()
+            elif step > 0:
+                vrow(step)
+            else:
+                sums(-step)
+        gcopy(V("ZI", 1, 768, 2), V("Y", 0, 4 * M))
+        gcopy(V("ZI", 769, 1536, 2), V("Y", 0, 4 * M))
+        finish()
+        H = SHARE[r]
+        counted(C - H, V("Fs", 95, 96), V("NB", 5 * C + H, 6 * C), V("nb", 6, 7), -1.0, H)
+        ts(V("NB", 5 * C, 5 * C + H), bank(4, 0, H), V("Fs", 95, 96), Op.is_gt)
+        quant("bq", "bs", C, V("BT", 4 * C, 4 * 576))
+        mm(7, "cq", "cs", 0, "bq", "bs", C, 256, False, True)
         ends = V("DS", 16 * DVE_ROWS + 31, C, 16)
         tt(ends, ends, V("RA", DVE_ROWS + 1, 20), Op.subtract)
-        nrows([4, 3, 2, 1])
+        scan(V("NS", C, C + H), V("ones", 0, H), V("NB", 5 * C, 5 * C + H), 0.0, Op.mult, Op.add)
+        for t in range(4, 0 if r else -1, -1):
+            counted(C, V("Fs", 16 * t + 15, 16 * t + 16), V("NB", C * t, C * t + C), V("nb", t, t + 1), -1.0)
         finish()
-        act(V("ZI", 1, 768, 2), V("Y", 0, 4 * M), Act.Copy, scale=0.5)
-        gcopy(V("ZI", 769, 1536, 2), V("ZI", 1, 768, 2))
+        act(V("Yh", 0, 4 * M), V("Y", 0, 4 * M), Act.Copy, scale=0.5)
+        act(V("Yh", 4 * M, 512), V("Y", 0, 128), Act.Copy, scale=0.5)
+        once(lambda: half(2))
         once(after_counts)
         once(before_base)
-        ts(V("NB", 0, 160), bank(4, 0, 160), V("Fs", 15, 16), Op.is_gt)
+        later(lambda: ts(V("NB", 0, 160), bank(4, 0, 160), V("Fs", 15, 16), Op.is_gt))
         tt(V("KB", 15, 512, 16), ind(V("SC"), V("ls")), V("DS", 15, 512, 16), Op.add)
         once(before_places)
-        ts(V("NB", 160, C), bank(4, 160, C), V("Fs", 15, 16), Op.is_gt)
+        later(lambda: ts(V("NB", 160, C), bank(4, 160, C), V("Fs", 15, 16), Op.is_gt))
         scan(V("Fc"), bank(7, 0, C), V("KB", 0, C), -4096.0, Op.max, Op.add)
         once(before_ranks)
-        scan(V("NS"), V("ones", 0, C), V("NB", 0, C), -160.0, Op.mult, Op.add)
+        later(lambda: scan(V("NS", 0, C), V("ones", 0, C), V("NB", 0, C), -160.0, Op.mult, Op.add))
         ts(V("rk"), V("Fc", 15, C, 16), 512.0, Op.add)
         once(before_order)
-        ts(V("nb", 0, 1), V("NS", C - 1, C), 160.0, Op.add)
+        later(lambda: ts(V("nb", 0, 1), V("NS", C - 1, C), 160.0, Op.add))
+        ts(V("nb", 5, 6), V("NS", C + H - 1, C + H), V("nb", 6, 7), Op.add)
         cp(ind(V("O", 0, C), V("rk")), V("IO"))
         once(after_order)
-        for k in range(F):
-            if k == 1:
+        for k in (2, 3, 1, 0):
+            if k == (0 if r else 2):
                 cp(V("O", C, 2 * C), V("O", 0, C))
-            ts(V("pos", 6 * k, 6 * k + 6), V("nb"), V("kpf", k, k + 1), Op.add)
+            ts(V("pos", 6 * k, 6 * k + 6), V("nb", 0, 6), V("kpf", k, k + 1), Op.add)
 
-        acopy(V("eb", 0, 384 - 16 * EB_DVE), ind(V("O"), V("pos", 0, 24 - EB_DVE)))
-        cp(V("eb", 384 - 16 * EB_DVE, 384), ind(V("O"), V("pos", 24 - EB_DVE, 24)))
-        once(after_lookup)
-        scan(V("Fe"), V("eb"), V("K4"), -4096.0, Op.max, Op.add)
-        once(after_discs)
-        ts(V("zo"), V("Fe", 3, 384, 4), 2048.0, Op.mult, zcol, Op.add)
-        once(after_offsets)
+        look(6, 14)
+        act(V("eb", 16 * 14, 384), ind(V("O"), V("pos", 14, 24)), Act.Copy, scale=1 / 512)
+        once(lambda: half(3))
+        look(0, 6)
+        discs(6, 14)
+        discs(14, 24)
+        offsets(6, 14)
+        discs(0, 6)
+        offsets(14, 24)
         for k, (a, b) in enumerate(Z_ACT):
             i0, i1 = zspan(a, b, k)
-            acopy(V("ZI", i0, i1, 2), ind(V("Xh"), V("zo", a // 4, b // 4)))
+            acopy(V("ZI", i0, i1, 2), ind(V("X", 0, 4 * C), V("zo", a // 4, b // 4)))
         for step in Z_DVE:
             if len(step) == 1:
                 a, b = Z_ACT[step[0]]
                 i0, i1 = zspan(a, b, step[0])
                 scan(V("ZJ", i0, i1), V("r2", 0, i1 - i0), V("ZI", i0, i1), 0.0, Op.mult, Op.add)
-                acopy(V("Z", 4 * a, 4 * b), V("ZJ", i0 + 1, i1, 2))
+                act(V("Z", 4 * a, 4 * b), V("ZJ", i0 + 1, i1, 2), Act.Copy, scale=0.5)
             elif len(step) == 2:
                 a, b = step
                 i0, i1 = zspan(a, b)
-                tt(V("Z", 4 * a, 4 * b), ind(V("Xh"), V("zo", a // 4, b // 4)), V("ZI", i0 + 1, i1, 2), Op.add)
+                tt(V("Z", 4 * a, 4 * b), ind(V("Xh"), V("zo", a // 4, b // 4)), V("Yh", i0 // 2, i1 // 2), Op.add)
+                if step == Z_DVE[0]:
+                    offsets(0, 6)
+                    once(after_discs)
             else:
                 a, b, readings = step
                 quant("zq", "zs", a, V("Z", 4 * a, 4 * b))
                 for k in readings:
                     mm(k, "zq", "zs", M * k, "uq", "us", 0, 128)
+        scan(V("E16"), V("eb"), V("K16"), -4096.0, Op.max, Op.add)
         once(after_readings)
+        tt(V("DE", 6, 24), V("E16", M + 15, 384, 16), V("E16", 15, 288, 16), Op.subtract)
+        tt(V("E0", 0, 24, 4), V("E16", 15, M, 16), V("T2"), Op.add)
 
         scan(V("pm", 1, 5), V("z4"), V("PA", 1, 2048, 512), -BIG, Op.add, Op.max)
-        ts(V("Bw", 0, 32), ind(V("pm", 0, 4), V("lw")), V("pm", 4, 5), Op.is_lt)
+        ts(V("Bw", 0, 96), ind(V("pm", 0, 4), V("lw")), V("pm", 4, 5), Op.is_lt)
         quant("bwq", "bws", 0, V("Bw"))
         mm(6, "cq", "cs", 128, "bwq", "bws", 0, 128)
+        cp(V("DT"), ind(V("DE"), V("ld")))
         once(after_bits)
-        tt(V("idf", 0, 6), bank(6, 0, 6), V("J", 20, 26), Op.add)
+        tt(V("idf", 0, 6), bank(6, 0, 24, 4), V("J", 20, 26), Op.add)
+        tt(V("PW"), bank(6, 0, 24), V("DT", 0, 24), Op.mult)
         cp(V("wi"), V("idf", 0, 6))
+        scan(V("Fw"), V("E0"), V("PW"), -4096.0, Op.max, Op.add)
+        once(after_list)
         tt(V("hf"), ind(V("idf"), V("lr", 0, 2)), V("B4", 0, 32), Op.add)
-        if r < R - 1:
-            acopy(V("ewb"), ind(V("eb"), V("wi")))
+        acopy(V("ewb"), ind(V("eb"), V("wi")))
         pick_codes("slotc%d" % r, "zq", F * M, V("wi"))
         pick_scales("slots%d" % r, "zs", F * M, V("wi"))
-        if r == R - 1:
-            acopy(V("ewb"), ind(V("eb"), V("wi")))
         for call in calls:
             def send(call=call, r=r):
                 tr = []
@@ -591,28 +631,29 @@ def rank_program(g, core, T, topo):
         ts(V("ho"), V("hf", 0, 24), 4.0, Op.mult, -4.0 * 1024, Op.add)
         acopy(V("H"), ind(V("Z", 0, 4 * F * M), V("ho")))
         acopy(V("KO", M * r, M * r + M), ind(V("Kc"), V("wi")))
-        scan(V("Fw"), V("ewb"), V("K16"), -4096.0, Op.max, Op.add)
-        for t in range(6):
-            ts(V("EQ", tri[t], tri[t + 1] - 4), V("ewb", 0, 16 * t + 16), -1.0, Op.add, V("Fw", 16 * t + 15, 16 * t + 16), Op.is_equal)
         tt(V("e5"), ind(V("Fw"), V("lr", 2, 4)), V("B4", 32, 64), Op.add)
-        scan(V("ES"), V("EQ"), V("CK"), 0.0, Op.max, Op.add)
-        once(after_twins)
-        tt(V("tg"), ind(V("ES"), V("lr", 4, 6)), V("e5"), Op.max)
-        once(after_spare)
-        ts(V("so"), V("tg", 0, 24), 2048.0, Op.mult, socol, Op.add)
+        for t in (4, 5, 0, 1, 2, 3):
+            ts(V("EQ", tri[t], tri[t + 1] - 4), V("ewb", 0, 16 * t + 16), 2.0 * t - 1.0, Op.add, V("Fw", 4 * t + 3, 4 * t + 4), Op.is_equal)
+        for a, b in ((tri[4], tri[6]), (0, tri[4])):
+            scan(V("ES", a, b), V("EQ", a, b), V("CK", a, b), 0.0, Op.max, Op.add)
+        tt(V("tg", 16, 32), ind(V("ES", tri[4], tri[6]), V("lr", 6, 7)), V("e5", 16, 32), Op.max)
+        tt(V("tg", 0, 16), ind(V("ES", 0, tri[4]), V("lr", 4, 5)), V("e5", 0, 16), Op.max)
+        for a, b in ((16, 24), (0, 16)):
+            ts(V("so", a, b), V("tg", a, b), 2048.0, Op.mult, socol, Op.add)
         cp(ind(V("X"), V("so")), V("H"))
+        once(after_rewriting)
 
-    def store(a, n, q):
-        outs.append(dma(q, T.oc[:, 4 * a:4 * (a + n)], cast(V("aq", a, a + n), dt.uint8)))
+    def store(a, n):
+        outs.append(dma("s", T.oc[:, 4 * a:4 * (a + n)], cast(V("aq", a, a + n), dt.uint8)))
         for j in range(4):
-            outs.append(dma(q, T.osc[4 * j:4 * j + 4, a:a + n], V("asc", a, a + n, p=(32 * j, 32 * j + 4))))
+            outs.append(dma("s", T.osc[4 * j:4 * j + 4, a:a + n], V("asc", a, a + n, p=(32 * j, 32 * j + 4))))
 
     outs.append(dma("s", T.ok[:], V("KO", p=(0, 1))))
     layer, join = message(R - 1)
     for k in range(2):
         quant("aq", "asc", 160 * k, V("X", 640 * k, 640 * k + 640))
         mm(4 + k, "vq", "vs", 0, "aq", "asc", 160 * k, 160)
-    store(0, C, "s")
+    store(0, C)
     for k, (copy, q) in enumerate(((acopy, "a"), (cp, "s"))):
         copy(V("yo", 160 * k, 160 * k + 160), bank(4 + k, 0, 160))
         outs.append(dma(q, T.y[:, 160 * k:160 * k + 160], V("yo", 160 * k, 160 * k + 160)))
@@ -620,13 +661,25 @@ def rank_program(g, core, T, topo):
     join()
     quant("aq", "asc", C, V("Y"))
     mm(2, "vq", "vs", 0, "aq", "asc", C, 128)
-    store(C, M, "a")
+    store(C, M)
     cp(V("yo", C, C + M), bank(2, 0, M))
-    outs.append(dma("s", T.y[:, C:C + M], V("yo", C, C + M)))
+    outs.append(dma("a", T.y[:, C:C + M], V("yo", C, C + M)))
 
     queue = {"v": g.vector, "a": g.scalar, "t": g.tensor, "g": g, "s": g.sync}
-    needed = set(d for o in ops for d in o["deps"])
-    count, seen, mark, knew, nd = {q: 0 for q in queue}, {q: {} for q in queue}, {}, {}, 0
+    lane = lambda i: ops[i]["q"] if ops[i]["kind"] == "c" else i
+    known, knew, waits = {q: {} for q in queue}, {}, []
+    for i, o in enumerate(ops):
+        seen, mine = known[o["q"]], []
+        for d in sorted(o["deps"], reverse=True):
+            if seen.get(lane(d), -1) < d:
+                mine.append(d)
+                seen[lane(d)] = d
+                for k, x in knew[d].items():
+                    seen[k] = max(seen.get(k, -1), x)
+        knew[i] = dict(seen)
+        waits.append(mine)
+    needed = set(d for w in waits for d in w)
+    count, seen, mark, nd = {q: 0 for q in queue}, {q: {} for q in queue}, {}, 0
 
     def wait(q, sem, val):
         if seen[q].get(sem, 0) < val:
@@ -634,25 +687,19 @@ def rank_program(g, core, T, topo):
             seen[q][sem] = val
 
     for i, o in enumerate(ops):
-        for d in sorted(o["deps"], reverse=True):
+        for d in waits[i]:
             wait(o["q"], *mark[d])
-            for s, v in knew[d].items():
-                seen[o["q"]][s] = max(seen[o["q"]].get(s, 0), v)
         if o["ext"]:
             wait(o["q"], *o["ext"])
-        knew[i] = dict(seen[o["q"]])
         ins = o["fn"]()
         if o["kind"] == "d":
             mark[i] = ("d%d" % nd, 16)
             ins.then_inc(T.sem["d%d" % nd], 16)
             nd += 1
-        elif o["kind"] == "c" and i in needed:
+        elif i in needed:
             count[o["q"]] += 1
             mark[i] = ("q" + o["q"], count[o["q"]])
             ins.then_inc(T.sem["q" + o["q"]], 1)
     for i in outs:
         wait(ops[i]["q"], *mark[i])
-    for q in "vatg":
-        if max(seen[k].get("q" + q, 0) for k in queue) < count[q]:
-            wait("g", "q" + q, count[q])
     g.wait_ge(T.sem.sent, R * sum(bits(p[4]) for call in calls for p in call))

import numpy as np
from concourse.bass import DstId, RemoteDMATransfer
from concourse.mybir import dt, AluOpType as Op, ActivationFunctionType as Act

C, M, F, R = 320, 96, 4, 3
BIG = 2.0 ** 93
BF, F16, F32, I32, U16, Q4, U8 = "bfloat16", "float16", "float32", "int32", "uint16", "float8_e4m3fn_x4", "uint8"

TILES = [(0, 320, (0, 17, 18, 19)), (320, 256, (13, 14, 15, 16)), (576, 192, (9, 10, 11, 12)),
         (768, 128, (5, 6, 7, 8)), (896, 64, (1, 2, 3, 4))]
DVE_ROWS = 12
SCW = 385
LAYER = [0, 4, 2]
ORDER = [[11, 10, "masked", "diagonal", "least", 9, 8, 7, 6, 5, 4, 3, 2, 1, "its sums", "narrow", "wide", 0, -1, -2, -3],
         [11, 10, "diagonal", 9, 8, 7, 6, 5, 4, 3, 2, 1, "its sums", "narrow", "join", 0, "scores", "wide", -1, "masked", -2, "least", -3],
         [11, 10, "diagonal", 9, 8, 7, 6, 5, 4, "join", 3, 2, 1, "scores", "its sums", "narrow", "masked", 0, "least", "wide", -1, -2, -3]]
SHARE = [192, 192, 160]
Z_ACT = [(224, 304), (304, 368)]
Z_DVE = [(96, 224), (0,), (368, 384), (1,), (0, 96), (128, 416, [2, 3]), (0, 128, [0, 1])]
PIECES = [("c", 0, 48, 0), ("c", 48, 96, 2), ("s", 0, 96, 1)]


def sb(n, t):
    return ("sbuf", [128, n], t)


SCRATCH = {
    "PA": ("psum", [128, 2048], F32), "PB": ("psum", [128, 2048], F32),
    "X": sb(4 * (C + M), BF), "Xh": sb(4 * C, BF), "Y": sb(512, BF), "Yh": sb(512, BF), "ub": sb(512, BF), "vb": sb(512, BF),
    "uq": sb(128, Q4), "us": sb(128, U8), "ugq": sb(128, Q4), "ugs": sb(128, U8), "vq": sb(128, Q4), "vs": sb(128, U8),
    "wq": sb(512, Q4), "wp": sb(512, U8), "aq": sb(448, Q4), "asc": sb(448, U8),
    "I": sb(128, BF), "E": sb(2048, BF), "eq": sb(512, Q4), "es": sb(512, U8), "CC": sb(1024, BF), "cq": sb(256, Q4), "cs": sb(256, U8),
    "BT": sb(4 * 960, BF), "bq": sb(1024, Q4), "bs": sb(1024, U8),
    "Z": sb(4 * 416, BF), "zq": sb(416, Q4), "zs": sb(416, U8), "Bw": sb(512, BF), "bwq": sb(128, Q4), "bws": sb(128, U8),
    "ones": sb(512, BF), "pc": sb(24, I32), "pf": sb(20, F32), "c16": sb(C + 16, BF), "c4": sb(96, BF),
    "M16": sb(C, BF), "K16": sb(384, BF), "r16": sb(C, BF), "rB": sb(384, BF), "K4": sb(384, BF),
    "KB": sb(512, F32), "r2": sb(768, BF), "ZI": sb(1536, BF), "ZJ": sb(1536, BF),
    "IO": sb(C, BF), "Kc": sb(384, F32), "CK": sb(360, BF), "B4": sb(64, F32), "B6": sb(24, F32), "t16": sb(26, F32), "J": sb(32, F32),
    "lui": sb(8, I32), "lu": sb(8, U16), "lwf": sb(8, F32), "lw": sb(6, U16), "ld": sb(2, U16), "lri": sb(8, F32), "lr": sb(8, U16),
    "E16": sb(384, F16), "DE": sb(24, F32), "DT": sb(32, F32), "E0": sb(24, F32), "PW": sb(24, F32), "T2": sb(6, F32),
    "kp1": sb(16, I32), "kpb": sb(16, I32), "kpf": sb(4, F32), "z4": sb(4, F32), "ls": sb(2, U16),
    "Pm": sb(C, F32), "Fv": sb(C, F32), "Sm": sb(M, F32), "Fs": sb(M, F32), "T": sb(12 * C, BF),
    "SC": sb(4 * SCW, BF), "DS": sb(2 * C, F16), "RA": sb(20, F32), "Fc": sb(C, F32),
    "rk": sb(20, U16), "O": sb(2 * C, BF), "NB": sb(6 * C, BF), "NS": sb(2 * C, BF), "nb": sb(8, F32),
    "pos": sb(24, U16), "Fe": sb(384, F16), "eb": sb(384, BF), "zo": sb(96, U16),
    "pm": sb(8, F32), "idf": sb(8, F32), "wi": sb(6, U16), "hf": sb(32, F32), "ho": sb(24, U16), "so": sb(24, U16), "H": sb(384, BF),
    "ewb": sb(M, BF), "Fw": sb(24, F32), "e5": sb(32, F32), "tg": sb(32, F32), "EQ": sb(360, BF), "ES": sb(360, BF),
    "RS": sb(384, F32), "KO": sb(R * M, F32), "yo": sb(C + M, F32),
}
for _r in range(R):
    for _n, _w in (("slot", M), ("hop", M), ("land", 128)):
        SCRATCH["%sc%d" % (_n, _r)] = sb(_w, Q4)
        SCRATCH["%ss%d" % (_n, _r)] = sb(_w, U8)

SEMAPHORES = (["qv", "qa", "qt", "qg", "sent"] + ["hop%d" % r for r in range(R)] + ["land%d" % r for r in range(R)]
              + ["d%d" % k for k in range(48)])


def helpers(topo, src, dst):
    h = [c for c in topo.cores_of(src) if c != src and topo.may_write(c, dst)]
    return sorted(h, key=lambda c: (topo.die(c) != topo.die(src), c))


def some(engines, k, n):
    w = len(engines) // n
    return sum(1 << e for e in engines[k * w:(k + 1) * w])


def piece(T, name, r, kind, a, b):
    v = T["%s%s%d" % (name, kind, r)][:, a:b]
    return v.bitcast(dt.uint8) if kind == "c" else v


def first_hop(topo, src, dst):
    h = helpers(topo, src, dst)
    calls = {}
    for kind, a, b, k in PIECES:
        calls.setdefault((b - a) * (4 if kind == "c" else 1), []).append((kind, a, b, h[k % len(h)]))
    return [[p + (some(topo.engines(src, p[3]), i, len(ps)),) for i, p in enumerate(ps)] for ps in calls.values()]


def bits(m):
    return bin(m).count("1")


def helper_program(g, core, T, topo, src, dst):
    mine = [p for call in first_hop(topo, src, dst) for p in call if p[3] == core]
    if not mine:
        return
    rid, pid = topo.addr(dst, core)
    mask = topo.mask(core, dst)
    n = 0
    for r in range(R):
        g.wait_ge(T.sem["hop%d" % r], sum(bits(p[4]) for p in mine))
        for kind, a, b, _, _ in mine:
            g.remote_dma(piece(T, "land", r, kind, a, b), piece(T, "hop", r, kind, a, b), T.sem["land%d" % r], T.sem.sent, pid, rid, mask)
            n += bits(mask)
    g.wait_ge(T.sem.sent, n)


def rank_program(g, core, T, topo):
    cores = list(T.cores)
    rank = T.rank_of(core)
    if rank is None:
        for i, c in enumerate(cores):
            if core in topo.cores_of(c):
                helper_program(g, core, T, topo, c, cores[(i + 1) % len(cores)])
        return
    nxt, prv = cores[(rank + 1) % len(cores)], cores[(rank - 1) % len(cores)]
    calls = first_hop(topo, core, nxt)
    landing = sum(bits(topo.mask(p[3], core)) for call in first_hop(topo, prv, core) for p in call)

    ops = []
    lastw = {n: np.full(s[1][1], -1) for n, s in SCRATCH.items()}
    lastr = {n: [set() for _ in range(s[1][1])] for n, s in SCRATCH.items()}

    def V(name, a=0, b=None, s=1, p=None):
        if b is None:
            b = SCRATCH[name][1][1]
        rows = slice(None) if p is None else slice(p[0], p[1])
        return {"ap": T[name][rows, a:b:s] if s > 1 else T[name][rows, a:b], "at": [(name, range(a, b, s))], "n": len(range(a, b, s)), "ind": False}

    def bank(k, a=0, b=512, s=1):
        return V("PA" if k < 4 else "PB", 512 * (k % 4) + a, 512 * (k % 4) + b, s)

    def ind(win, off, word=None):
        w = win["ap"].bitcast(word) if word else win["ap"]
        return {"ap": w.indirect(off["ap"]), "at": win["at"] + off["at"], "n": 16 * off["n"], "ind": True, "win": win, "off": off}

    def add(q, fn, outs, ins, after=(), ext=None, kind="c"):
        me, deps = len(ops), set(after)
        reads, writes = [], []
        for v in ins:
            if isinstance(v, dict):
                reads += v["at"]
        for v in outs:
            writes += v["win"]["at"] if v["ind"] else v["at"]
            reads += v["off"]["at"] if v["ind"] else []
        psum = lambda n: SCRATCH[n][0] == "psum"
        whole = lambda n, cols: sorted(set(c // 512 * 512 for c in cols)) if psum(n) else cols
        for n, cols in reads:
            for c in whole(n, cols):
                deps.add(int(lastw[n][c]))
                if psum(n):
                    deps.update(o for o in lastr[n][c] if ops[o]["q"] != q)
        for n, cols in writes:
            for c in whole(n, cols):
                if not psum(n):
                    deps.add(int(lastw[n][c]))
                deps.update(lastr[n][c])
        for n, cols in reads:
            for c in whole(n, cols):
                lastr[n][c].add(me)
        for n, cols in writes:
            for c in whole(n, cols):
                lastw[n][c] = me
                lastr[n][c] = set()
        deps -= {-1, me}
        ops.append({"q": q, "fn": fn, "deps": deps, "ext": ext, "kind": kind})
        return me

    def ap(v):
        return v["ap"] if isinstance(v, dict) else v

    def ts(out, in0, s1, op0, s2=None, op1=None):
        if op1 is None:
            fn = lambda: g.vector.tensor_scalar(out["ap"], in0["ap"], ap(s1), None, op0)
        else:
            fn = lambda: g.vector.tensor_scalar(out["ap"], in0["ap"], ap(s1), ap(s2), op0, op1)
        add("v", fn, [out], [in0, s1, s2])

    def tt(out, a, b, op):
        add("v", lambda: g.vector.tensor_tensor(out["ap"], a["ap"], b["ap"], op), [out], [a, b])

    def cp(out, a):
        add("v", lambda: g.vector.tensor_copy(out["ap"], a["ap"]), [out], [a])

    def scan(out, d0, d1, init, op0, op1):
        add("v", lambda: g.vector.tensor_tensor_scan(out["ap"], d0["ap"], d1["ap"], init, op0, op1), [out], [d0, d1])

    def fill(out, c):
        add("v", lambda: g.vector.memset(out["ap"], c), [out], [])

    def quant(q, s, a, src):
        n = src["n"] // 4
        oq, osc = V(q, a, a + n), V(s, a, a + n)
        add("v", lambda: g.vector.quantize_mx(oq["ap"], osc["ap"], src["ap"]), [oq, osc], [src])

    def act(out, a, func, bias=None, scale=None, acc=None):
        kw = {}
        if bias is not None:
            kw["bias"] = ap(bias)
        if scale is not None:
            kw["scale"] = scale
        if acc is not None:
            kw["accum_out"] = acc["ap"]
        add("a", lambda: g.scalar.activation(out["ap"], a["ap"], func, **kw), [out] + ([acc] if acc else []), [a, bias])

    def mm(k, lq, ls, la, rq, rs, ra, n, start=True, stop=True, ext=None):
        o, l, l2, m1, m2 = bank(k, 0, n), V(lq, la, la + 128), V(ls, la, la + 128), V(rq, ra, ra + n), V(rs, ra, ra + n)
        add("t", lambda: g.tensor.matmul_mx(o["ap"], l["ap"], l2["ap"], m1["ap"], m2["ap"], start, stop), [o], [l, l2, m1, m2], ext=ext)

    def iota(out, pattern, base=0, cm=0):
        if SCRATCH[out["at"][0][0]][2] == I32:
            fn = lambda: g.iota(out["ap"], pattern, base, cm)
        else:
            fn = lambda: g.iota(out["ap"], pattern, base, cm, allow_small_or_imprecise_dtypes=True)
        add("g", fn, [out], [])

    def dma(q, out, in_, after=(), slow=False):
        eng = {"s": g.sync, "a": g.scalar, "g": g}[q]
        if slow:
            fn = lambda: eng.dma_start(ap(out), ap(in_), allow_slow_non_contiguous=True)
        else:
            fn = lambda: eng.dma_start(ap(out), ap(in_))
        return add(q, fn, [out] if isinstance(out, dict) else [], [in_], after=after, kind="d")

    def cast(v, t):
        w = dict(v)
        w["ap"] = v["ap"].bitcast(t)
        return w

    def acopy(out, a):
        act(out, a, Act.Copy)

    def gcopy(out, a):
        add("g", lambda: g.affine_select(out["ap"], a["ap"], [[0, out["n"]]], Op.is_equal, 0.0, 0, 0), [out], [a])

    def pick_codes(oq, q, n, off):
        cp(cast(V(oq, 0, 16 * off["n"]), dt.uint32), ind(V(q, 0, n), off, dt.uint32))

    def pick_scales(os_, s, n, off):
        acopy(V(os_, 0, 16 * off["n"]), ind(V(s, 0, n), off))

    def spread(name, w, n, a=0):
        while w < n:
            k = min(w, n - w)
            gcopy(V(name, a + w, a + w + k), V(name, a, a + k))
            w += k

    def keeper(name, n, c, tmp, col, w, unit):
        out = V(name, 0, n)

        def first():
            ts(out, c, col, Op.is_lt, -4.0 * unit, Op.mult)
            ts(tmp, c, col, Op.is_equal, unit, Op.mult)
        return first, lambda: tt(out, out, tmp, Op.add), lambda: ts(V(name, w - 1, n, w), V(name, w - 1, n, w), -2.0 * unit, Op.add)

    def pad(k):
        a, n, _ = TILES[k]
        fill(V("BT", 4 * (a + n - 48), 4 * (a + n)), 0.0)

    dma("s", V("ub"), T.u[:])
    lx = dma("s", V("X", 0, 4 * C), T.x[:])
    dma("s", V("Y", 0, 4 * M), T.m[:])

    bcol, b1col, _, bmcol, i4col, qcol, icol, gcol, zcol, mcol, s0, s1, ecol, socol, lcol, b6col, w0, w1, wcol, l2col = (V("pf", k, k + 1) for k in range(20))
    tri = [8 * t * t + 12 * t for t in range(7)]
    iota(V("pc", 0, 16), [[1, 16]], 0, 1)
    iota(V("c16", 0, C), [[0, 20], [1, 16]])
    iota(V("lui"), [[16, 8]])
    iota(V("t16", 0, 20), [[16, 20]])
    iota(V("t16", 20, 26), [[16, 6]])
    iota(V("c4", 0, 48), [[0, 12], [1, 4]])
    iota(V("CC", 512, 576), [[1, 16], [0, 4]])
    dma("g", V("kp1", p=(0, 1)), T.kap[:], slow=True)
    iota(V("IO"), [[1, C]], -160)
    iota(V("CC", 0, 512), [[1, 8], [0, 64]])
    iota(V("lwf", 0, 2), [[4, 2]])
    iota(V("lwf", 2, 8), [[1, 6]])
    iota(V("SC", 0, 4 * SCW, SCW), [[0, 4]])

    fill(V("ones"), 1.0)
    ts(V("pc", 16, 20), V("pc", 0, 4), 3, Op.bitwise_and)
    ts(V("pc", 20, 22), V("pc", 0, 16, 15), 2, Op.arith_shift_right, 3, Op.bitwise_and)
    ts(V("pc", 22, 23), V("pc", 0, 1), 15, Op.bitwise_and)
    ts(V("pc", 23, 24), V("pc", 0, 1), 4, Op.arith_shift_right)
    pad(0)
    cp(V("pf", 0, 8), V("pc", 16, 24))
    pad(1)
    pad(2)
    fill(V("Y", 4 * M, 512), 0.0)
    act(V("Bw"), V("ones"), Act.Copy, scale=0.0)
    act(mcol, icol, Act.Copy, scale=-BIG)
    act(V("r16"), V("c16", 0, C), Act.Relu, scale=-BIG, bias=BIG)
    act(V("M16"), V("c16", 0, C), Act.Abs, scale=BIG, bias=mcol)
    k16 = keeper("KB", 16, V("c16", 0, 16), V("c16", C, C + 16), icol, 16, 512.0)
    k4 = keeper("K4", 48, V("c4", 0, 48), V("c4", 48, 96), i4col, 4, 1.0)
    k16[0]()
    ts(V("DS", C, 2 * C), V("c16", 0, C), 0.0, Op.is_gt, -2048.0, Op.mult)
    k16[1]()
    cp(V("lu"), V("lui"))
    pad(3)
    k16[2]()
    quant("bq", "bs", 896, V("Bw"))
    quant("uq", "us", 0, V("ub"))
    k4[0]()
    pick_codes("ugq", "uq", 128, V("lu"))
    k4[1]()
    pad(4)
    dma("s", V("rB"), V("ones", 0, 384), after=[lx])
    dma("s", cast(V("wq"), dt.uint8), T.wc[:])
    dma("s", V("wp"), T.ws[:])
    dma("s", V("vb"), T.v[:])
    dma("s", V("Z", 4 * F * M, 4 * 416), V("Bw", 0, 128))
    for a in range(0, 2048, 512):
        dma("s", V("E", a, a + 512), V("Bw"))
    for r in range(R):
        dma("s", cast(V("landc%d" % r, M, 128), dt.uint8), cast(V("bq", 960, 992), dt.uint8))
        dma("s", V("lands%d" % r, M, 128), V("bs", 960, 992))
    acopy(V("KB", 16, 32), V("KB", 0, 16))
    act(zcol, bcol, Act.Identity, bias=4.0 * (160 + 512))
    act(b6col, bcol, Act.Copy, scale=6.0)
    act(s0, qcol, Act.Square, bias=0.5)
    acopy(V("KB", 32, 64), V("KB", 0, 32))
    act(s1, s0, Act.Identity, scale=-32.0, bias=392.0)
    acopy(V("KB", 64, 128), V("KB", 0, 64))
    pick_scales("ugs", "us", 128, V("lu"))
    acopy(V("KB", 128, 256), V("KB", 0, 128))
    act(V("J", 0, 26), V("t16", 0, 26), Act.Identity, bias=icol)
    acopy(V("KB", 256, C), V("KB", 0, 64))
    act(V("K16", C, 384), V("KB", 0, 64), Act.Copy, scale=1 / 512)
    act(V("K16", 0, C), V("KB", 0, C), Act.Copy, scale=1 / 512)

    def after_x():
        ts(V("CC", 512, 576), V("CC", 512, 576), icol, Op.is_equal, float(M), Op.mult)
        k4[2]()
        ts(V("DS", C, 2 * C, 16), V("J", 0, 20), V("KB", 15, 16), Op.add)
        fill(V("ls", 1, 2), 3 * SCW)
        ts(V("CC", 515, 576, 4), V("CC", 515, 576, 4), 1.0, Op.min)
        spread("K4", 48, 384)
        for a, n, rows in TILES[2:]:
            iota(V("rB", a - 576, a - 575), [[0, 1]])
        iota(V("r2"), [[0, 384], [1, 2]])
        add("g", lambda: g.partition_broadcast(T.kpb[:], T.kp1[0:1, :], 128), [V("kpb")], [V("kp1")])
        iota(V("pm", 0, 1), [[0, 1]], 1)
        iota(V("B4", 0, 32), [[0, 8], [1, 4]], 4 * 1024)
        spread("CC", 64, 512, 512)

    def after_own():
        ts(V("CC", 0, 512), V("CC", 0, 512), gcol, Op.is_equal)

    def after_message():
        quant("cq", "cs", 0, V("CC", 0, 512))

    def before_diagonal():
        ts(V("ls", 0, 1), bmcol, float(SCW), Op.mult, s1, Op.add)

    def after_counts():
        iota(V("T2"), [[2, 6]])
        iota(V("DE", 0, 6), [[0, 6]])
        iota(V("E0"), [[0, 24]], -4096)
        for t in range(6):
            iota(V("CK", tri[t], tri[t + 1]), [[1, 16 * t + 20]], 1 - 16 * t)
        iota(V("z4"), [[0, 4]])
        add("g", lambda: g.affine_select(T.I[:], T.ones[:, 0:128], [[1, 128]], Op.is_equal, 0.0, 0, -1), [V("I")], [V("ones", 0, 128)])
        iota(V("B6"), [[0, 24]], 1)
        iota(V("B4", 32, 64), [[-4096, 8], [1, 4]], 4 * 304)
        iota(V("B6", 0, 24, 4), [[64, 6]], -4096 - 192)
        iota(V("idf"), [[0, 8]])

    def before_base():
        ts(w0, i4col, 0.0, Op.is_equal, b1col, Op.mult)
        ts(w1, bcol, 3.0, Op.is_equal, i4col, Op.mult)

    def before_places():
        cp(V("kpf"), V("kpb", 0, 4))
        ts(wcol, w0, w1, Op.add)

    def before_ranks():
        ts(V("lri", 0, 2), V("lwf", 0, 2), i4col, Op.add, 5.0, Op.min)

    def before_order():
        ts(V("lw"), V("lwf", 2, 8), gcol, Op.is_equal, wcol, Op.mult)
        ts(V("ld"), V("lri", 0, 2), b6col, Op.add)

    def after_order():
        cp(V("lr", 0, 2), V("lri", 0, 2))

    def after_discs():
        ts(V("lr", 2, 4), V("lri", 0, 2), 4.0, Op.mult, 3.0, Op.add)

    def after_readings():
        quant("cq", "cs", 128, V("CC", 512, 1024))
        ts(V("CK"), V("CK"), icol, Op.is_equal)
        act(V("pm", 0, 1), V("pm", 0, 1), Act.Copy, scale=BIG)
        act(V("lri", 2, 4), V("lri", 0, 2), Act.Square, bias=1.75)
        act(lcol, bcol, Act.Identity, bias=-8.5)
        act(l2col, bcol, Act.Identity, bias=-8.5 - tri[4])
        for b in range(4):
            acopy(V("E", 512 * b + b, 512 * b + 512, 4), V("I"))
        act(ecol, icol, Act.Copy, scale=-1 / 512)
        act(V("B4", 0, 32), V("B4", 0, 32), Act.Copy, scale=0.25)
        act(socol, icol, Act.Identity, scale=4.0, bias=4.0 * 368)
        act(V("B4", 32, 64), V("B4", 32, 64), Act.Identity, scale=1 / 2048, bias=ecol)
        iota(V("Kc"), [[1, 4], [0, M]])
        for t in range(6):
            act(V("CK", tri[t + 1] - 4, tri[t + 1]), V("B6", 4 * t, 4 * t + 4), Act.Copy, scale=1 / 2048)
            iota(V("EQ", tri[t + 1] - 4, tri[t + 1]), [[0, 4]], -4)

    def after_bits():
        quant("eq", "es", 0, V("E", 0, 1024))
        ts(V("lr", 4, 5), V("lri", 2, 3), 8.0, Op.mult, lcol, Op.add)

    def after_list():
        ts(V("lr", 6, 7), V("lri", 3, 4), 8.0, Op.mult, l2col, Op.add)

    def after_rewriting():
        quant("eq", "es", 256, V("E", 1024, 1536))

    slot = {t: (a, b) for a, n, rows in TILES for b, t in enumerate(rows)}

    def rowview(t, n):
        a, b = slot[t]
        return V("BT", 4 * a + b, 4 * (a + n), 4)

    def message(r):
        lc, ls, ext = "landc%d" % r, "lands%d" % r, ("land%d" % r, landing)
        wb, db = (0, 1, 2, 3), (6, 7, 0, 1) if r < R - 1 else (6, 7, 4, 5)

        def layer():
            for b in range(4):
                mm(wb[b], "wq", "wp", 128 * b, lc, ls, 0, 128, ext=ext)
                act(V("RS", M * b, M * b + M), bank(wb[b], 0, M), Act.Relu, scale=0.03125)
            for b in range(4):
                mm(db[b], "eq", "es", 128 * b, lc, ls, 0, 128, ext=ext)

        def join():
            for b in range(4):
                tt(V("Y", b, 4 * M, 4), V("RS", M * b, M * b + M), bank(db[b], 0, M), Op.add)
        return layer, join

    def half(h):
        act(V("Xh", C * h, C * h + C), V("X", C * h, C * h + C), Act.Copy, scale=0.5)

    def vrow(t):
        ts(rowview(t, 16 * t), bank(4, 0, 16 * t), V("Fv", 16 * t + 15, 16 * t + 16), Op.is_lt)

    waiting = []

    def counted(n, col, out, acc, scale, a=0):
        signs = V("T", C * (len(waiting) % 12), C * (len(waiting) % 12) + n)
        act(signs, bank(5, a, a + n), Act.Sign, bias=col, scale=-1.0)
        finish()
        waiting.append(lambda: act(out, signs, Act.Relu, scale=scale, acc=acc))

    def finish():
        if waiting and waiting[-1]:
            waiting[-1]()
            waiting[-1] = None

    def scores():
        quant("aq", "asc", C, V("Y"))
        mm(6, "ugq", "ugs", 0, "aq", "asc", C, 128)

    def diagonal():
        tt(rowview(0, C), V("Fv"), bank(4, 0, C), Op.is_ge)

    def narrow():
        quant("bq", "bs", 576, V("BT", 4 * 576, 4 * 960))

    def wide():
        quant("bq", "bs", 0, V("BT", 0, 4 * C))
        for a, n, _ in TILES[:1] + TILES[2:]:
            mm(7, "cq", "cs", 0, "bq", "bs", a, max(n, 128), a == 0, False)

    def sums(b):
        scan(V("SC", SCW * b + 1, SCW * b + SCW), V("rB"), V("BT", 4 * 576 + b, 4 * 960, 4), 0.0, Op.mult, Op.subtract)

    def look(a, b):
        ts(V("eb", 16 * a, 16 * b), ind(V("O"), V("pos", a, b)), 1 / 512, Op.mult)

    def discs(a, b):
        scan(V("Fe", 16 * a, 16 * b), V("eb", 16 * a, 16 * b), V("K4", 0, 16 * (b - a)), -4096.0, Op.max, Op.add)

    def offsets(a, b):
        ts(V("zo", 4 * a, 4 * b), V("Fe", 16 * a + 3, 16 * b, 4), 2048.0, Op.mult, zcol, Op.add)

    def zspan(a, b, k=0):
        return 768 * k + 8 * (a % M), 768 * k + 8 * (a % M + b - a)

    outs = []
    for r in range(R):
        layer, join = message(r - 1) if r else (lambda: None, None)
        once = (lambda f: None) if r else (lambda f: f())
        later = (lambda f: f()) if r else (lambda f: None)
        quant("aq", "asc", 160, V("X", 640, 4 * C))
        mm(7, "ugq", "ugs", 0, "aq", "asc", 160, 160)
        quant("aq", "asc", 0, V("X", 0, 640))
        mm(3, "ugq", "ugs", 0, "aq", "asc", 0, 160)
        mm(5, "ugq", "ugs", 0, "aq", "asc", 0, C)
        mm(4, "ugq", "ugs", 0, "aq", "asc", 0, C)
        once(after_x)
        if r == 1:
            quant("eq", "es", 384, V("E", 1536, 2048))
        if r == 2:
            quant("vq", "vs", 0, V("vb"))
        for h in range(4 if r else 2):
            half(h)
        tt(V("Pm", 160, C), bank(7, 0, 160), V("M16", 160, C), Op.add)
        tt(V("Pm", 0, 160), bank(3, 0, 160), V("M16", 0, 160), Op.add)
        scan(V("Fv", 192, C), V("r16", 192, C), V("Pm", 192, C), 0.0, Op.add, Op.min)
        scan(V("Fv", 0, 192), V("r16", 0, 192), V("Pm", 0, 192), 0.0, Op.add, Op.min)
        once(scores)
        vrow(12)
        for k, t in enumerate(range(19, DVE_ROWS, -1)):
            if k == LAYER[r]:
                layer()
            counted(16 * t, V("Fv", 16 * t + 15, 16 * t + 16), rowview(t, 16 * t), V("RA", t, t + 1), 1.0)

        def diagonal_sums():
            once(before_diagonal)
            scan(V("DS", 0, C), V("DS", C, 2 * C), rowview(0, C), -2048.0, Op.max, Op.subtract)

        def masked():
            tt(V("Sm"), bank(6, 0, M), V("M16", 0, M), Op.add)
            once(after_own)

        def least():
            scan(V("Fs"), V("r16", 0, M), V("Sm"), 0.0, Op.add, Op.min)
            once(after_message)

        steps = {"diagonal": diagonal, "its sums": diagonal_sums, "narrow": narrow, "wide": wide,
                 "join": join, "scores": scores, "masked": masked, "least": least}
        for step in ORDER[r]:
            if step in steps:
                steps[step]()
            elif step > 0:
                vrow(step)
            else:
                sums(-step)
        gcopy(V("ZI", 1, 768, 2), V("Y", 0, 4 * M))
        gcopy(V("ZI", 769, 1536, 2), V("Y", 0, 4 * M))
        finish()
        H = SHARE[r]
        counted(C - H, V("Fs", 95, 96), V("NB", 5 * C + H, 6 * C), V("nb", 6, 7), -1.0, H)
        ts(V("NB", 5 * C, 5 * C + H), bank(4, 0, H), V("Fs", 95, 96), Op.is_gt)
        quant("bq", "bs", C, V("BT", 4 * C, 4 * 576))
        mm(7, "cq", "cs", 0, "bq", "bs", C, 256, False, True)
        ends = V("DS", 16 * DVE_ROWS + 31, C, 16)
        tt(ends, ends, V("RA", DVE_ROWS + 1, 20), Op.subtract)
        scan(V("NS", C, C + H), V("ones", 0, H), V("NB", 5 * C, 5 * C + H), 0.0, Op.mult, Op.add)
        for t in range(4, 0 if r else -1, -1):
            counted(C, V("Fs", 16 * t + 15, 16 * t + 16), V("NB", C * t, C * t + C), V("nb", t, t + 1), -1.0)
        finish()
        act(V("Yh", 0, 4 * M), V("Y", 0, 4 * M), Act.Copy, scale=0.5)
        act(V("Yh", 4 * M, 512), V("Y", 0, 128), Act.Copy, scale=0.5)
        once(lambda: half(2))
        once(after_counts)
        once(before_base)
        later(lambda: ts(V("NB", 0, 160), bank(4, 0, 160), V("Fs", 15, 16), Op.is_gt))
        tt(V("KB", 15, 512, 16), ind(V("SC"), V("ls")), V("DS", 15, 512, 16), Op.add)
        once(before_places)
        later(lambda: ts(V("NB", 160, C), bank(4, 160, C), V("Fs", 15, 16), Op.is_gt))
        scan(V("Fc"), bank(7, 0, C), V("KB", 0, C), -4096.0, Op.max, Op.add)
        once(before_ranks)
        later(lambda: scan(V("NS", 0, C), V("ones", 0, C), V("NB", 0, C), -160.0, Op.mult, Op.add))
        ts(V("rk"), V("Fc", 15, C, 16), 512.0, Op.add)
        once(before_order)
        later(lambda: ts(V("nb", 0, 1), V("NS", C - 1, C), 160.0, Op.add))
        ts(V("nb", 5, 6), V("NS", C + H - 1, C + H), V("nb", 6, 7), Op.add)
        cp(ind(V("O", 0, C), V("rk")), V("IO"))
        once(after_order)
        for k in (2, 3, 1, 0):
            if k == (0 if r else 2):
                cp(V("O", C, 2 * C), V("O", 0, C))
            ts(V("pos", 6 * k, 6 * k + 6), V("nb", 0, 6), V("kpf", k, k + 1), Op.add)

        look(6, 14)
        act(V("eb", 16 * 14, 384), ind(V("O"), V("pos", 14, 24)), Act.Copy, scale=1 / 512)
        once(lambda: half(3))
        look(0, 6)
        discs(6, 14)
        discs(14, 24)
        offsets(6, 14)
        discs(0, 6)
        offsets(14, 24)
        for k, (a, b) in enumerate(Z_ACT):
            i0, i1 = zspan(a, b, k)
            acopy(V("ZI", i0, i1, 2), ind(V("X", 0, 4 * C), V("zo", a // 4, b // 4)))
        for step in Z_DVE:
            if len(step) == 1:
                a, b = Z_ACT[step[0]]
                i0, i1 = zspan(a, b, step[0])
                scan(V("ZJ", i0, i1), V("r2", 0, i1 - i0), V("ZI", i0, i1), 0.0, Op.mult, Op.add)
                act(V("Z", 4 * a, 4 * b), V("ZJ", i0 + 1, i1, 2), Act.Copy, scale=0.5)
            elif len(step) == 2:
                a, b = step
                i0, i1 = zspan(a, b)
                tt(V("Z", 4 * a, 4 * b), ind(V("Xh"), V("zo", a // 4, b // 4)), V("Yh", i0 // 2, i1 // 2), Op.add)
                if step == Z_DVE[0]:
                    offsets(0, 6)
                    once(after_discs)
            else:
                a, b, readings = step
                quant("zq", "zs", a, V("Z", 4 * a, 4 * b))
                for k in readings:
                    mm(k, "zq", "zs", M * k, "uq", "us", 0, 128)
        scan(V("E16"), V("eb"), V("K16"), -4096.0, Op.max, Op.add)
        once(after_readings)
        tt(V("DE", 6, 24), V("E16", M + 15, 384, 16), V("E16", 15, 288, 16), Op.subtract)
        tt(V("E0", 0, 24, 4), V("E16", 15, M, 16), V("T2"), Op.add)

        scan(V("pm", 1, 5), V("z4"), V("PA", 1, 2048, 512), -BIG, Op.add, Op.max)
        ts(V("Bw", 0, 96), ind(V("pm", 0, 4), V("lw")), V("pm", 4, 5), Op.is_lt)
        quant("bwq", "bws", 0, V("Bw"))
        mm(6, "cq", "cs", 128, "bwq", "bws", 0, 128)
        cp(V("DT"), ind(V("DE"), V("ld")))
        once(after_bits)
        tt(V("idf", 0, 6), bank(6, 0, 24, 4), V("J", 20, 26), Op.add)
        tt(V("PW"), bank(6, 0, 24), V("DT", 0, 24), Op.mult)
        cp(V("wi"), V("idf", 0, 6))
        scan(V("Fw"), V("E0"), V("PW"), -4096.0, Op.max, Op.add)
        once(after_list)
        tt(V("hf"), ind(V("idf"), V("lr", 0, 2)), V("B4", 0, 32), Op.add)
        acopy(V("ewb"), ind(V("eb"), V("wi")))
        pick_codes("slotc%d" % r, "zq", F * M, V("wi"))
        pick_scales("slots%d" % r, "zs", F * M, V("wi"))
        for call in calls:
            def send(call=call, r=r):
                tr = []
                for kind, a, b, h, mask in call:
                    rid, pid = topo.addr(h, core)
                    if len(call) == 1:
                        return g.remote_dma(piece(T, "hop", r, kind, a, b), piece(T, "slot", r, kind, a, b), T.sem["hop%d" % r], T.sem.sent, pid, rid, mask)
                    tr.append(RemoteDMATransfer(dst_ids=[DstId(rid=rid, pnc=pid)], dma_engine_mask=mask, remote_sem=T.sem["hop%d" % r],
                                                src=piece(T, "slot", r, kind, a, b), dst=piece(T, "hop", r, kind, a, b)))
                return g.remote_dma_fused(tr, local_sem=T.sem.sent)
            add("g", send, [], [V("slot%s%d" % (p[0], r), p[1], p[2]) for p in call], kind="r")

        ts(V("ho"), V("hf", 0, 24), 4.0, Op.mult, -4.0 * 1024, Op.add)
        acopy(V("H"), ind(V("Z", 0, 4 * F * M), V("ho")))
        acopy(V("KO", M * r, M * r + M), ind(V("Kc"), V("wi")))
        tt(V("e5"), ind(V("Fw"), V("lr", 2, 4)), V("B4", 32, 64), Op.add)
        for t in (4, 5, 0, 1, 2, 3):
            ts(V("EQ", tri[t], tri[t + 1] - 4), V("ewb", 0, 16 * t + 16), 2.0 * t - 1.0, Op.add, V("Fw", 4 * t + 3, 4 * t + 4), Op.is_equal)
        for a, b in ((tri[4], tri[6]), (0, tri[4])):
            scan(V("ES", a, b), V("EQ", a, b), V("CK", a, b), 0.0, Op.max, Op.add)
        tt(V("tg", 16, 32), ind(V("ES", tri[4], tri[6]), V("lr", 6, 7)), V("e5", 16, 32), Op.max)
        tt(V("tg", 0, 16), ind(V("ES", 0, tri[4]), V("lr", 4, 5)), V("e5", 0, 16), Op.max)
        for a, b in ((16, 24), (0, 16)):
            ts(V("so", a, b), V("tg", a, b), 2048.0, Op.mult, socol, Op.add)
        cp(ind(V("X"), V("so")), V("H"))
        once(after_rewriting)

    def store(a, n):
        outs.append(dma("s", T.oc[:, 4 * a:4 * (a + n)], cast(V("aq", a, a + n), dt.uint8)))
        for j in range(4):
            outs.append(dma("s", T.osc[4 * j:4 * j + 4, a:a + n], V("asc", a, a + n, p=(32 * j, 32 * j + 4))))

    outs.append(dma("s", T.ok[:], V("KO", p=(0, 1))))
    layer, join = message(R - 1)
    for k in range(2):
        quant("aq", "asc", 160 * k, V("X", 640 * k, 640 * k + 640))
        mm(4 + k, "vq", "vs", 0, "aq", "asc", 160 * k, 160)
    store(0, C)
    for k, (copy, q) in enumerate(((acopy, "a"), (cp, "s"))):
        copy(V("yo", 160 * k, 160 * k + 160), bank(4 + k, 0, 160))
        outs.append(dma(q, T.y[:, 160 * k:160 * k + 160], V("yo", 160 * k, 160 * k + 160)))
    layer()
    join()
    quant("aq", "asc", C, V("Y"))
    mm(2, "vq", "vs", 0, "aq", "asc", C, 128)
    store(C, M)
    cp(V("yo", C, C + M), bank(2, 0, M))
    outs.append(dma("a", T.y[:, C:C + M], V("yo", C, C + M)))

    queue = {"v": g.vector, "a": g.scalar, "t": g.tensor, "g": g, "s": g.sync}
    lane = lambda i: ops[i]["q"] if ops[i]["kind"] == "c" else i
    known, knew, waits = {q: {} for q in queue}, {}, []
    for i, o in enumerate(ops):
        seen, mine = known[o["q"]], []
        for d in sorted(o["deps"], reverse=True):
            if seen.get(lane(d), -1) < d:
                mine.append(d)
                seen[lane(d)] = d
                for k, x in knew[d].items():
                    seen[k] = max(seen.get(k, -1), x)
        knew[i] = dict(seen)
        waits.append(mine)
    needed = set(d for w in waits for d in w)
    count, seen, mark, nd = {q: 0 for q in queue}, {q: {} for q in queue}, {}, 0

    def wait(q, sem, val):
        if seen[q].get(sem, 0) < val:
            queue[q].wait_ge(T.sem[sem], val)
            seen[q][sem] = val

    for i, o in enumerate(ops):
        for d in waits[i]:
            wait(o["q"], *mark[d])
        if o["ext"]:
            wait(o["q"], *o["ext"])
        ins = o["fn"]()
        if o["kind"] == "d":
            mark[i] = ("d%d" % nd, 16)
            ins.then_inc(T.sem["d%d" % nd], 16)
            nd += 1
        elif i in needed:
            count[o["q"]] += 1
            mark[i] = ("q" + o["q"], count[o["q"]])
            ins.then_inc(T.sem["q" + o["q"]], 1)
    for i in outs:
        wait(ops[i]["q"], *mark[i])
    g.wait_ge(T.sem.sent, R * sum(bits(p[4]) for call in calls for p in call))
